import numpy as np, ml_dtypes
CORES = [2,3,42,43,82,83,122,123]
N = 8
import mx_ref
BF = ml_dtypes.bfloat16
def gcols(t, e):
    v = np.concatenate([t.reshape(8, 16, -1, 4), np.zeros((8, 16, 1, 4), BF)], axis=2)
    return np.ascontiguousarray(np.stack([v[g][:, e[g]] for g in range(8)])).reshape(128, -1)
def tile(rs):
    return np.stack(rs, axis=2).reshape(128, -1).astype(BF)
def pick(q, e):
    c = np.concatenate([q[0].reshape(128, -1, 4), np.zeros((128, 1, 4), np.uint8)], axis=1); s = np.concatenate([q[1], np.ones((16, 1), np.uint8)], axis=1)
    return (np.ascontiguousarray(c[:, e].reshape(128, -1)), np.ascontiguousarray(s[:, e]))
def join(*qs):
    return (np.concatenate([q[0] for q in qs], axis=1), np.concatenate([q[1] for q in qs], axis=1))
def put(q, e, v):
    c, s = q[0].reshape(128, -1, 4).copy(), q[1].copy(); c[:, e] = v[0].reshape(128, -1, 4); s[:, e] = v[1]
    return (c.reshape(128, -1), s)
def pk(c, s):
    return (np.ascontiguousarray(c), mx_ref.live(s))
def emit(q):
    return q[0], q[1]
def packed(v, rng):
    q = [mx_ref.quantize(np.ascontiguousarray(v[r])) for r in range(N)]
    return np.stack([a for a, b in q]), np.stack([mx_ref.plane(b, rng) for a, b in q])
def values_of_codes():
    e, c = np.zeros((128, 128, 4), np.float32), np.zeros((128, 2, 4), np.uint8)
    e[np.arange(128), np.arange(128), 0] = 1
    c[:127, :, 0] = np.arange(256).reshape(2, 128).T[:127]
    return mx_ref.matmul(mx_ref.quantize(e.reshape(128, 512).astype(BF)), (c.reshape(128, 8), np.full((16, 2), 127, np.uint8))).T.reshape(-1).astype(np.float64)
CODE_VALUE, SCALE_VALUE = values_of_codes(), 2.0 ** (np.arange(256) - 127.0)
def decode(q):
    return (CODE_VALUE[q[0]].reshape(16, 8, -1, 4) * SCALE_VALUE[q[1]][:, None, :, None] + 0.0).reshape(128, -1).astype(np.float32)
def f(rng, *shape):
    return mx_ref.flush((rng.standard_normal(shape, dtype=np.float32) * np.exp2(rng.integers(-2, 3, shape[:-1] + (1,)))).astype(BF))
def wide(rng, *shape, cols=0):
    v = rng.standard_normal(shape, dtype=np.float32) * np.exp2(rng.integers(-12, 13, shape)).astype(np.float32)
    if cols: v *= np.repeat(np.exp2(rng.integers(-cols, cols + 1, shape[:-2] + (1, shape[-1] // 4))) * (rng.random(shape[:-2] + (1, shape[-1] // 4)) > 0.0625), 4, axis=-1).astype(np.float32)
    return mx_ref.flush(v.astype(BF))
C, R = 512, 2
SETS = np.arange(256)
ONE = (1 << np.arange(8))[:, None]
DECIDE = [16 * g + k for g in range(8) for k in range(10)] + [15]
def bits(b):
    return np.packbits(b, axis=-2, bitorder="little")[..., 0, :].astype(np.int64)
def numbers_of(rng):
    return {"x": np.array(f(rng, N, 128, 4 * C)), "u": np.array(f(rng, N, 128, 512)), "v": np.array(f(rng, N, 128, 512))}
def same(rng, w):
    c, s = packed(np.stack([w] * N), rng)
    return {"wc": c, "ws": np.stack([s[0]] * N)}
def weights(rng, keep=np.ones((8, 16), bool)):
    w = f(rng, 128, 2048).astype(np.float32).reshape(8, 16, 4, 8, 16, 4)
    w = np.where(keep[:, :, None, None, None, None] & keep[:, :, None], w, np.float32(0.0))
    return same(rng, w.reshape(128, 2048).astype(BF))
def setup_inputs(rng):
    return {**numbers_of(rng), **weights(rng)}
def setup_inputs_ties(rng):
    d = numbers_of(rng)
    e = rng.permutation(N)
    x = d["x"].reshape(N, 8, 16, C, 4)
    x[:, :, 0] = rng.integers(0, 3, (N, 8, C, 4)).astype(np.float32).astype(BF)
    x[e[0], 0, 0, :, 3] = 2.0
    x[e[1]] = 0.0
    u = d["u"].reshape(N, 128, 128, 4)
    u[:, :, DECIDE] = 0.0
    for g in range(8):
        u[:, 16 * g, 16 * g, 0] = 1.0
        u[:, 16 * g, 16 * g + 1, 1] = 1.0
        for k in range(8): u[:, 16 * ((g + k) % 8), 16 * g + 2 + k, 2] = 1.0
    u[:, 0, 15, 3] = 1.0
    u[e[2], 0, 15, 3] = -1.0
    keep = np.ones((8, 16), bool)
    keep[:, 0] = False
    return {"x": x.reshape(N, 128, 4 * C), "u": u.reshape(N, 128, 512), "v": d["v"], **weights(rng, keep)}
def setup_inputs_near(rng):
    d = numbers_of(rng)
    x = d["x"].astype(np.float32).reshape(N, 8, 16, C, 4)
    digits = lambda a: ((a[..., None] >> np.arange(4)) & 1) * np.exp2(np.arange(4) - 23.0)
    o = rng.permutation(N)
    n = rng.integers(0, 16, (N, 8, 3, C))
    far = []
    for r in range(N):
        if o[r] % 2 == 0:
            j, g = int(rng.integers(C)), int(rng.integers(5))
            n[r, :, 0, j] = 0
            n[r, g, 0, j] = 15
            n[r, g, 1, j] = 0
            far.append((r, j))
    have = n[:, :, 0] > n[:, :, 1]
    kind = np.where(have[:, 7], np.where(have[:, 6], 2, 1), 0)
    s = digits(2 * (7 - np.count_nonzero(have[:, :7], axis=1)) + rng.integers(0, 2, (N, C)))
    x[:, :, 8:] = 0
    x[:, 5:, :8] = 0
    x[:, :, 8:11] = digits(n)
    x[:, :, 11, :, 0] = 2.0 ** -10
    x[:, 7, 0, :, 0] = 1.0
    for k in range(2):
        x[:, k, 12] = s * (kind == k)[:, :, None]
        x[:, k, 13, :, 0] = (kind == k) * 2.0 ** -10
        x[:, 7 - k, 1, :, 0] = kind == k
    x[:, 5, 1, :, 0] = np.where(kind == 2, -(1.0 + 0.125 * rng.integers(0, 3, (N, C))) * 2.0 ** -30, 0.0)
    for r, j in far: x[r, 7, 1, j, 0] = 2.0 ** 30
    u = d["u"].reshape(N, 128, 128, 4)
    u[:, :, DECIDE] = 0.0
    for r in range(N):
        k = 2.0 ** -30 if o[r] < N // 2 else 1.0
        for g in range(8):
            for i in range(10):
                h = 16 * g + i
                u[r, 112, h, 0] = k
                u[r, 16 * g + 11, h, 0] = k
                u[r, 16 * g + 8 + i if i < 2 else 16 * ((g + i - 2) % 8) + 10, h] = k
    for p, k in ((113, 1.0), (13, 1.0), (97, 2.0 ** -30), (29, 2.0 ** -30), (81, 2.0 ** -30)): u[:, p, 15, 0] = k
    u[:, 12, 15] = 1.0
    u[:, 28, 15] = 2.0 ** -30
    keep = np.zeros((8, 16), bool)
    keep[:5, :8] = True
    return {"x": x.reshape(N, 128, 4 * C).astype(BF), "u": u.reshape(N, 128, 512), "v": d["v"], **weights(rng, keep)}
def setup_inputs_huge(rng):
    d = numbers_of(rng)
    c = rng.integers(0, 2, (N, 1, 1, C, 1)) * 2.0 - 1.0
    x = (0.9 + 0.05 * rng.random((N, 8, 16, C, 4))) * 2.0 ** 30 * c
    u = d["u"].reshape(N, 128, 128, 4)
    u[:, :, DECIDE] = 0.0
    for r in range(N):
        for h in DECIDE[:-1]: u[r, rng.permutation(128)[:64], h] = 2.0 ** 30
        u[r, :, 112] = 0.0
        u[r, :, 15] = (2.0 ** 30 * (1.0 - 0.03 * rng.random((128, 4)))).astype(np.float32).astype(BF)
    w = np.zeros((128, 4, 128, 4), np.float32)
    i = np.arange(128)
    for b in range(4): w[i, b, i, b] = -0.5
    return {"x": x.astype(np.float32).reshape(N, 128, 4 * C).astype(BF), "u": u.reshape(N, 128, 512), "v": d["v"], **same(rng, w.reshape(128, 2048).astype(BF))}
def setup_inputs_few(rng):
    d = numbers_of(rng)
    e = rng.permutation(N)
    x = d["x"].reshape(N, 8, 16, C, 4)
    k = (1.0 + (2 * rng.integers(0, 64, (N, 8, 8, C, 4)) + 1) * 2.0 ** -7) * np.exp2(-rng.integers(8, 15, (N, 8, 8, C, 4)).astype(np.float32))
    x[:, :, 8:] = (k * rng.choice([-1.0, 1.0], (N, 8, 8, C, 4))).astype(np.float32).astype(BF)
    x[:, :, 8, :, 0] = 1.96875
    have = rng.random((N, 8, C)) < 0.5
    have[e[0]] = True
    have[e[1]] = False
    have[e[2]] = np.arange(8)[:, None] == rng.integers(0, 7, C)
    j = int(rng.integers(C))
    have[e[3], 0, j] = False
    have[e[3], 1:, j] = True
    have[:, 7] = False
    x[:, :, 0, :, 0] = np.where(have, 1.0, -1.0).astype(np.float32).astype(BF)
    x[e[3], 0, 2, :, 0] = np.where(have[e[3], 0], -1.0, 1.0).astype(np.float32).astype(BF)
    s = rng.integers(-8, 9, (N, C))
    s[e[0]] = 64 + 8 * rng.integers(0, 8, C)
    s[e[0], C - 1] = 128
    x[:, 0, 1, :, 0] = s.astype(np.float32).astype(BF)
    u = d["u"].reshape(N, 128, 128, 4)
    u[:, :, ::16] = 0.0
    u[:, :, 1::16] = 0.0
    u[:, :, 15] = 0.0
    for h in range(0, 128, 16): u[:, h, h, 0] = 1.0
    u[:, 1, 15, 0] = 1.0
    u[e[3], 112, 112, 0] = 0.0
    u[e[3], 2, 112, 0] = 1.0
    u[e[3], :, 9] = 0.0
    w = f(rng, 128, 2048).astype(np.float32).reshape(8, 16, 4, 8, 16, 4)
    w[:, :, :, :, 8:] = 0
    i = np.arange(8)
    for p in range(8, 16):
        for b in range(4): w[i, p, b, i, p, b] = 32.0
    w[:, 8, 0, :, 8, 0] = 0
    w[:, :, 0, 0, 2] = 0
    w[0, 0, 0, 0, 2, 0] = -64.0
    w[:, :, 0, 7, 0] = 0
    return {"x": x.reshape(N, 128, 4 * C), "u": u.reshape(N, 128, 512), "v": d["v"], **same(rng, w.reshape(128, 2048).astype(BF))}
def setup_inputs_spread(rng):
    d = setup_inputs(rng)
    d["x"] = wide(rng, N, 128, 4 * C, cols=6)
    return d
def check_inputs(d):
    b = []
    for k in ("x", "u", "v"):
        a = np.abs(d[k].astype(np.float32))
        if not (np.isfinite(a).all() and ((a == 0) | (a >= 2.0 ** -30) & (a <= 2.0 ** 30)).all()): b.append("a value of " + k)
    if ((d["wc"] & 0x7F) == 0x7F).any(): b.append("a code of wc that is no number")
    for k in ("wc", "ws"):
        if (d[k] != d[k][:1]).any(): b.append(k + " isn't the same on all ranks")
    none, least, most = [emit(mx_ref.quantize(np.full((128, 16), k, np.float32).astype(BF)))[1][0, 0] for k in (0.0, 2.0 ** -30, 2.0 ** 30)]
    for r in range(N):
        a = mx_ref.live(d["ws"][r])
        if not ((a == none) | (a >= least) & (a <= most)).all(): b.append("a scale of ws")
    return b
def reference(x, u, v, wc, ws):
    qu = [mx_ref.quantize(u[r]) for r in range(N)]
    lay = pk(wc[0], ws[0])
    now = [x[r] for r in range(N)]
    for t in range(R):
        q = [mx_ref.quantize(now[r]) for r in range(N)]
        best, rep = np.zeros((N, 256), np.float32), np.zeros((N, 256), np.int64)
        here, want = np.zeros((N, 8, C), bool), np.zeros((N, 8, C), np.int64)
        for r in range(N):
            s = mx_ref.matmul(qu[r], q[r]) + np.float32(0.0)
            a = s.reshape(8, 16, C)
            here[r] = a[:, 0] > a[:, 1]
            m = bits(here[r])
            want[r] = (m & bits(a[:, 2:10] > a[:, 1:2])) | ONE
            holds = (m & SETS[:, None]) == SETS[:, None]
            strong = np.where(holds, s[15], np.float32(-np.inf))
            rep[r] = np.argmax(strong, axis=1)
            best[r] = np.max(strong, axis=1)
        win = np.argmax(best, axis=0)
        got = pick(join(*q), np.where(np.isfinite(best[win, SETS]), C * win + rep[win, SETS], -1))
        made = tile([mx_ref.matmul(pick(lay, np.arange(128 * b, 128 * b + 128)), got) * np.float32(0.03125) for b in range(4)])
        table = decode(mx_ref.quantize(made)).astype(BF)
        for r in range(N):
            now[r] = (now[r].astype(np.float32) + gcols(table, np.where(here[r], -1, want[r])).astype(np.float32)).astype(BF)
    y, wl = np.zeros((N, 128, C), np.float32), np.zeros((N, 8, C), np.float32)
    oc, osc = np.zeros((N, 128, 4 * C), np.uint8), np.zeros((N, 16, C), np.uint8)
    for r in range(N):
        q = mx_ref.quantize(now[r])
        y[r] = mx_ref.matmul(mx_ref.quantize(v[r]), q)
        wl[r] = want[r]
        oc[r], osc[r] = emit(q)
    return {"y": y, "wl": wl, "oc": oc, "osc": osc}

@@ -1,0 +1,488 @@
+from concourse.bass import DstId, RemoteDMATransfer
+from concourse.mybir import dt, AluOpType, ActivationFunctionType
+import comms_topo
+
+A = AluOpType
+F = ActivationFunctionType
+CODE = "float8_e4m3fn_x4"
+NONE = -float(2 ** 84)
+LOW = -float(2 ** 85)
+MISS = -float(2 ** 90)
+ROUNDS = 2
+SPOT = [32, 1, 2, 4, 8, 64, 128, 16]
+
+SCRATCH = {}
+PLACES = {}
+
+
+def _sb(name, cols, dtype):
+    SCRATCH[name] = ("sbuf", [128, cols], dtype)
+
+
+def _mx(name, cols):
+    _sb(name + "c", cols, CODE)
+    _sb(name + "s", cols, "uint8")
+
+
+def _parts(name, dtype, *parts):
+    at = 0
+    for n, c in parts:
+        PLACES[n] = (name, at)
+        at += c
+    _sb(name, at, dtype)
+
+
+for _k in range(8):
+    SCRATCH["ps%d" % _k] = ("psum", [128, 512], "float32")
+for _n, _c in (("xa", 2048), ("xb", 2048), ("xc", 2048), ("ut", 512), ("vt", 512), ("wm", 512), ("nd", 512), ("zb", 520),
+               ("hb", 512), ("zt", 520), ("junk", 1280), ("yt0", 272), ("yt1", 272), ("yt2", 272), ("yt3", 272),
+               ("f1", 1032), ("f2", 520), ("f3", 520), ("f4", 520), ("f5", 520), ("f6", 520)):
+    _sb(_n, _c, "bfloat16")
+for _n, _c in (("sq", 512), ("acc", 16), ("dg", 32), ("yo", 512), ("wo", 512)):
+    _sb(_n, _c, "float32")
+_parts("work", "float32", ("va", 512), ("vb", 512), ("sa", 520), ("sb", 520), ("ra", 520), ("rb", 520))
+_parts("fixed", "float32", ("m8", 8), ("d5", 128), ("d0b", 128), ("lm", 128), ("d3", 32), ("d3b", 32), ("d4", 8), ("im", 256),
+       ("yy", 256), ("j64", 8), ("gcol", 8), ("rowm", 8), ("par", 8), ("npar", 8), ("mneg", 8))
+_parts("lists", "float32", ("lx", 128), ("ls", 128))
+_parts("whole", "int32", ("ip", 128), ("ip2", 128), ("il", 128), ("il2", 128), ("bi", 256), ("bj", 256), ("io1", 8), ("ij1", 8),
+       ("ij2", 8), ("ij3", 8), ("ij4", 8), ("ij6", 8))
+for _n, _c in (("ulist", 16), ("off", 16), ("offs", 32)):
+    _sb(_n, _c, "uint16")
+for _n, _c in (("uq", 128), ("up", 256), ("vq", 128), ("wq", 512), ("c1", 1024), ("c2", 512), ("c3", 128), ("c4", 512),
+               ("c5", 128), ("c6", 512), ("pq", 128), ("nq", 128), ("zq", 128), ("xq2", 512)):
+    _mx(_n, _c)
+for _t in range(ROUNDS):
+    for _n, _c in (("xq", 640), ("cq", 256), ("lq", 256), ("mq", 64), ("eq", 128), ("tq", 128), ("hq", 128), ("tl", 192)):
+        _mx("%s%d" % (_n, _t), _c)
+    for _n, _c in (("ss", 4), ("st", 16), ("sx", 4), ("se", 8)):
+        _sb("%s%d" % (_n, _t), _c, "float32")
+    _parts("choose%d" % _t, "float32", *[("%s%d" % (_n, _t), _c) for _n, _c in (
+        ("cc", 8), ("mm", 8), ("pp", 8), ("ch", 4), ("qq", 4), ("ff", 4), ("c2f", 4), ("f2f", 4))])
+    _parts("chosen%d" % _t, "uint16", ("om%d" % _t, 8), ("oe%d" % _t, 8))
+    for _n in ("offm", "offe"):
+        _sb("%s%d" % (_n, _t), 4, "uint16")
+SEMAPHORES = ["nv", "ns", "nt", "ng", "lu", "lxa", "lxb", "lw", "lv", "done", "left"] + [
+    "%s%d" % (a, t) for t in range(ROUNDS) for a in ("ac", "as", "bc", "bs", "gc", "om", "oe")]
+
+
+def rank_program(g, core, T, topo):
+    rank = T.rank_of(core)
+    if rank is None:
+        return
+    o, block, partner = rank % 4, rank // 4, rank ^ 4
+    queue = {"v": g.vector, "s": g.scalar, "t": g.tensor, "g": g, "y": g.sync}
+    counter = {"v": "nv", "s": "ns", "t": "nt", "g": "ng"}
+    total, known, snaps, seen, waited = {}, {q: {} for q in queue}, {}, {}, {}
+
+    def P(name, a, b, step=1, r0=0, r1=128):
+        name, at = PLACES.get(name, (name, 0))
+        return (name, at + a, at + b, step, r0, r1)
+
+    def V(p):
+        return T[p[0]][:, p[1]:p[2]:p[3]] if p[3] > 1 else T[p[0]][:, p[1]:p[2]]
+
+    def VR(p):
+        return T[p[0]][p[4]:p[5], p[1]:p[2]:p[3]] if p[3] > 1 else T[p[0]][p[4]:p[5], p[1]:p[2]]
+
+    def meet(a, b):
+        if max(a[4], b[4]) >= min(a[5], b[5]) or max(a[1], b[1]) >= min(a[2], b[2]):
+            return False
+        return not (a[3] == b[3] and a[3] > 1 and (a[1] - b[1]) % a[3])
+
+    def conflicts(q, reads, writes):
+        out = {}
+        for p, w in [(p, False) for p in reads] + [(p, True) for p in writes]:
+            bank = p[0][:2] == "ps"
+            for p2, w2, q2, tok in seen.get(p[0], []):
+                if bank:
+                    if q2 == q and not (w or w2):
+                        continue
+                else:
+                    if not (w or w2) or not meet(p, p2):
+                        continue
+                if q2 == q and not w2:
+                    continue
+                out[tok[0]] = max(out.get(tok[0], 0), tok[1])
+        return out
+
+    def wait(q, deps):
+        deps = {s: n for s, n in deps.items() if known[q].get(s, 0) < n}
+        keep = [s for s in deps if not any(e != s and snaps.get((e, deps[e]), {}).get(s, 0) >= deps[s] for e in deps)]
+        for s in keep:
+            queue[q].wait_ge(T.sem[s], deps[s])
+            waited[s] = max(waited.get(s, 0), deps[s])
+            for e, n in [(s, deps[s])] + list(snaps.get((s, deps[s]), {}).items()):
+                known[q][e] = max(known[q].get(e, 0), n)
+
+    def note(q, reads, writes, tok):
+        for p in reads:
+            seen.setdefault(p[0], []).append((p, False, q, tok))
+        for p in writes:
+            seen.setdefault(p[0], []).append((p, True, q, tok))
+
+    def do(q, call, reads, writes):
+        wait(q, conflicts(q, reads, writes))
+        s = counter[q]
+        total[s] = total.get(s, 0) + 1
+        call().then_inc(T.sem[s], 1)
+        snaps[(s, total[s])] = dict(known[q])
+        note(q, reads, writes, (s, total[s]))
+
+    def dma(q, out, src, s, full, reads, writes):
+        wait(q, conflicts("dma", reads, []))
+        total[s] = total.get(s, 0) + 16
+        queue[q].dma_start(out, src).then_inc(T.sem[s], 16)
+        note("dma", reads, writes, (s, full))
+
+    def fill(p, c):
+        do("v", lambda: g.vector.memset(VR(p), c), [], [p])
+
+    def tt(out, a, b, op):
+        do("v", lambda: g.vector.tensor_tensor(V(out), V(a), V(b), op), [a, b], [out])
+
+    def ts(out, a, s1, op0, s2=None, op1=None, rows=False):
+        W = VR if rows else V
+        sc = [s for s in (s1, s2) if isinstance(s, tuple)]
+        x1, x2 = [V(s) if isinstance(s, tuple) else s for s in (s1, s2)]
+        if op1 is None:
+            do("v", lambda: g.vector.tensor_scalar(W(out), W(a), x1, None, op0), [a] + sc, [out])
+        else:
+            do("v", lambda: g.vector.tensor_scalar(W(out), W(a), x1, x2, op0, op1), [a] + sc, [out])
+
+    def copy(out, a):
+        do("v", lambda: g.vector.tensor_copy(V(out), V(a)), [a], [out])
+
+    def scan(out, d0, d1, initial, op0, op1):
+        do("v", lambda: g.vector.tensor_tensor_scan(V(out), V(d0), V(d1), initial, op0, op1), [d0, d1], [out])
+
+    def act(out, a, func=F.Copy, scale=None):
+        if scale is None:
+            do("s", lambda: g.scalar.activation(V(out), V(a), func), [a], [out])
+        else:
+            do("s", lambda: g.scalar.activation(V(out), V(a), func, scale=scale), [a], [out])
+
+    def below(out, r, end, first, step, at):
+        src, junk = P(r, first, 512, step), P("junk", at, at + 512 // step)
+        do("s", lambda: g.scalar.activation(V(junk), V(src), F.Sign, bias=V(end), scale=-1.0, accum_out=V(out)),
+           [src, end], [junk, out])
+
+    def quant(q, a, b, src):
+        do("v", lambda: g.vector.quantize_mx(T[q + "c"][:, a:b], T[q + "s"][:, a:b], V(src)), [src],
+           [P(q + "c", a, b), P(q + "s", a, b)])
+
+    def mm(bank, n, w, wa, x, xa):
+        do("t", lambda: g.tensor.matmul_mx(T["ps%d" % bank][:, 0:n], T[w + "c"][:, wa:wa + 128], T[w + "s"][:, wa:wa + 128],
+                                           T[x + "c"][:, xa:xa + n], T[x + "s"][:, xa:xa + n], True, True),
+           [P(w + "c", wa, wa + 128), P(w + "s", wa, wa + 128), P(x + "c", xa, xa + n), P(x + "s", xa, xa + n)],
+           [P("ps%d" % bank, 0, n)])
+
+    def pick(out, c, d, win, b, lst, e, f):
+        i = P(lst, e, f)
+        do("v", lambda: g.vector.tensor_copy(T[out + "c"][:, c:d].bitcast(dt.uint32),
+                                             T[win + "c"][:, 0:b].bitcast(dt.uint32).indirect(V(i))),
+           [P(win + "c", 0, b), i], [P(out + "c", c, d)])
+        do("s", lambda: g.scalar.activation(T[out + "s"][:, c:d], T[win + "s"][:, 0:b].indirect(V(i)), F.Copy),
+           [P(win + "s", 0, b), i], [P(out + "s", c, d)])
+
+    def ps(k, a, b, r1=128):
+        return P("ps%d" % k, a, b, 1, 0, r1)
+
+    def address(r):
+        rid, pid = topo.addr(T.cores[r])[:2]
+        return DstId(rid=rid, pnc=pid)
+
+    def bitmask(engines):
+        return sum(1 << e for e in engines)
+
+    mates = [4 * block + d for d in range(4) if d != o]
+    far = [r for r in mates if topo.chip(T.cores[r]) != topo.chip(core)]
+    near = [r for r in mates if r not in far]
+    outside = topo.engines(core, T.cores[far[0]])
+    share = len(outside) // len(far)
+    masks = {r: bitmask(outside[k * share:(k + 1) * share]) for k, r in enumerate(far)}
+    inside = [e for e in topo.engines(core, T.cores[near[0]]) if e not in outside]
+    for k, r in enumerate(near):
+        masks[r] = bitmask(inside[k * share:(k + 1) * share])
+    masks[partner] = topo.mask(core, T.cores[partner])
+
+    def send(moves, s, reads):
+        wait("g", conflicts("g", reads, []))
+        g.remote_dma_fused([RemoteDMATransfer(dst_ids=[address(r)], dma_engine_mask=masks[r], remote_sem=T.sem[s], src=a, dst=b)
+                            for r, a, b in moves], local_sem=T.sem.left)
+        total["left"] = total.get("left", 0) + sum(bin(masks[r]).count("1") for r, a, b in moves)
+
+    def land(s, n, places):
+        total[s] = n
+        note("remote", [], places, (s, n))
+
+    def U8(name, a, b):
+        return T[name][:, a:b].bitcast(dt.uint8)
+
+    dma("y", T.ut[:], T.u[:], "lu", 16, [], [P("ut", 0, 512)])
+    dma("s", T.xa[:, 0:1024], T.x[:, 0:1024], "lxa", 16, [], [P("xa", 0, 1024)])
+    dma("y", T.xa[:, 1024:2048], T.x[:, 1024:2048], "lxb", 16, [], [P("xa", 1024, 2048)])
+    dma("y", U8("wqc", 0, 512), T.wc[:], "lw", 32, [], [P("wqc", 0, 512)])
+    dma("y", T.wqs[:], T.ws[:], "lw", 32, [], [P("wqs", 0, 512)])
+    dma("y", T.vt[:], T.v[:], "lv", 16, [], [P("vt", 0, 512)])
+
+    def iota(p, pattern, base, ch, f=False):
+        if f:
+            do("g", lambda: g.iota(V(p), pattern, base, ch, allow_small_or_imprecise_dtypes=True), [], [p])
+        else:
+            do("g", lambda: g.iota(V(p), pattern, base, ch), [], [p])
+
+    def select(out, src, pattern, op, value, base, ch):
+        do("g", lambda: g.affine_select(V(out), V(src), pattern, op, value, base, ch), [src], [out])
+
+    iota(P("io1", 0, 8), [[16, 8]], 1, 0)
+    iota(P("ij2", 0, 8), [[0, 8]], 0, 1)
+    iota(P("im", 0, 256), [[1, 256]], 0, 0, True)
+    iota(P("ip", 0, 128), [[-2, 128]], 256, 1)
+    fill(P("zt", 0, 520), 0.0)
+    act(P("f1", 0, 516), P("zt", 0, 516))
+    act(P("f1", 516, 1032), P("zt", 0, 516))
+    for f in ("f5", "f2", "zb"):
+        act(P(f, 0, 520), P("zt", 0, 520))
+    fill(P("ulist", 8, 16), 15)
+    copy(P("ulist", 0, 8), P("io1", 0, 8))
+    for k in range(4):
+        fill(P("gcol", 0, 1, 1, 32 * k, 32 * k + 32), 2.0 ** -(2 * k + 1))
+    for k in range(4):
+        fill(P("gcol", 0, 1, 1, 32 * k, 32 * k + 16), 2.0 ** -(2 * k))
+    ts(P("ij3", 0, 8), P("ij2", 0, 8), 15, A.bitwise_and)
+    ts(P("ij6", 0, 8), P("ij2", 0, 8), 1, A.bitwise_and)
+    fill(P("m8", 0, 8), 1.0)
+    ts(P("rowm", 0, 1), P("ij3", 0, 1), 0.0, A.is_equal)
+    ts(P("yy", 0, 256), P("im", 0, 256), P("gcol", 0, 1), A.mult, -0.498046875, A.add)
+    copy(P("bi", 0, 256), P("yy", 0, 256))
+    ts(P("bj", 0, 256), P("bi", 0, 256), 1, A.bitwise_and)
+    ts(P("f1", 3, 1027, 4), P("bj", 0, 256), P("rowm", 0, 1), A.mult)
+    quant("uq", 0, 128, P("ut", 0, 512))
+    pick("up", 0, 256, "uq", 128, "ulist", 0, 16)
+    select(P("m8", 0, 8), P("m8", 0, 8), [[-32, 4], [0, 2]], A.is_ge, 0.0, 0, 1)
+    select(P("m8", 0, 8), P("m8", 0, 8), [[32, 4], [0, 2]], A.is_ge, 0.0, 31, -1)
+    select(P("f2", 3, 515, 4), P("f2", 3, 515, 4), [[0, 8], [16, 16]], A.not_equal, 1.0, -32, -1)
+    select(P("f2", 3, 515, 4), P("f2", 3, 515, 4), [[16, 8], [1000, 16]], A.not_equal, 1.0, 0, -1)
+    iota(P("il", 0, 128), [[4, 128]], 259, -1)
+    iota(P("ij1", 0, 8), [[128, 2], [0, 2], [16, 2]], 0, 0)
+    iota(P("d3", 0, 32), [[0, 32]], 0, 0, True)
+    for k in range(8):
+        turned = (k == 5 and o & 1) or (k == 6 and o & 2)
+        select(P("d3", 0, 32), P("d3", 0, 32), [[-16, 8], [0, 4]], A.not_equal, float(SPOT[k] if turned else -SPOT[k]), -2 - k, 1)
+    select(P("d3", 0, 32), P("d3", 0, 32), [[-17, 8], [0, 4]], A.not_equal, 0.0, -2, 1)
+    select(P("d3b", 0, 32), P("d3", 0, 32), [[-16, 8], [0, 4]], A.not_equal, -256.0, 0, 1)
+
+    def constants_early():
+        for b in range(4):
+            quant("c1", 256 * b, 256 * b + 256, P("f1", 3 - b, 1027 - b))
+        ts(P("ip2", 0, 128), P("ip", 0, 128), 30, A.bitwise_and)
+        ts(P("d5", 0, 128), P("ip2", 0, 128), 0.0, A.is_equal)
+        ts(P("par", 0, 1), P("ij6", 0, 1), 1.0, A.is_equal)
+        ts(P("npar", 0, 1), P("ij6", 0, 1), 0.0, A.is_equal)
+        fill(P("sa", 512, 516), NONE)
+        fill(P("sb", 512, 516), NONE)
+        for t in range(ROUNDS):
+            fill(P("ss%d" % t, 0, 4), 0.0)
+        ts(P("m8", 1, 8, 2), P("m8", 1, 8, 2), P("par", 0, 1), A.mult)
+        ts(P("m8", 0, 8, 2), P("m8", 0, 8, 2), P("npar", 0, 1), A.mult)
+        ts(P("mneg", 0, 8), P("m8", 0, 8), 1.0, A.subtract, 65536.0, A.mult)
+        for e, w in ((0, 64.0), (1, 8.0), (2, 1.0)):
+            act(P("f5", e, 512, 4), P("d5", 0, 128), scale=w)
+
+    def constants_mid():
+        quant("c5", 0, 128, P("f5", 0, 512))
+        quant("xq0", 512, 640, P("zt", 0, 512))
+
+    def constants_wait():
+        for f in ("f6", "f4", "f3"):
+            act(P(f, 0, 520), P("zt", 0, 520))
+        select(P("f6", 3, 515, 4), P("f6", 3, 515, 4), [[-1, 128]], A.not_equal, 1.0, 0, 1)
+        ts(P("ij4", 0, 8), P("ij2", 0, 8), 30, A.bitwise_and)
+        ts(P("j64", 0, 8), P("ij4", 0, 8), 1.0 / 128, A.mult)
+        ts(P("yy", 0, 8), P("ij1", 0, 8), 1.0 / 64, A.mult)
+        tt(P("im", 0, 8), P("j64", 0, 8), P("yy", 0, 8), A.add)
+        ts(P("yy", 8, 9), P("par", 0, 1), 0.5, A.mult)
+        ts(P("j64", 0, 8), P("im", 0, 8), P("yy", 8, 9), A.add)
+
+    def constants_lists():
+        for b in range(4):
+            quant("c2", 128 * b, 128 * b + 128, P("f2", 3 - b, 515 - b))
+        fill(P("d0b", 0, 128), 1.0)
+        fill(P("d0b", 0, 128, 4), 0.0)
+        ts(P("il2", 0, 128), P("il", 0, 128), 12, A.bitwise_and)
+        ts(P("lm", 0, 128), P("il2", 0, 128), 0.0, A.is_equal)
+        for b in range(4):
+            act(P("f3", 5 * b, 512, 16), P("d3b", 0, 32))
+        quant("c3", 0, 128, P("f3", 0, 512))
+
+    def constants_last():
+        fill(P("hb", 0, 512), 0.0)
+        for t in range(ROUNDS):
+            quant("tq%d" % t, 0, 128, P("zt", 0, 512))
+        quant("xq1", 512, 640, P("zt", 0, 512))
+        for b in range(4):
+            fill(P("yt%d" % b, 256, 272), 0.0)
+        for b in range(4):
+            quant("c6", 128 * b, 128 * b + 128, P("f6", 3 - b, 515 - b))
+        quant("vq", 0, 128, P("vt", 0, 512))
+
+    def constants_swap():
+        iota(P("d4", 0, 8), [[0, 8]], 0, 0, True)
+        for k in range(8):
+            select(P("d4", 0, 8), P("d4", 0, 8), [[-16, 8]], A.not_equal, float(2 ** k), -2 - k, 1)
+        select(P("d4", 0, 8), P("d4", 0, 8), [[-17, 8]], A.not_equal, 0.0, -2, 1)
+
+    state = ["xa", "xb", "xc"]
+    place = {0: 0, 2: 4, 1: 8, 3: 12}
+    pieces = ((0, 384), (384, 512))
+
+    def new_state(t, a, b):
+        X, Z = state[t], state[t + 1]
+        for e in range(4):
+            i, y = P("offs", a // 16, b // 16), P("yt%d" % e, 0, 272)
+            do("v", lambda: g.vector.tensor_tensor(T[Z][:, 4 * a + e:4 * b:4], V(y).indirect(V(i)), T[X][:, 4 * a + e:4 * b:4], A.add),
+               [y, i, P(X, 4 * a + e, 4 * b, 4)], [P(Z, 4 * a + e, 4 * b, 4)])
+
+    for t in range(ROUNDS):
+        N = lambda s: "%s%d" % (s, t)
+        X, xq = state[t], N("xq")
+        last = t == ROUNDS - 1
+        for k, (a, b) in enumerate(pieces):
+            if t:
+                new_state(t - 1, a, b)
+            quant(xq, a, b, P(X, 4 * a, 4 * b))
+            mm((1, 3)[k], b - a, "up", 0, xq, a)
+            mm((0, 4)[k], b - a, "uq", 0, xq, a)
+            act(P("sq", a, b), ps((1, 3)[k], 0, b - a))
+        mm(2, 512, "up", 128, xq, 0)
+        if t == 0:
+            constants_early()
+        for k, (a, b) in enumerate(pieces):
+            tt(P("wm", a, b), ps((0, 4)[k], 0, b - a), P("sq", a, b), A.is_le)
+        quant("pq", 0, 128, P("wm", 0, 512))
+        if t == 0:
+            constants_mid()
+        banks = ((5, 6, 7, 1), (3, 0, 4, 5))
+        for h in range(2):
+            for b in range(4):
+                mm(banks[h][b], 128, "c1", 256 * b + 128 * h, "pq", 0)
+                act(P(("va", "vb")[h], 128 * b, 128 * b + 128), ps(banks[h][b], 0, 128), scale=MISS)
+        for h in range(2):
+            va, sa, ra = ("va", "sa", "ra") if h == 0 else ("vb", "sb", "rb")
+            for b in range(4):
+                tt(P(sa, b, 512, 4), P("ps2", b, 512, 4), P(va, 128 * b, 128 * b + 128), A.add)
+            scan(P(ra, 0, 513), P(sa, 0, 513), P(sa, 0, 513), LOW, A.max, A.max)
+            for k, (first, step) in enumerate(((63, 64), (7, 8), (0, 1))):
+                below(P("acc", 8 * h + k, 8 * h + k + 1), ra, P(ra, 512, 513), first, step, 640 * h + (0, 16, 128)[k])
+        for h in range(2):
+            copy(P(N("ss"), h, h + 1), P(("ra", "rb")[h], 512, 513))
+        st = N("st")
+        send([(r, T[N("ss")][:, 0:4], T[st][:, place[o]:place[o] + 4]) for r in mates], N("as"), [P(N("ss"), 0, 4)])
+        copy(P(st, place[o], place[o] + 4), P(N("ss"), 0, 4))
+        land(N("as"), sum(bin(masks[r]).count("1") for r in mates), [P(st, place[r % 4], place[r % 4] + 4) for r in mates])
+        for h in range(2):
+            d = 8 * h
+            ts(P("zb", 4 * h, 64, 8), P("m8", 0, 8), P("acc", d, d + 1), A.mult)
+            for k in range(2):
+                dg = P("dg", 16 * h + 8 * k, 16 * h + 8 * k + 8)
+                ts(dg, P("mneg", 0, 8), P("acc", d + k, d + k + 1), A.subtract, 8.0, A.mult)
+                ts(P("zb", 4 * h + k + 1, 64, 8), dg, P("acc", d + k + 1, d + k + 2), A.add, 0.0, A.max)
+        quant("zq", 0, 128, P("zb", 0, 512))
+        mm(6, 128, "c5", 0, "zq", 0)
+        copy(P("off", 0, 16), ps(6, 0, 16))
+        pick(N("cq"), 0, 256, xq, 544, "off", 0, 16)
+        cq, lq = N("cq"), N("lq")
+        send([(r, U8(cq + "c", 64 * (r % 4), 64 * (r % 4) + 64), U8(lq + "c", 64 * o, 64 * o + 64)) for r in mates], N("ac"),
+             [P(cq + "c", 0, 256)])
+        send([(r, T[cq + "s"][:, 64 * (r % 4):64 * (r % 4) + 64], T[lq + "s"][:, 64 * o:64 * o + 64]) for r in mates], N("ac"),
+             [P(cq + "s", 0, 256)])
+        pick(lq, 64 * o, 64 * o + 64, xq, 544, "off", 4 * o, 4 * o + 4)
+        land(N("ac"), 2 * sum(bin(masks[r]).count("1") for r in mates),
+             [P(lq + k, 64 * (r % 4), 64 * (r % 4) + 64) for r in mates for k in "cs"])
+        if t == 0:
+            constants_wait()
+        cc, mx_, pp, se, ff = N("cc"), N("mm"), N("pp"), N("se"), N("ff")
+
+        def lay_out(src, dst, s):
+            for k in range(8):
+                dma("sy"[k % 2], T[dst][16 * k:16 * k + 16, 0:4], VR(P(src, 0, 2, 1, 32 * o, 32 * o + 32)), s, 128,
+                    [P(src, 0, 2)], [P(dst, 0, 4, 1, 16 * k, 16 * k + 16)])
+
+        tt(P(mx_, 0, 8), P(st, 8, 16), P(st, 0, 8), A.max)
+        tt(P(cc, 0, 8), P(st, 8, 16), P(st, 0, 8), A.is_gt)
+        tt(P(N("sx"), 0, 4), P(mx_, 4, 8), P(mx_, 0, 4), A.max)
+        tt(P(N("ch"), 0, 4), P(mx_, 4, 8), P(mx_, 0, 4), A.is_gt)
+        tt(P(pp, 0, 8), P(cc, 0, 8), P("j64", 0, 8), A.add)
+        tt(P(N("qq"), 0, 4), P(N("ch"), 0, 4), P(pp, 4, 8), A.mult)
+        tt(P(ff, 0, 4), P(N("qq"), 0, 4), P(pp, 0, 4), A.max)
+        ts(P(N("om"), 0, 4), P(ff, 0, 4), 64.0, A.mult)
+        lay_out(N("om"), N("offm"), N("om"))
+        send([(partner, T[N("sx")][:, 0:4], T[se][:, 4 * block:4 * block + 4])], N("bs"), [P(N("sx"), 0, 4)])
+        copy(P(se, 4 * block, 4 * block + 4), P(N("sx"), 0, 4))
+        n = bin(masks[partner]).count("1")
+        theirs = 1 - block
+        land(N("bs"), n, [P(se, 4 * theirs, 4 * theirs + 4)])
+        if t == 0:
+            constants_lists()
+        for b in range(4):
+            mm((3, 0, 4, 5)[b], 128, "c2", 128 * b, "pq", 0)
+        for b in range(4):
+            tt(P("nd", b, 512, 4), ps((3, 0, 4, 5)[b], 0, 128), P("wm", b, 512, 4), A.max)
+        quant("nq", 0, 128, P("nd", 0, 512))
+        mm(7, 128, "c3", 0, "nq", 0)
+        mq, eq = N("mq"), N("eq")
+        pick(mq, 0, 64, lq, 256, N("offm"), 0, 4)
+        send([(partner, U8(mq + "c", 0, 64), U8(eq + "c", 64 * block, 64 * block + 64))], N("bc"), [P(mq + "c", 0, 64)])
+        send([(partner, T[mq + "s"][:, 0:64], T[eq + "s"][:, 64 * block:64 * block + 64])], N("bc"), [P(mq + "s", 0, 64)])
+        pick(eq, 64 * block, 64 * block + 64, lq, 256, N("offm"), 0, 4)
+        land(N("bc"), 2 * n, [P(eq + k, 64 * theirs, 64 * theirs + 64) for k in "cs"])
+        tt(P(N("c2f"), 0, 4), P(se, 4, 8), P(se, 0, 4), A.is_gt)
+        tt(P(N("f2f"), 0, 4), P(N("c2f"), 0, 4), P("j64", 0, 4), A.add)
+        ts(P(N("oe"), 0, 4), P(N("f2f"), 0, 4), 64.0, A.mult)
+        lay_out(N("oe"), N("offe"), N("oe"))
+        if t == 0:
+            constants_last()
+        tt(P("lx", 0, 128), ps(7, 0, 128), P("lm", 0, 128), A.mult)
+        scan(P("ls", 0, 128), P("d0b", 0, 128), P("lx", 0, 128), 0.0, A.mult, A.add)
+        ts(P("offs", 0, 32), P("ls", 3, 128, 4), float(511 - 64 * o), A.add, 256.0, A.min)
+        if last:
+            act(P("f4", 3, 35, 4), P("d4", 0, 8))
+            for b in range(4):
+                quant("c4", 128 * b, 128 * b + 128, P("f4", 3 - b, 515 - b))
+                mm(4 + b, 128, "c4", 128 * b, "nq", 0)
+            for b in range(4):
+                ts(P("wo", b, 512, 4, 0, 8), ps(4 + b, 0, 128, 8), -1.0, A.mult, 255.0, A.add, rows=True)
+            dma("y", T.wl[:, 0:512], T.wo[0:8, 0:512], "done", 0, [P("wo", 0, 512)], [])
+        tq, hq, tl = N("tq"), N("hq"), N("tl")
+        pick(tq, 0, 64, eq, 128, N("offe"), 0, 4)
+        for b in range(4):
+            mm(b, 128, "wq", 128 * b, tq, 0)
+        for b in range(4):
+            if b % 2:
+                ts(P("hb", b, 256, 4), ps(b, 0, 64), 0.03125, A.mult)
+            else:
+                act(P("hb", b, 256, 4), ps(b, 0, 64), scale=0.03125)
+        quant(hq, 0, 128, P("hb", 0, 512))
+        slot = {r: 64 * ((o ^ (r % 4)) - 1) for r in mates}
+        send([(r, U8(hq + "c", 0, 64), U8(tl + "c", slot[r], slot[r] + 64)) for r in mates], N("gc"), [P(hq + "c", 0, 64)])
+        send([(r, T[hq + "s"][:, 0:64], T[tl + "s"][:, slot[r]:slot[r] + 64]) for r in mates], N("gc"), [P(hq + "s", 0, 64)])
+        land(N("gc"), 2 * sum(bin(masks[r]).count("1") for r in mates), [P(tl + k, 0, 192) for k in "cs"])
+        if t == 0:
+            constants_swap()
+        for a, n, src, bank in ((0, 64, hq, 4), (64, 192, tl, 0)):
+            for b in range(4):
+                mm(bank + b, max(n, 128), "c6", 128 * b, src, 0)
+            for b in range(4):
+                (copy if b % 2 and a == 0 else act)(P("yt%d" % b, a, a + n), ps(bank + b, 0, n))
+    for k, (a, b) in enumerate(pieces):
+        new_state(ROUNDS - 1, a, b)
+        quant("xq2", a, b, P(state[ROUNDS], 4 * a, 4 * b))
+        mm(4 + k, b - a, "vq", 0, "xq2", a)
+        act(P("yo", a, b), ps(4 + k, 0, b - a))
+        dma("y", T.oc[:, 4 * a:4 * b], U8("xq2c", a, b), "done", 0, [P("xq2c", a, b)], [])
+        dma("y", T.y[:, a:b], V(P("yo", a, b)), "done", 0, [P("yo", a, b)], [])
+    for k in range(4):
+        dma("s", T.osc[4 * k:4 * k + 4, 0:512], T.xq2s[32 * k:32 * k + 4, 0:512], "done", 0, [P("xq2s", 0, 512)], [])
+    for s in total:
+        if waited.get(s, 0) < total[s]:
+            g.wait_ge(T.sem[s], total[s])

@@ -1,5 +1,6 @@
+import math
 from concourse.bass import DstId, RemoteDMATransfer
-from concourse.mybir import dt, AluOpType, ActivationFunctionType
+from concourse.mybir import dt, AluOpType, ActivationFunctionType, AxisListType
 import comms_topo
 
 A = AluOpType
@@ -9,7 +10,7 @@ NONE = -float(2 ** 84)
 LOW = -float(2 ** 85)
 MISS = -float(2 ** 90)
 ROUNDS = 2
-SPOT = [32, 1, 2, 4, 8, 64, 128, 16]
+HEAD = 64
 
 SCRATCH = {}
 PLACES = {}
@@ -34,35 +35,31 @@ def _parts(name, dtype, *parts):
 
 for _k in range(8):
     SCRATCH["ps%d" % _k] = ("psum", [128, 512], "float32")
-for _n, _c in (("xa", 2048), ("xb", 2048), ("xc", 2048), ("ut", 512), ("vt", 512), ("wm", 512), ("nd", 512), ("zb", 520),
-               ("hb", 512), ("zt", 520), ("junk", 1280), ("yt0", 272), ("yt1", 272), ("yt2", 272), ("yt3", 272),
+for _n, _c in (("xa", 2056), ("xb", 2056), ("xc", 2048), ("ut", 512), ("vt", 512), ("wm", 512), ("nd", 512), ("zb", 1040),
+               ("hb", 512), ("zt", 520), ("junk", 1408), ("yt0", 272), ("yt1", 272), ("yt2", 272), ("yt3", 272),
                ("f1", 1032), ("f2", 520), ("f3", 520), ("f4", 520), ("f5", 520), ("f6", 520)):
     _sb(_n, _c, "bfloat16")
 for _n, _c in (("sq", 512), ("acc", 16), ("dg", 32), ("yo", 512), ("wo", 512)):
     _sb(_n, _c, "float32")
-_parts("work", "float32", ("va", 512), ("vb", 512), ("sa", 520), ("sb", 520), ("ra", 520), ("rb", 520))
-_parts("fixed", "float32", ("m8", 8), ("d5", 128), ("d0b", 128), ("lm", 128), ("d3", 32), ("d3b", 32), ("d4", 8), ("im", 256),
-       ("yy", 256), ("j64", 8), ("gcol", 8), ("rowm", 8), ("par", 8), ("npar", 8), ("mneg", 8))
+_parts("work", "float32", ("va", 512), ("vb", 512), ("sa", 520), ("sb", 520))
+_parts("fixed", "float32", ("m8", 8), ("k8", 8), ("d5", 128), ("d0b", 128), ("lm", 128), ("d3", 32), ("d3b", 32), ("d4", 8),
+       ("im", 128), ("uf", 16), ("gcol", 8), ("last", 8), ("rs", 64), ("p2", 8))
 _parts("lists", "float32", ("lx", 128), ("ls", 128))
-_parts("whole", "int32", ("ip", 128), ("ip2", 128), ("il", 128), ("il2", 128), ("bi", 256), ("bj", 256), ("io1", 8), ("ij1", 8),
-       ("ij2", 8), ("ij3", 8), ("ij4", 8), ("ij6", 8))
-for _n, _c in (("ulist", 16), ("off", 16), ("offs", 32)):
+_parts("choose", "float32", ("cm", 8), ("tr", 32), ("row", 32), ("bc", 64), ("mk", 64), ("fold", 64))
+_parts("whole", "int32", ("ip", 128), ("ip2", 128), ("il", 128), ("il2", 128), ("bi", 128), ("bj", 128))
+for _n, _c in (("ulist", 16), ("off", 16), ("offs", 32), ("offm", 4), ("offe", 4)):
     _sb(_n, _c, "uint16")
 for _n, _c in (("uq", 128), ("up", 256), ("vq", 128), ("wq", 512), ("c1", 1024), ("c2", 512), ("c3", 128), ("c4", 512),
-               ("c5", 128), ("c6", 512), ("pq", 128), ("nq", 128), ("zq", 128), ("xq2", 512)):
+               ("c5", 128), ("c6", 512), ("pq", 128), ("nq", 128), ("zq", 256), ("xq2", 512)):
     _mx(_n, _c)
 for _t in range(ROUNDS):
-    for _n, _c in (("xq", 640), ("cq", 256), ("lq", 256), ("mq", 64), ("eq", 128), ("tq", 128), ("hq", 128), ("tl", 192)):
+    for _n, _c in (("xq", 544), ("cq", 192), ("lq", 256), ("mq", 64), ("eq", 128), ("tq", 128), ("hq", 192), ("tl", 128)):
         _mx("%s%d" % (_n, _t), _c)
-    for _n, _c in (("ss", 4), ("st", 16), ("sx", 4), ("se", 8)):
+    _parts("run%d" % _t, "float32", ("ra%d" % _t, HEAD + 520), ("rb%d" % _t, HEAD + 520))
+    for _n, _c in (("st", 16), ("rr", 8), ("se", 4)):
         _sb("%s%d" % (_n, _t), _c, "float32")
-    _parts("choose%d" % _t, "float32", *[("%s%d" % (_n, _t), _c) for _n, _c in (
-        ("cc", 8), ("mm", 8), ("pp", 8), ("ch", 4), ("qq", 4), ("ff", 4), ("c2f", 4), ("f2f", 4))])
-    _parts("chosen%d" % _t, "uint16", ("om%d" % _t, 8), ("oe%d" % _t, 8))
-    for _n in ("offm", "offe"):
-        _sb("%s%d" % (_n, _t), 4, "uint16")
 SEMAPHORES = ["nv", "ns", "nt", "ng", "lu", "lxa", "lxb", "lw", "lv", "done", "left"] + [
-    "%s%d" % (a, t) for t in range(ROUNDS) for a in ("ac", "as", "bc", "bs", "gc", "om", "oe")]
+    "%s%d" % (a, t) for t in range(ROUNDS) for a in ("ac", "as", "bc", "bs", "gc", "gn")]
 
 
 def rank_program(g, core, T, topo):
@@ -72,22 +69,25 @@ def rank_program(g, core, T, topo):
     o, block, partner = rank % 4, rank // 4, rank ^ 4
     queue = {"v": g.vector, "s": g.scalar, "t": g.tensor, "g": g, "y": g.sync}
     counter = {"v": "nv", "s": "ns", "t": "nt", "g": "ng"}
+    span = [set()]
     total, known, snaps, seen, waited = {}, {q: {} for q in queue}, {}, {}, {}
 
     def P(name, a, b, step=1, r0=0, r1=128):
         name, at = PLACES.get(name, (name, 0))
         return (name, at + a, at + b, step, r0, r1)
 
-    def V(p):
-        return T[p[0]][:, p[1]:p[2]:p[3]] if p[3] > 1 else T[p[0]][:, p[1]:p[2]]
+    def Q(name, a, b, step=1):
+        return P(name, a, b, step, 64 * (o & 1), 64 * (o & 1) + 64)
 
-    def VR(p):
-        return T[p[0]][p[4]:p[5], p[1]:p[2]:p[3]] if p[3] > 1 else T[p[0]][p[4]:p[5], p[1]:p[2]]
+    def V(p):
+        rows = slice(None) if (p[4], p[5]) == (0, 128) else slice(p[4], p[5])
+        return T[p[0]][rows, p[1]:p[2]:p[3]] if p[3] > 1 else T[p[0]][rows, p[1]:p[2]]
 
     def meet(a, b):
         if max(a[4], b[4]) >= min(a[5], b[5]) or max(a[1], b[1]) >= min(a[2], b[2]):
             return False
-        return not (a[3] == b[3] and a[3] > 1 and (a[1] - b[1]) % a[3])
+        step = math.gcd(*[0 if p[2] - p[1] == 1 else p[3] for p in (a, b)])
+        return step == 0 or (a[1] - b[1]) % step == 0
 
     def conflicts(q, reads, writes):
         out = {}
@@ -123,6 +123,11 @@ def rank_program(g, core, T, topo):
     def do(q, call, reads, writes):
         wait(q, conflicts(q, reads, writes))
         s = counter[q]
+        if q == "g":
+            rows = {p[4:6] for p in reads + writes}
+            if total.get(s) and rows | span[0] != {(0, 128)}:
+                wait(q, {s: total[s]})
+            span[0] = rows
         total[s] = total.get(s, 0) + 1
         call().then_inc(T.sem[s], 1)
         snaps[(s, total[s])] = dict(known[q])
@@ -135,19 +140,18 @@ def rank_program(g, core, T, topo):
         note("dma", reads, writes, (s, full))
 
     def fill(p, c):
-        do("v", lambda: g.vector.memset(VR(p), c), [], [p])
+        do("v", lambda: g.vector.memset(V(p), c), [], [p])
 
     def tt(out, a, b, op):
         do("v", lambda: g.vector.tensor_tensor(V(out), V(a), V(b), op), [a, b], [out])
 
-    def ts(out, a, s1, op0, s2=None, op1=None, rows=False):
-        W = VR if rows else V
+    def ts(out, a, s1, op0, s2=None, op1=None):
         sc = [s for s in (s1, s2) if isinstance(s, tuple)]
         x1, x2 = [V(s) if isinstance(s, tuple) else s for s in (s1, s2)]
         if op1 is None:
-            do("v", lambda: g.vector.tensor_scalar(W(out), W(a), x1, None, op0), [a] + sc, [out])
+            do("v", lambda: g.vector.tensor_scalar(V(out), V(a), x1, None, op0), [a] + sc, [out])
         else:
-            do("v", lambda: g.vector.tensor_scalar(W(out), W(a), x1, x2, op0, op1), [a] + sc, [out])
+            do("v", lambda: g.vector.tensor_scalar(V(out), V(a), x1, x2, op0, op1), [a] + sc, [out])
 
     def copy(out, a):
         do("v", lambda: g.vector.tensor_copy(V(out), V(a)), [a], [out])
@@ -155,14 +159,14 @@ def rank_program(g, core, T, topo):
     def scan(out, d0, d1, initial, op0, op1):
         do("v", lambda: g.vector.tensor_tensor_scan(V(out), V(d0), V(d1), initial, op0, op1), [d0, d1], [out])
 
-    def act(out, a, func=F.Copy, scale=None):
-        if scale is None:
-            do("s", lambda: g.scalar.activation(V(out), V(a), func), [a], [out])
-        else:
-            do("s", lambda: g.scalar.activation(V(out), V(a), func, scale=scale), [a], [out])
+    def act(out, a, func=F.Copy, scale=None, bias=None):
+        more = {k: x for k, x in (("scale", scale), ("bias", bias)) if x is not None}
+        do("s", lambda: g.scalar.activation(V(out), V(a), func, **{k: V(x) if isinstance(x, tuple) else x for k, x in more.items()}),
+           [a] + [x for x in more.values() if isinstance(x, tuple)], [out])
 
-    def below(out, r, end, first, step, at):
-        src, junk = P(r, first, 512, step), P("junk", at, at + 512 // step)
+    def below(out, r, step, at):
+        n = HEAD + 512
+        src, end, junk = P(r, step - 1, n, step), P(r, n, n + 1), P("junk", at, at + n // step)
         do("s", lambda: g.scalar.activation(V(junk), V(src), F.Sign, bias=V(end), scale=-1.0, accum_out=V(out)),
            [src, end], [junk, out])
 
@@ -201,13 +205,17 @@ def rank_program(g, core, T, topo):
     share = len(outside) // len(far)
     masks = {r: bitmask(outside[k * share:(k + 1) * share]) for k, r in enumerate(far)}
     inside = [e for e in topo.engines(core, T.cores[near[0]]) if e not in outside]
-    for k, r in enumerate(near):
-        masks[r] = bitmask(inside[k * share:(k + 1) * share])
+    masks[near[0]] = bitmask(inside)
+    assert [r % 4 for r in near] == [o ^ 1]
     masks[partner] = topo.mask(core, T.cores[partner])
+    from_mates = sum(bin(masks[r]).count("1") for r in mates)
+    from_partner = bin(masks[partner]).count("1")
+    from_near = len(inside)
 
-    def send(moves, s, reads):
+    def send(moves, s, reads, s_near=None):
         wait("g", conflicts("g", reads, []))
-        g.remote_dma_fused([RemoteDMATransfer(dst_ids=[address(r)], dma_engine_mask=masks[r], remote_sem=T.sem[s], src=a, dst=b)
+        g.remote_dma_fused([RemoteDMATransfer(dst_ids=[address(r)], dma_engine_mask=masks[r],
+                                              remote_sem=T.sem[s_near if s_near and r in near else s], src=a, dst=b)
                             for r, a, b in moves], local_sem=T.sem.left)
         total["left"] = total.get("left", 0) + sum(bin(masks[r]).count("1") for r, a, b in moves)
 
@@ -218,9 +226,12 @@ def rank_program(g, core, T, topo):
     def U8(name, a, b):
         return T[name][:, a:b].bitcast(dt.uint8)
 
-    dma("y", T.ut[:], T.u[:], "lu", 16, [], [P("ut", 0, 512)])
-    dma("s", T.xa[:, 0:1024], T.x[:, 0:1024], "lxa", 16, [], [P("xa", 0, 1024)])
-    dma("y", T.xa[:, 1024:2048], T.x[:, 1024:2048], "lxb", 16, [], [P("xa", 1024, 2048)])
+    pieces = ((0, 384), (384, 512))
+    cut = 4 * pieces[0][1]
+    dma("s", T.ut[:], T.u[:], "lu", 16, [], [P("ut", 0, 512)])
+    dma("y", T.xa[:, 0:cut], T.x[:, 0:cut], "lxa", 16, [], [P("xa", 0, cut)])
+    dma("y", T.xa[:, cut:2048], T.x[:, cut:2048], "lxb", 16, [], [P("xa", cut, 2048)])
+    wait("y", {"lxa": 16, "lxb": 16})
     dma("y", U8("wqc", 0, 512), T.wc[:], "lw", 32, [], [P("wqc", 0, 512)])
     dma("y", T.wqs[:], T.ws[:], "lw", 32, [], [P("wqs", 0, 512)])
     dma("y", T.vt[:], T.v[:], "lv", 16, [], [P("vt", 0, 512)])
@@ -234,107 +245,98 @@ def rank_program(g, core, T, topo):
     def select(out, src, pattern, op, value, base, ch):
         do("g", lambda: g.affine_select(V(out), V(src), pattern, op, value, base, ch), [src], [out])
 
-    iota(P("io1", 0, 8), [[16, 8]], 1, 0)
-    iota(P("ij2", 0, 8), [[0, 8]], 0, 1)
-    iota(P("im", 0, 256), [[1, 256]], 0, 0, True)
-    iota(P("ip", 0, 128), [[-2, 128]], 256, 1)
+    iota(P("ip", 0, 128), [[0, 8], [-1, 16]], 16, 1)
+    iota(P("im", 0, 128), [[1, 128]], 0, 0, True)
+    iota(P("uf", 0, 16), [[16, 16]], 1, 0, True)
+    select(P("uf", 0, 16), P("uf", 0, 16), [[-1, 16]], A.is_ge, 15.0, 7, 0)
     fill(P("zt", 0, 520), 0.0)
     act(P("f1", 0, 516), P("zt", 0, 516))
     act(P("f1", 516, 1032), P("zt", 0, 516))
-    for f in ("f5", "f2", "zb"):
-        act(P(f, 0, 520), P("zt", 0, 520))
-    fill(P("ulist", 8, 16), 15)
-    copy(P("ulist", 0, 8), P("io1", 0, 8))
+    act(P("zb", 0, 520), P("zt", 0, 520))
+    act(P("zb", 520, 1040), P("zt", 0, 520))
     for k in range(4):
-        fill(P("gcol", 0, 1, 1, 32 * k, 32 * k + 32), 2.0 ** -(2 * k + 1))
+        fill(P("gcol", 0, 1, 1, 32 * k, 32 * k + 32), 2.0 ** (6 - 2 * k))
     for k in range(4):
-        fill(P("gcol", 0, 1, 1, 32 * k, 32 * k + 16), 2.0 ** -(2 * k))
-    ts(P("ij3", 0, 8), P("ij2", 0, 8), 15, A.bitwise_and)
-    ts(P("ij6", 0, 8), P("ij2", 0, 8), 1, A.bitwise_and)
-    fill(P("m8", 0, 8), 1.0)
-    ts(P("rowm", 0, 1), P("ij3", 0, 1), 0.0, A.is_equal)
-    ts(P("yy", 0, 256), P("im", 0, 256), P("gcol", 0, 1), A.mult, -0.498046875, A.add)
-    copy(P("bi", 0, 256), P("yy", 0, 256))
-    ts(P("bj", 0, 256), P("bi", 0, 256), 1, A.bitwise_and)
-    ts(P("f1", 3, 1027, 4), P("bj", 0, 256), P("rowm", 0, 1), A.mult)
+        fill(P("gcol", 0, 1, 1, 32 * k, 32 * k + 16), 2.0 ** (7 - 2 * k))
+    ts(P("ip2", 0, 128), P("ip", 0, 128), 15, A.bitwise_and)
+    ts(P("bi", 0, 128), P("im", 0, 128), P("gcol", 0, 1), A.mult)
+    ts(P("d5", 0, 128), P("ip2", 0, 128), 0.0, A.is_equal)
+    ts(P("bj", 0, 128), P("bi", 0, 128), 128, A.bitwise_and)
+    ts(P("last", 0, 1), P("gcol", 0, 1), 1.0, A.is_equal, P("d5", 0, 1), A.mult)
+    fill(P("xa", 2048, 2056), 0.0)
+    top = 512 * (o >> 1)
+    ts(P("f1", 515 - top, 1027 - top, 4), P("bj", 0, 128), P("d5", 0, 1), A.mult)
+    ts(P("f1", 3 + top, 515 + top, 4), P("bj", 0, 128), P("d5", 0, 1), A.mult, P("last", 0, 1), A.add)
+    copy(P("ulist", 0, 16), P("uf", 0, 16))
+    for e, w in ((0, 64.0), (1, 8.0), (2, 1.0), (3, 0.0)):
+        act(P("f5", e, 512, 4), P("d5", 0, 128), scale=w)
+    act(P("f2", 0, 520), P("zt", 0, 520))
+    for b in range(2):
+        quant("c1", 256 * b, 256 * b + 256, P("f1", 3 - b, 1027 - b))
     quant("uq", 0, 128, P("ut", 0, 512))
-    pick("up", 0, 256, "uq", 128, "ulist", 0, 16)
-    select(P("m8", 0, 8), P("m8", 0, 8), [[-32, 4], [0, 2]], A.is_ge, 0.0, 0, 1)
-    select(P("m8", 0, 8), P("m8", 0, 8), [[32, 4], [0, 2]], A.is_ge, 0.0, 31, -1)
-    select(P("f2", 3, 515, 4), P("f2", 3, 515, 4), [[0, 8], [16, 16]], A.not_equal, 1.0, -32, -1)
-    select(P("f2", 3, 515, 4), P("f2", 3, 515, 4), [[16, 8], [1000, 16]], A.not_equal, 1.0, 0, -1)
-    iota(P("il", 0, 128), [[4, 128]], 259, -1)
-    iota(P("ij1", 0, 8), [[128, 2], [0, 2], [16, 2]], 0, 0)
+    pick("up", 0, 128, "uq", 128, "ulist", 0, 8)
+    pick("up", 128, 256, "uq", 128, "ulist", 8, 16)
+    for name, inside_value, outside_value in (("m8", 1, 0.0), ("k8", -8, -1024.0)):
+        iota(P(name, 0, 8), [[0, 8]], inside_value, 0, True)
+        select(P(name, 0, 8), P(name, 0, 8), [[-16, 8]], A.is_ge, outside_value, 0, 1)
+        select(P(name, 0, 8), P(name, 0, 8), [[16, 8]], A.is_ge, outside_value, 15, -1)
+    iota(Q("cm", 3, 4), [[0, 1]], 0, 1, True)
     iota(P("d3", 0, 32), [[0, 32]], 0, 0, True)
     for k in range(8):
-        turned = (k == 5 and o & 1) or (k == 6 and o & 2)
-        select(P("d3", 0, 32), P("d3", 0, 32), [[-16, 8], [0, 4]], A.not_equal, float(SPOT[k] if turned else -SPOT[k]), -2 - k, 1)
+        turned = (64 * o >> k) & 1
+        select(P("d3", 0, 32), P("d3", 0, 32), [[-16, 8], [0, 4]], A.not_equal, float(2 ** k if turned else -2 ** k), -2 - k, 1)
     select(P("d3", 0, 32), P("d3", 0, 32), [[-17, 8], [0, 4]], A.not_equal, 0.0, -2, 1)
     select(P("d3b", 0, 32), P("d3", 0, 32), [[-16, 8], [0, 4]], A.not_equal, -256.0, 0, 1)
+    select(P("f2", 3, 515, 4), P("f2", 3, 515, 4), [[0, 8], [16, 16]], A.not_equal, 1.0, -32, -1)
+    select(P("f2", 3, 515, 4), P("f2", 3, 515, 4), [[16, 8], [1000, 16]], A.not_equal, 1.0, 0, -1)
 
     def constants_early():
-        for b in range(4):
+        for b in range(2, 4):
             quant("c1", 256 * b, 256 * b + 256, P("f1", 3 - b, 1027 - b))
-        ts(P("ip2", 0, 128), P("ip", 0, 128), 30, A.bitwise_and)
-        ts(P("d5", 0, 128), P("ip2", 0, 128), 0.0, A.is_equal)
-        ts(P("par", 0, 1), P("ij6", 0, 1), 1.0, A.is_equal)
-        ts(P("npar", 0, 1), P("ij6", 0, 1), 0.0, A.is_equal)
-        fill(P("sa", 512, 516), NONE)
-        fill(P("sb", 512, 516), NONE)
-        for t in range(ROUNDS):
-            fill(P("ss%d" % t, 0, 4), 0.0)
-        ts(P("m8", 1, 8, 2), P("m8", 1, 8, 2), P("par", 0, 1), A.mult)
-        ts(P("m8", 0, 8, 2), P("m8", 0, 8, 2), P("npar", 0, 1), A.mult)
-        ts(P("mneg", 0, 8), P("m8", 0, 8), 1.0, A.subtract, 65536.0, A.mult)
-        for e, w in ((0, 64.0), (1, 8.0), (2, 1.0)):
-            act(P("f5", e, 512, 4), P("d5", 0, 128), scale=w)
 
     def constants_mid():
+        fill(P("sa", 512, 516), NONE)
+        fill(P("sb", 512, 516), NONE)
+        for r in ("ra0", "rb0"):
+            fill(P(r, 0, HEAD), LOW)
         quant("c5", 0, 128, P("f5", 0, 512))
-        quant("xq0", 512, 640, P("zt", 0, 512))
 
     def constants_wait():
+        act(Q("p2", 0, 1), Q("cm", 3, 4), scale=1.0 / 64)
         for f in ("f6", "f4", "f3"):
             act(P(f, 0, 520), P("zt", 0, 520))
-        select(P("f6", 3, 515, 4), P("f6", 3, 515, 4), [[-1, 128]], A.not_equal, 1.0, 0, 1)
-        ts(P("ij4", 0, 8), P("ij2", 0, 8), 30, A.bitwise_and)
-        ts(P("j64", 0, 8), P("ij4", 0, 8), 1.0 / 128, A.mult)
-        ts(P("yy", 0, 8), P("ij1", 0, 8), 1.0 / 64, A.mult)
-        tt(P("im", 0, 8), P("j64", 0, 8), P("yy", 0, 8), A.add)
-        ts(P("yy", 8, 9), P("par", 0, 1), 0.5, A.mult)
-        ts(P("j64", 0, 8), P("im", 0, 8), P("yy", 8, 9), A.add)
-
-    def constants_lists():
-        for b in range(4):
-            quant("c2", 128 * b, 128 * b + 128, P("f2", 3 - b, 515 - b))
-        fill(P("d0b", 0, 128), 1.0)
-        fill(P("d0b", 0, 128, 4), 0.0)
-        ts(P("il2", 0, 128), P("il", 0, 128), 12, A.bitwise_and)
-        ts(P("lm", 0, 128), P("il2", 0, 128), 0.0, A.is_equal)
         for b in range(4):
             act(P("f3", 5 * b, 512, 16), P("d3b", 0, 32))
-        quant("c3", 0, 128, P("f3", 0, 512))
+        fill(Q("tr", 0, 32), 0.0)
+        fill(P("rs", 0, 64), 1.0)
+        fill(P("hb", 0, 512), 0.0)
+        fill(P("rs", 0, 64, 16), 0.0)
+        for b in range(4):
+            quant("c2", 128 * b, 128 * b + 128, P("f2", 3 - b, 515 - b))
+        quant("tq0", 0, 128, P("zt", 0, 512))
 
     def constants_last():
-        fill(P("hb", 0, 512), 0.0)
-        for t in range(ROUNDS):
-            quant("tq%d" % t, 0, 128, P("zt", 0, 512))
-        quant("xq1", 512, 640, P("zt", 0, 512))
-        for b in range(4):
-            fill(P("yt%d" % b, 256, 272), 0.0)
         for b in range(4):
             quant("c6", 128 * b, 128 * b + 128, P("f6", 3 - b, 515 - b))
-        quant("vq", 0, 128, P("vt", 0, 512))
+        quant("c3", 0, 128, P("f3", 0, 512))
+        fill(P("d0b", 0, 128), 1.0)
+        ts(P("il2", 0, 128), P("il", 0, 128), 12, A.bitwise_and)
+        fill(P("d0b", 0, 128, 4), 0.0)
+        ts(P("lm", 0, 128), P("il2", 0, 128), 0.0, A.is_equal)
+        for b in range(4):
+            fill(P("yt%d" % b, 256, 272), 0.0)
+        fill(P("xb", 2048, 2056), 0.0)
+        for r in ("ra1", "rb1"):
+            fill(P(r, 0, HEAD), LOW)
 
     def constants_swap():
+        iota(P("il", 0, 128), [[4, 128]], 259, -1)
         iota(P("d4", 0, 8), [[0, 8]], 0, 0, True)
         for k in range(8):
             select(P("d4", 0, 8), P("d4", 0, 8), [[-16, 8]], A.not_equal, float(2 ** k), -2 - k, 1)
         select(P("d4", 0, 8), P("d4", 0, 8), [[-17, 8]], A.not_equal, 0.0, -2, 1)
 
     state = ["xa", "xb", "xc"]
-    place = {0: 0, 2: 4, 1: 8, 3: 12}
-    pieces = ((0, 384), (384, 512))
 
     def new_state(t, a, b):
         X, Z = state[t], state[t + 1]
@@ -343,6 +345,18 @@ def rank_program(g, core, T, topo):
             do("v", lambda: g.vector.tensor_tensor(T[Z][:, 4 * a + e:4 * b:4], V(y).indirect(V(i)), T[X][:, 4 * a + e:4 * b:4], A.add),
                [y, i, P(X, 4 * a + e, 4 * b, 4)], [P(Z, 4 * a + e, 4 * b, 4)])
 
+    def spread():
+        do("v", lambda: g.vector.transpose(V(Q("row", 0, 32)), V(Q("tr", 0, 32))), [Q("tr", 0, 32)], [Q("row", 0, 32)])
+        for k in range(2):
+            first = 64 * (o & 1) + 32 * k
+            src, out = P("row", 0, 32, 1, first, first + 1), P("bc", 32 * k, 32 * k + 32)
+            do("g", lambda: g.partition_broadcast(V(out), V(src), 128), [src], [out])
+
+    def fold(dst, scale):
+        tt(P("mk", 0, 64), P("bc", 0, 64), P("d5", 0, 64), A.mult)
+        scan(P("fold", 0, 64), P("rs", 0, 64), P("mk", 0, 64), 0.0, A.mult, A.add)
+        ts(P(dst, 0, 4), P("fold", 15, 64, 16), scale, A.mult)
+
     for t in range(ROUNDS):
         N = lambda s: "%s%d" % (s, t)
         X, xq = state[t], N("xq")
@@ -350,98 +364,124 @@ def rank_program(g, core, T, topo):
         for k, (a, b) in enumerate(pieces):
             if t:
                 new_state(t - 1, a, b)
-            quant(xq, a, b, P(X, 4 * a, 4 * b))
+            more = 2 if b == 512 else 0
+            quant(xq, a, b + more, P(X, 4 * a, 4 * (b + more)))
             mm((1, 3)[k], b - a, "up", 0, xq, a)
             mm((0, 4)[k], b - a, "uq", 0, xq, a)
             act(P("sq", a, b), ps((1, 3)[k], 0, b - a))
-        mm(2, 512, "up", 128, xq, 0)
         if t == 0:
             constants_early()
+        mm(2, 512, "up", 128, xq, 0)
         for k, (a, b) in enumerate(pieces):
             tt(P("wm", a, b), ps((0, 4)[k], 0, b - a), P("sq", a, b), A.is_le)
         quant("pq", 0, 128, P("wm", 0, 512))
         if t == 0:
             constants_mid()
         banks = ((5, 6, 7, 1), (3, 0, 4, 5))
+        st, cq, lq = N("st"), N("cq"), N("lq")
+        end = HEAD + 512
+        count = lambda h, k: P("acc", 8 * h + k, 8 * h + k + 1)
+        digit = lambda h, k: P("zb", 520 * h + k, 520 * h + 32, 4)
         for h in range(2):
             for b in range(4):
                 mm(banks[h][b], 128, "c1", 256 * b + 128 * h, "pq", 0)
-                act(P(("va", "vb")[h], 128 * b, 128 * b + 128), ps(banks[h][b], 0, 128), scale=MISS)
+                act(P("vb", b, 512, 4) if h else P("va", 128 * b, 128 * b + 128), ps(banks[h][b], 0, 128), scale=MISS)
         for h in range(2):
-            va, sa, ra = ("va", "sa", "ra") if h == 0 else ("vb", "sb", "rb")
-            for b in range(4):
-                tt(P(sa, b, 512, 4), P("ps2", b, 512, 4), P(va, 128 * b, 128 * b + 128), A.add)
-            scan(P(ra, 0, 513), P(sa, 0, 513), P(sa, 0, 513), LOW, A.max, A.max)
-            for k, (first, step) in enumerate(((63, 64), (7, 8), (0, 1))):
-                below(P("acc", 8 * h + k, 8 * h + k + 1), ra, P(ra, 512, 513), first, step, 640 * h + (0, 16, 128)[k])
+            if h:
+                tt(P("sb", 0, 512), ps(2, 0, 512), P("vb", 0, 512), A.add)
+            else:
+                for b in range(4):
+                    tt(P("sa", b, 512, 4), P("ps2", b, 512, 4), P("va", 128 * b, 128 * b + 128), A.add)
+            sa, run = P(("sa", "sb")[h], 0, 513), N(("ra", "rb")[h])
+            scan(P(run, HEAD, end + 1), sa, sa, LOW, A.max, A.max)
+            send([(r, V(P(run, end, end + 1)), T[st][:, 4 * o:4 * o + 1]) for r in (far, near)[h]], N("as"), [P(run, end, end + 1)])
+            for k, step in enumerate((64, 8, 1)):
+                below(count(h, k), run, step, 704 * h + (0, 16, 128)[k])
+            if h == 0:
+                act(digit(0, 0), P("m8", 0, 8), scale=count(0, 0))
+                act(digit(0, 1), P("k8", 0, 8), F.Relu, count(0, 0), count(0, 1))
+            act(digit(h, 2), P("k8", 0, 8), F.Relu, count(h, 1), count(h, 2))
+        land(N("as"), from_mates, [P(st, 4 * (r % 4), 4 * (r % 4) + 1) for r in mates])
+        slot = {r: 64 * (r & 1) for r in far}
+        slot[near[0]] = 128
         for h in range(2):
-            copy(P(N("ss"), h, h + 1), P(("ra", "rb")[h], 512, 513))
-        st = N("st")
-        send([(r, T[N("ss")][:, 0:4], T[st][:, place[o]:place[o] + 4]) for r in mates], N("as"), [P(N("ss"), 0, 4)])
-        copy(P(st, place[o], place[o] + 4), P(N("ss"), 0, 4))
-        land(N("as"), sum(bin(masks[r]).count("1") for r in mates), [P(st, place[r % 4], place[r % 4] + 4) for r in mates])
-        for h in range(2):
-            d = 8 * h
-            ts(P("zb", 4 * h, 64, 8), P("m8", 0, 8), P("acc", d, d + 1), A.mult)
-            for k in range(2):
-                dg = P("dg", 16 * h + 8 * k, 16 * h + 8 * k + 8)
-                ts(dg, P("mneg", 0, 8), P("acc", d + k, d + k + 1), A.subtract, 8.0, A.mult)
-                ts(P("zb", 4 * h + k + 1, 64, 8), dg, P("acc", d + k + 1, d + k + 2), A.add, 0.0, A.max)
-        quant("zq", 0, 128, P("zb", 0, 512))
-        mm(6, 128, "c5", 0, "zq", 0)
-        copy(P("off", 0, 16), ps(6, 0, 16))
-        pick(N("cq"), 0, 256, xq, 544, "off", 0, 16)
-        cq, lq = N("cq"), N("lq")
-        send([(r, U8(cq + "c", 64 * (r % 4), 64 * (r % 4) + 64), U8(lq + "c", 64 * o, 64 * o + 64)) for r in mates], N("ac"),
-             [P(cq + "c", 0, 256)])
-        send([(r, T[cq + "s"][:, 64 * (r % 4):64 * (r % 4) + 64], T[lq + "s"][:, 64 * o:64 * o + 64]) for r in mates], N("ac"),
-             [P(cq + "s", 0, 256)])
-        pick(lq, 64 * o, 64 * o + 64, xq, 544, "off", 4 * o, 4 * o + 4)
-        land(N("ac"), 2 * sum(bin(masks[r]).count("1") for r in mates),
-             [P(lq + k, 64 * (r % 4), 64 * (r % 4) + 64) for r in mates for k in "cs"])
+            quant("zq", 128 * h, 128 * h + 128, P("zb", 520 * h, 520 * h + 512))
+            mm(6 + h, 128, "c5", 0, "zq", 128 * h)
+            if h == 0:
+                ts(digit(1, 0), P("m8", 0, 8), count(1, 0), A.mult)
+                ts(P("dg", 0, 8), P("k8", 0, 8), count(1, 0), A.mult, count(1, 1), A.add)
+            ts(P("off", 8 * h, 8 * h + 8), ps(6 + h, 0, 8), -float(HEAD), A.add)
+            if h == 0:
+                pick(cq, 0, 128, xq, 514, "off", 0, 8)
+                ts(digit(1, 1), P("dg", 0, 8), 0.0, A.max)
+                copy(P(st, 4 * o, 4 * o + 1), P(N("rb"), end, end + 1))
+            else:
+                there = 8 + 4 * (near[0] & 1)
+                pick(cq, 128, 192, xq, 514, "off", there, there + 4)
+            send([(r, U8(cq + "c", slot[r], slot[r] + 64), U8(lq + "c", 64 * o, 64 * o + 64)) for r in (far, near)[h]], N("ac"),
+                 [P(cq + "c", slot[r], slot[r] + 64) for r in (far, near)[h]])
+        send([(r, T[cq + "s"][:, slot[r]:slot[r] + 64], T[lq + "s"][:, 64 * o:64 * o + 64]) for r in mates], N("ac"),
+             [P(cq + "s", 0, 192)])
+        pick(lq, 64 * o, 64 * o + 64, xq, 514, "off", 8 + 4 * (o & 1), 12 + 4 * (o & 1))
+        land(N("ac"), 2 * from_mates, [P(lq + k, 64 * (r % 4), 64 * (r % 4) + 64) for r in mates for k in "cs"])
         if t == 0:
             constants_wait()
-        cc, mx_, pp, se, ff = N("cc"), N("mm"), N("pp"), N("se"), N("ff")
-
-        def lay_out(src, dst, s):
-            for k in range(8):
-                dma("sy"[k % 2], T[dst][16 * k:16 * k + 16, 0:4], VR(P(src, 0, 2, 1, 32 * o, 32 * o + 32)), s, 128,
-                    [P(src, 0, 2)], [P(dst, 0, 4, 1, 16 * k, 16 * k + 16)])
-
-        tt(P(mx_, 0, 8), P(st, 8, 16), P(st, 0, 8), A.max)
-        tt(P(cc, 0, 8), P(st, 8, 16), P(st, 0, 8), A.is_gt)
-        tt(P(N("sx"), 0, 4), P(mx_, 4, 8), P(mx_, 0, 4), A.max)
-        tt(P(N("ch"), 0, 4), P(mx_, 4, 8), P(mx_, 0, 4), A.is_gt)
-        tt(P(pp, 0, 8), P(cc, 0, 8), P("j64", 0, 8), A.add)
-        tt(P(N("qq"), 0, 4), P(N("ch"), 0, 4), P(pp, 4, 8), A.mult)
-        tt(P(ff, 0, 4), P(N("qq"), 0, 4), P(pp, 0, 4), A.max)
-        ts(P(N("om"), 0, 4), P(ff, 0, 4), 64.0, A.mult)
-        lay_out(N("om"), N("offm"), N("om"))
-        send([(partner, T[N("sx")][:, 0:4], T[se][:, 4 * block:4 * block + 4])], N("bs"), [P(N("sx"), 0, 4)])
-        copy(P(se, 4 * block, 4 * block + 4), P(N("sx"), 0, 4))
-        n = bin(masks[partner]).count("1")
-        theirs = 1 - block
-        land(N("bs"), n, [P(se, 4 * theirs, 4 * theirs + 4)])
-        if t == 0:
-            constants_lists()
         for b in range(4):
             mm((3, 0, 4, 5)[b], 128, "c2", 128 * b, "pq", 0)
+        rr, se = N("rr"), N("se")
+        scan(P(rr, 0, 4), P(st, 0, 16, 4), P(st, 0, 16, 4), LOW, A.max, A.max)
+        send([(partner, T[rr][:, 3:4], T[se][:, 0:1])], N("bs"), [P(rr, 3, 4)])
+        land(N("bs"), from_partner, [P(se, 0, 1)])
+        ts(Q("cm", 0, 3), Q(rr, 0, 3), Q(rr, 3, 4), A.is_lt, 64.0, A.mult)
+        src, out = Q("cm", 0, 4), Q("tr", 0, 1)
+        do("v", lambda: g.vector.tensor_reduce(V(out), V(src), AxisListType.X, A.add), [src], [out])
+        spread()
+        if t == 0:
+            select(P("f6", 3, 515, 4), P("f6", 3, 515, 4), [[-1, 128]], A.not_equal, 1.0, 0, 1)
         for b in range(4):
             tt(P("nd", b, 512, 4), ps((3, 0, 4, 5)[b], 0, 128), P("wm", b, 512, 4), A.max)
-        quant("nq", 0, 128, P("nd", 0, 512))
-        mm(7, 128, "c3", 0, "nq", 0)
+        fold("offm", 1.0)
         mq, eq = N("mq"), N("eq")
-        pick(mq, 0, 64, lq, 256, N("offm"), 0, 4)
+        pick(mq, 0, 64, lq, 256, "offm", 0, 4)
+        theirs = 1 - block
         send([(partner, U8(mq + "c", 0, 64), U8(eq + "c", 64 * block, 64 * block + 64))], N("bc"), [P(mq + "c", 0, 64)])
         send([(partner, T[mq + "s"][:, 0:64], T[eq + "s"][:, 64 * block:64 * block + 64])], N("bc"), [P(mq + "s", 0, 64)])
-        pick(eq, 64 * block, 64 * block + 64, lq, 256, N("offm"), 0, 4)
-        land(N("bc"), 2 * n, [P(eq + k, 64 * theirs, 64 * theirs + 64) for k in "cs"])
-        tt(P(N("c2f"), 0, 4), P(se, 4, 8), P(se, 0, 4), A.is_gt)
-        tt(P(N("f2f"), 0, 4), P(N("c2f"), 0, 4), P("j64", 0, 4), A.add)
-        ts(P(N("oe"), 0, 4), P(N("f2f"), 0, 4), 64.0, A.mult)
-        lay_out(N("oe"), N("offe"), N("oe"))
+        land(N("bc"), 2 * from_partner, [P(eq + k, 64 * theirs, 64 * theirs + 64) for k in "cs"])
+        pair = [Q(rr, 3, 4), Q(se, 0, 1)]
+        ts(Q("tr", 0, 1), pair[theirs], pair[block], A.is_gt, Q("p2", 0, 1), A.add)
+        spread()
+        pick(eq, 64 * block, 64 * block + 64, lq, 256, "offm", 0, 4)
+        quant("nq", 0, 128, P("nd", 0, 512))
+        fold("offe", 64.0)
+        tq, hq, tl = N("tq"), N("hq"), N("tl")
+        pick(tq, 0, 64, eq, 128, "offe", 0, 4)
+        for b in range(4):
+            mm(b, 128, "wq", 128 * b, tq, 0)
+        for b in range(4):
+            if b % 2:
+                ts(P("hb", 256 + b, 512, 4), ps(b, 0, 64), 0.03125, A.mult)
+            else:
+                act(P("hb", 256 + b, 512, 4), ps(b, 0, 64), scale=0.03125)
+        quant(hq, 0, 128, P("hb", 0, 512))
+        spot = {r: (tl, 64 * ((o ^ r) & 1)) for r in far}
+        spot[near[0]] = (hq, 128)
+        send([(r, U8(hq + "c", 64, 128), U8(spot[r][0] + "c", spot[r][1], spot[r][1] + 64)) for r in mates], N("gc"),
+             [P(hq + "c", 64, 128)], N("gn"))
+        send([(r, T[hq + "s"][:, 64:128], T[spot[r][0] + "s"][:, spot[r][1]:spot[r][1] + 64]) for r in mates], N("gc"),
+             [P(hq + "s", 64, 128)], N("gn"))
+        land(N("gc"), 2 * (from_mates - from_near), [P(tl + k, 0, 128) for k in "cs"])
+        land(N("gn"), 2 * from_near, [P(hq + k, 128, 192) for k in "cs"])
         if t == 0:
+            constants_swap()
             constants_last()
+
+        def unpack(a, src, first, bank):
+            for b in range(4):
+                mm(bank + b, 128, "c6", 128 * b, src, first)
+            for b in range(4):
+                act(P("yt%d" % b, a, a + 128), ps(bank + b, 0, 128))
+
+        mm(7, 128, "c3", 0, "nq", 0)
         tt(P("lx", 0, 128), ps(7, 0, 128), P("lm", 0, 128), A.mult)
         scan(P("ls", 0, 128), P("d0b", 0, 128), P("lx", 0, 128), 0.0, A.mult, A.add)
         ts(P("offs", 0, 32), P("ls", 3, 128, 4), float(511 - 64 * o), A.add, 256.0, A.min)
@@ -451,38 +491,22 @@ def rank_program(g, core, T, topo):
                 quant("c4", 128 * b, 128 * b + 128, P("f4", 3 - b, 515 - b))
                 mm(4 + b, 128, "c4", 128 * b, "nq", 0)
             for b in range(4):
-                ts(P("wo", b, 512, 4, 0, 8), ps(4 + b, 0, 128, 8), -1.0, A.mult, 255.0, A.add, rows=True)
+                ts(P("wo", b, 512, 4, 0, 8), ps(4 + b, 0, 128, 8), -1.0, A.mult, 255.0, A.add)
             dma("y", T.wl[:, 0:512], T.wo[0:8, 0:512], "done", 0, [P("wo", 0, 512)], [])
-        tq, hq, tl = N("tq"), N("hq"), N("tl")
-        pick(tq, 0, 64, eq, 128, N("offe"), 0, 4)
-        for b in range(4):
-            mm(b, 128, "wq", 128 * b, tq, 0)
-        for b in range(4):
-            if b % 2:
-                ts(P("hb", b, 256, 4), ps(b, 0, 64), 0.03125, A.mult)
-            else:
-                act(P("hb", b, 256, 4), ps(b, 0, 64), scale=0.03125)
-        quant(hq, 0, 128, P("hb", 0, 512))
-        slot = {r: 64 * ((o ^ (r % 4)) - 1) for r in mates}
-        send([(r, U8(hq + "c", 0, 64), U8(tl + "c", slot[r], slot[r] + 64)) for r in mates], N("gc"), [P(hq + "c", 0, 64)])
-        send([(r, T[hq + "s"][:, 0:64], T[tl + "s"][:, slot[r]:slot[r] + 64]) for r in mates], N("gc"), [P(hq + "s", 0, 64)])
-        land(N("gc"), 2 * sum(bin(masks[r]).count("1") for r in mates), [P(tl + k, 0, 192) for k in "cs"])
-        if t == 0:
-            constants_swap()
-        for a, n, src, bank in ((0, 64, hq, 4), (64, 192, tl, 0)):
-            for b in range(4):
-                mm(bank + b, max(n, 128), "c6", 128 * b, src, 0)
-            for b in range(4):
-                (copy if b % 2 and a == 0 else act)(P("yt%d" % b, a, a + n), ps(bank + b, 0, n))
+        else:
+            quant("vq", 0, 128, P("vt", 0, 512))
+            quant("tq%d" % (t + 1), 0, 128, P("zt", 0, 512))
+        unpack(0, hq, 64, 4)
+        unpack(128, tl, 0, 0)
     for k, (a, b) in enumerate(pieces):
         new_state(ROUNDS - 1, a, b)
         quant("xq2", a, b, P(state[ROUNDS], 4 * a, 4 * b))
         mm(4 + k, b - a, "vq", 0, "xq2", a)
         act(P("yo", a, b), ps(4 + k, 0, b - a))
         dma("y", T.oc[:, 4 * a:4 * b], U8("xq2c", a, b), "done", 0, [P("xq2c", a, b)], [])
-        dma("y", T.y[:, a:b], V(P("yo", a, b)), "done", 0, [P("yo", a, b)], [])
+        dma("ys"[k], T.y[:, a:b], V(P("yo", a, b)), "done", 0, [P("yo", a, b)], [])
     for k in range(4):
-        dma("s", T.osc[4 * k:4 * k + 4, 0:512], T.xq2s[32 * k:32 * k + 4, 0:512], "done", 0, [P("xq2s", 0, 512)], [])
+        dma("y", T.osc[4 * k:4 * k + 4, 0:512], T.xq2s[32 * k:32 * k + 4, 0:512], "done", 0, [P("xq2s", 0, 512)], [])
     for s in total:
         if waited.get(s, 0) < total[s]:
             g.wait_ge(T.sem[s], total[s])

@@ -10,6 +10,11 @@ NONE = -float(2 ** 84)
 LOW = -float(2 ** 85)
 MISS = -float(2 ** 90)
 ROUNDS = 2
+FOUR = 1
+AHEAD = (0, 2)
+SC1 = (0, 0)
+NEAR = 8
+TAIL = ((0, 256), (256, 384), (384, 512))
 HEAD = 64
 
 SCRATCH = {}
@@ -35,31 +40,31 @@ def _parts(name, dtype, *parts):
 
 for _k in range(8):
     SCRATCH["ps%d" % _k] = ("psum", [128, 512], "float32")
-for _n, _c in (("xa", 2056), ("xb", 2056), ("xc", 2048), ("ut", 512), ("vt", 512), ("wm", 512), ("nd", 512), ("zb", 1040),
-               ("hb", 512), ("zt", 520), ("junk", 1408), ("yt0", 272), ("yt1", 272), ("yt2", 272), ("yt3", 272),
+for _n, _c in (("xa", 2056), ("xb", 2056), ("xc", 2048), ("ut", 512), ("vt", 512), ("wm", 1024), ("nd", 512), ("zb", 1040),
+               ("hw", 512), ("hb", 512), ("zt", 520), ("junk", 1408), ("yt", 528),
                ("f1", 1032), ("f2", 520), ("f3", 520), ("f4", 520), ("f5", 520), ("f6", 520)):
     _sb(_n, _c, "bfloat16")
 for _n, _c in (("sq", 512), ("acc", 16), ("dg", 32), ("yo", 512), ("wo", 512)):
     _sb(_n, _c, "float32")
 _parts("work", "float32", ("va", 512), ("vb", 512), ("sa", 520), ("sb", 520))
-_parts("fixed", "float32", ("m8", 8), ("k8", 8), ("d5", 128), ("d0b", 128), ("lm", 128), ("d3", 32), ("d3b", 32), ("d4", 8),
-       ("im", 128), ("uf", 16), ("gcol", 8), ("last", 8), ("rs", 64), ("p2", 8))
-_parts("lists", "float32", ("lx", 128), ("ls", 128))
+_parts("fixed", "float32", ("m8", 8), ("k8", 8), ("d5", 128), ("lm", 32), ("d3", 16), ("wr", 48), ("wx", 32), ("im", 128), ("uf", 16),
+       ("gcol", 8), ("rs", 64), ("kk", 64), ("has", 64), ("part", 64), ("bcol", 8), ("p2", 8))
+_parts("lists", "float32", ("la", 128))
 _parts("choose", "float32", ("cm", 8), ("tr", 32), ("row", 32), ("bc", 64), ("mk", 64), ("fold", 64))
-_parts("whole", "int32", ("ip", 128), ("ip2", 128), ("il", 128), ("il2", 128), ("bi", 128), ("bj", 128))
-for _n, _c in (("ulist", 16), ("off", 16), ("offs", 32), ("offm", 4), ("offe", 4)):
+_parts("whole", "int32", ("ip", 128), ("ip2", 128), ("il", 32), ("il2", 32), ("bi", 128), ("bj", 128), ("ib", 8))
+for _n, _c in (("ulist", 16), ("off", 16), ("offs", 128), ("offm", 4), ("offe", 8)):
     _sb(_n, _c, "uint16")
-for _n, _c in (("uq", 128), ("up", 256), ("vq", 128), ("wq", 512), ("c1", 1024), ("c2", 512), ("c3", 128), ("c4", 512),
-               ("c5", 128), ("c6", 512), ("pq", 128), ("nq", 128), ("zq", 256), ("xq2", 512)):
+for _n, _c in (("uq", 128), ("up", 256), ("vq", 128), ("wq", 512), ("c1", 512), ("c2", 256), ("c3", 128), ("c4", 512),
+               ("c5", 128), ("c6", 512), ("pq", 256), ("nq", 128), ("zq", 256), ("xq2", 512)):
     _mx(_n, _c)
 for _t in range(ROUNDS):
-    for _n, _c in (("xq", 544), ("cq", 192), ("lq", 256), ("mq", 64), ("eq", 128), ("tq", 128), ("hq", 192), ("tl", 128)):
+    for _n, _c in (("xq", 544), ("cq", 192), ("lq", 256), ("eq", 256), ("hq", 224)):
         _mx("%s%d" % (_n, _t), _c)
     _parts("run%d" % _t, "float32", ("ra%d" % _t, HEAD + 520), ("rb%d" % _t, HEAD + 520))
-    for _n, _c in (("st", 16), ("rr", 8), ("se", 4)):
+    for _n, _c in (("st", 16), ("rr", 4), ("se", 4)):
         _sb("%s%d" % (_n, _t), _c, "float32")
-SEMAPHORES = ["nv", "ns", "nt", "ng", "lu", "lxa", "lxb", "lw", "lv", "done", "left"] + [
-    "%s%d" % (a, t) for t in range(ROUNDS) for a in ("ac", "as", "bc", "bs", "gc", "gn")]
+SEMAPHORES = ["nv", "ns", "nt", "ng", "lu", "lx0", "lx1", "lx2", "lw", "lv", "done", "left"] + [
+    "%s%d" % (a, t) for t in range(ROUNDS) for a in ("ac", "ad", "as", "bc", "bs", "gc")]
 
 
 def rank_program(g, core, T, topo):
@@ -100,8 +105,6 @@ def rank_program(g, core, T, topo):
                 else:
                     if not (w or w2) or not meet(p, p2):
                         continue
-                if q2 == q and not w2:
-                    continue
                 out[tok[0]] = max(out.get(tok[0], 0), tok[1])
         return out
 
@@ -120,12 +123,12 @@ def rank_program(g, core, T, topo):
         for p in writes:
             seen.setdefault(p[0], []).append((p, True, q, tok))
 
-    def do(q, call, reads, writes):
+    def do(q, call, reads, writes, alike=False):
         wait(q, conflicts(q, reads, writes))
         s = counter[q]
         if q == "g":
             rows = {p[4:6] for p in reads + writes}
-            if total.get(s) and rows | span[0] != {(0, 128)}:
+            if total.get(s) and rows | span[0] != {(0, 128)} and not alike:
                 wait(q, {s: total[s]})
             span[0] = rows
         total[s] = total.get(s, 0) + 1
@@ -157,7 +160,9 @@ def rank_program(g, core, T, topo):
         do("v", lambda: g.vector.tensor_copy(V(out), V(a)), [a], [out])
 
     def scan(out, d0, d1, initial, op0, op1):
-        do("v", lambda: g.vector.tensor_tensor_scan(V(out), V(d0), V(d1), initial, op0, op1), [d0, d1], [out])
+        held = isinstance(initial, tuple)
+        do("v", lambda: g.vector.tensor_tensor_scan(V(out), V(d0), V(d1), V(initial) if held else initial, op0, op1),
+           [d0, d1] + [initial] * held, [out])
 
     def act(out, a, func=F.Copy, scale=None, bias=None):
         more = {k: x for k, x in (("scale", scale), ("bias", bias)) if x is not None}
@@ -205,19 +210,19 @@ def rank_program(g, core, T, topo):
     share = len(outside) // len(far)
     masks = {r: bitmask(outside[k * share:(k + 1) * share]) for k, r in enumerate(far)}
     inside = [e for e in topo.engines(core, T.cores[near[0]]) if e not in outside]
-    masks[near[0]] = bitmask(inside)
+    masks[near[0]] = bitmask(inside[:NEAR])
     assert [r % 4 for r in near] == [o ^ 1]
     masks[partner] = topo.mask(core, T.cores[partner])
     from_mates = sum(bin(masks[r]).count("1") for r in mates)
     from_partner = bin(masks[partner]).count("1")
-    from_near = len(inside)
+    halves = [masks[r] for r in far]
 
-    def send(moves, s, reads, s_near=None):
+    def send(moves, reads):
         wait("g", conflicts("g", reads, []))
-        g.remote_dma_fused([RemoteDMATransfer(dst_ids=[address(r)], dma_engine_mask=masks[r],
-                                              remote_sem=T.sem[s_near if s_near and r in near else s], src=a, dst=b)
-                            for r, a, b in moves], local_sem=T.sem.left)
-        total["left"] = total.get("left", 0) + sum(bin(masks[r]).count("1") for r, a, b in moves)
+        moves = [m if len(m) == 5 else m + (masks[m[0]],) for m in moves]
+        g.remote_dma_fused([RemoteDMATransfer(dst_ids=[address(r)], dma_engine_mask=e, remote_sem=T.sem[s], src=a, dst=b)
+                            for r, a, b, s, e in moves], local_sem=T.sem.left)
+        total["left"] = total.get("left", 0) + sum(bin(m[4]).count("1") for m in moves)
 
     def land(s, n, places):
         total[s] = n
@@ -226,12 +231,11 @@ def rank_program(g, core, T, topo):
     def U8(name, a, b):
         return T[name][:, a:b].bitcast(dt.uint8)
 
-    pieces = ((0, 384), (384, 512))
-    cut = 4 * pieces[0][1]
+    pieces = ((0, 256), (256, 384), (384, 512))
     dma("s", T.ut[:], T.u[:], "lu", 16, [], [P("ut", 0, 512)])
-    dma("y", T.xa[:, 0:cut], T.x[:, 0:cut], "lxa", 16, [], [P("xa", 0, cut)])
-    dma("y", T.xa[:, cut:2048], T.x[:, cut:2048], "lxb", 16, [], [P("xa", cut, 2048)])
-    wait("y", {"lxa": 16, "lxb": 16})
+    for k, (a, b) in enumerate(pieces):
+        dma("y", T.xa[:, 4 * a:4 * b], T.x[:, 4 * a:4 * b], "lx%d" % k, 16, [], [P("xa", 4 * a, 4 * b)])
+    wait("y", {"lx%d" % k: 16 for k in range(3)})
     dma("y", U8("wqc", 0, 512), T.wc[:], "lw", 32, [], [P("wqc", 0, 512)])
     dma("y", T.wqs[:], T.ws[:], "lw", 32, [], [P("wqs", 0, 512)])
     dma("y", T.vt[:], T.v[:], "lv", 16, [], [P("vt", 0, 512)])
@@ -246,247 +250,342 @@ def rank_program(g, core, T, topo):
         do("g", lambda: g.affine_select(V(out), V(src), pattern, op, value, base, ch), [src], [out])
 
     iota(P("ip", 0, 128), [[0, 8], [-1, 16]], 16, 1)
-    iota(P("im", 0, 128), [[1, 128]], 0, 0, True)
+    iota(P("im", 0, 128), [[128 - 256 * (1 - (o >> 1)), 2], [2, 64]], 128 * (1 - (o >> 1)), 0, True)
     iota(P("uf", 0, 16), [[16, 16]], 1, 0, True)
     select(P("uf", 0, 16), P("uf", 0, 16), [[-1, 16]], A.is_ge, 15.0, 7, 0)
     fill(P("zt", 0, 520), 0.0)
     act(P("f1", 0, 516), P("zt", 0, 516))
     act(P("f1", 516, 1032), P("zt", 0, 516))
-    act(P("zb", 0, 520), P("zt", 0, 520))
-    act(P("zb", 520, 1040), P("zt", 0, 520))
+    act(P("f2", 0, 520), P("zt", 0, 520))
     for k in range(4):
         fill(P("gcol", 0, 1, 1, 32 * k, 32 * k + 32), 2.0 ** (6 - 2 * k))
     for k in range(4):
         fill(P("gcol", 0, 1, 1, 32 * k, 32 * k + 16), 2.0 ** (7 - 2 * k))
     ts(P("ip2", 0, 128), P("ip", 0, 128), 15, A.bitwise_and)
+    fill(P("xa", 2048, 2056), 0.0)
     ts(P("bi", 0, 128), P("im", 0, 128), P("gcol", 0, 1), A.mult)
     ts(P("d5", 0, 128), P("ip2", 0, 128), 0.0, A.is_equal)
+    fill(P("wm", 2, 1024, 4), 0.0)
     ts(P("bj", 0, 128), P("bi", 0, 128), 128, A.bitwise_and)
-    ts(P("last", 0, 1), P("gcol", 0, 1), 1.0, A.is_equal, P("d5", 0, 1), A.mult)
-    fill(P("xa", 2048, 2056), 0.0)
-    top = 512 * (o >> 1)
-    ts(P("f1", 515 - top, 1027 - top, 4), P("bj", 0, 128), P("d5", 0, 1), A.mult)
-    ts(P("f1", 3 + top, 515 + top, 4), P("bj", 0, 128), P("d5", 0, 1), A.mult, P("last", 0, 1), A.add)
+    fill(P("wm", 3, 1024, 4), 0.0)
+    ts(P("f1", 3, 1027, 8), P("bj", 0, 128), P("d5", 0, 1), A.mult)
+    ts(P("f1", 7, 1031, 8), P("bj", 0, 128), 0.0, A.is_equal, P("d5", 0, 1), A.mult)
     copy(P("ulist", 0, 16), P("uf", 0, 16))
     for e, w in ((0, 64.0), (1, 8.0), (2, 1.0), (3, 0.0)):
         act(P("f5", e, 512, 4), P("d5", 0, 128), scale=w)
-    act(P("f2", 0, 520), P("zt", 0, 520))
-    for b in range(2):
-        quant("c1", 256 * b, 256 * b + 256, P("f1", 3 - b, 1027 - b))
+    fill(P("sa", 512, 516), NONE)
+    fill(P("sb", 512, 516), NONE)
+    quant("c1", 0, 256, P("f1", 3, 1027))
     quant("uq", 0, 128, P("ut", 0, 512))
+    quant("c1", 256, 512, P("f1", 2, 1026))
     pick("up", 0, 128, "uq", 128, "ulist", 0, 8)
-    pick("up", 128, 256, "uq", 128, "ulist", 8, 16)
-    for name, inside_value, outside_value in (("m8", 1, 0.0), ("k8", -8, -1024.0)):
-        iota(P(name, 0, 8), [[0, 8]], inside_value, 0, True)
-        select(P(name, 0, 8), P(name, 0, 8), [[-16, 8]], A.is_ge, outside_value, 0, 1)
-        select(P(name, 0, 8), P(name, 0, 8), [[16, 8]], A.is_ge, outside_value, 15, -1)
-    iota(Q("cm", 3, 4), [[0, 1]], 0, 1, True)
-    iota(P("d3", 0, 32), [[0, 32]], 0, 0, True)
-    for k in range(8):
-        turned = (64 * o >> k) & 1
-        select(P("d3", 0, 32), P("d3", 0, 32), [[-16, 8], [0, 4]], A.not_equal, float(2 ** k if turned else -2 ** k), -2 - k, 1)
-    select(P("d3", 0, 32), P("d3", 0, 32), [[-17, 8], [0, 4]], A.not_equal, 0.0, -2, 1)
-    select(P("d3b", 0, 32), P("d3", 0, 32), [[-16, 8], [0, 4]], A.not_equal, -256.0, 0, 1)
+    iota(P("m8", 0, 8), [[0, 8]], 1, 0, True)
+    iota(P("il", 0, 32), [[4, 32]], 259, -1)
+    select(P("m8", 0, 8), P("m8", 0, 8), [[-64, 2], [16, 4]], A.is_ge, 0.0, -48, 1)
     select(P("f2", 3, 515, 4), P("f2", 3, 515, 4), [[0, 8], [16, 16]], A.not_equal, 1.0, -32, -1)
+    select(P("m8", 0, 8), P("m8", 0, 8), [[64, 2], [-16, 4]], A.is_ge, 0.0, 63, -1)
     select(P("f2", 3, 515, 4), P("f2", 3, 515, 4), [[16, 8], [1000, 16]], A.not_equal, 1.0, 0, -1)
+    iota(Q("cm", 3, 4), [[0, 1]], 0, 1, True)
 
     def constants_early():
-        for b in range(2, 4):
-            quant("c1", 256 * b, 256 * b + 256, P("f1", 3 - b, 1027 - b))
-
-    def constants_mid():
-        fill(P("sa", 512, 516), NONE)
-        fill(P("sb", 512, 516), NONE)
         for r in ("ra0", "rb0"):
             fill(P(r, 0, HEAD), LOW)
+        fill(Q("tr", 0, 32), 0.0)
+        ts(P("k8", 0, 8), P("m8", 0, 8), 1016.0, A.mult, -1024.0, A.add)
+
+    def constants_mid():
+        act(P("zb", 520, 1040), P("zt", 0, 520))
         quant("c5", 0, 128, P("f5", 0, 512))
 
     def constants_wait():
-        act(Q("p2", 0, 1), Q("cm", 3, 4), scale=1.0 / 64)
-        for f in ("f6", "f4", "f3"):
+        for f in ("f6", "f3", "f4"):
             act(P(f, 0, 520), P("zt", 0, 520))
-        for b in range(4):
-            act(P("f3", 5 * b, 512, 16), P("d3b", 0, 32))
-        fill(Q("tr", 0, 32), 0.0)
+        act(Q("p2", 0, 1), Q("cm", 3, 4), scale=1.0 / 64)
+        fill(P("kk", 0, 64), 4096.0)
         fill(P("rs", 0, 64), 1.0)
-        fill(P("hb", 0, 512), 0.0)
-        fill(P("rs", 0, 64, 16), 0.0)
-        for b in range(4):
-            quant("c2", 128 * b, 128 * b + 128, P("f2", 3 - b, 515 - b))
-        quant("tq0", 0, 128, P("zt", 0, 512))
+        copy(P("bcol", 2, 3), P("ip2", 0, 1))
+        ts(P("il2", 0, 32), P("il", 0, 32), 12, A.bitwise_and)
+        for s in range(4):
+            fill(P("kk", 16 * s, 16 * s + 1), 0.75 - 0.25 * s)
+        quant("eq0", 64, 192, P("zt", 0, 512))
+        own = 64 + 32 * (o & 1)
+        ts(P("has", 0, 32), P("bj", own, own + 32), 0.0, A.not_equal)
+        ts(P("has", 32, 64), P("bj", own, own + 32), 0.0, A.is_equal)
+        ts(P("lm", 0, 32), P("il2", 0, 32), 0.0, A.is_equal)
 
-    def constants_last():
-        for b in range(4):
-            quant("c6", 128 * b, 128 * b + 128, P("f6", 3 - b, 515 - b))
-        quant("c3", 0, 128, P("f3", 0, 512))
-        fill(P("d0b", 0, 128), 1.0)
-        ts(P("il2", 0, 128), P("il", 0, 128), 12, A.bitwise_and)
-        fill(P("d0b", 0, 128, 4), 0.0)
-        ts(P("lm", 0, 128), P("il2", 0, 128), 0.0, A.is_equal)
-        for b in range(4):
-            fill(P("yt%d" % b, 256, 272), 0.0)
+    def constants_weights():
+        fill(P("wr", 0, 32), 0.0)
+        fill(P("wr", 32, 48), 2.0)
+        fill(P("rs", 0, 64, 8), 0.0)
+        ts(P("ib", 0, 1), P("ip", 0, 1), 3, A.bitwise_and)
+        scan(P("wr", 18, 26), P("wr", 32, 40), P("wr", 0, 8), 0.5, A.mult, A.add)
+        for s in range(2):
+            tt(P("part", s, 64, 2), P("has", 32 * s, 32 * s + 32), P("lm", 0, 32), A.mult)
+        copy(P("bcol", 0, 1), P("ib", 0, 1))
+        ts(P("wr", 3, 8), P("wr", 19, 24), -1.0, A.mult)
+        for at, w in ((0, -1024.0), (2, 256.0), (8, 64.0 if o & 1 else -64.0), (9, 128.0 if o & 2 else -128.0)):
+            fill(P("wr", at, at + 1), w)
+
+    def constants_hop():
+        fill(P("hb", 0, 384), 0.0)
+        tt(P("wx", 0, 32), P("wr", 0, 32), P("d5", 0, 32), A.mult)
+        ts(P("bcol", 1, 2), P("ib", 0, 1), -2.0, A.add)
+        fill(P("yt", 512, 528), 0.0)
         fill(P("xb", 2048, 2056), 0.0)
+        for k in range(2):
+            src, out = P("wx", 16 * k, 16 * k + 16), P("bcol", 4 + k, 5 + k)
+            do("v", lambda: g.vector.tensor_reduce(V(out), V(src), AxisListType.X, A.add), [src], [out])
         for r in ("ra1", "rb1"):
             fill(P(r, 0, HEAD), LOW)
+        for k in range(2):
+            ts(P("d3", 8 * k, 8 * k + 8), P("wr", 32, 40), P("bcol", 4 + k, 5 + k), A.mult, 0.5, A.mult)
 
-    def constants_swap():
-        iota(P("il", 0, 128), [[4, 128]], 259, -1)
-        iota(P("d4", 0, 8), [[0, 8]], 0, 0, True)
-        for k in range(8):
-            select(P("d4", 0, 8), P("d4", 0, 8), [[-16, 8]], A.not_equal, float(2 ** k), -2 - k, 1)
-        select(P("d4", 0, 8), P("d4", 0, 8), [[-17, 8]], A.not_equal, 0.0, -2, 1)
+    def constants_blocks():
+        select(P("d3", 0, 16), P("d3", 0, 16), [[0, 2], [-16, 8]], A.is_ge, 0.0, 0, 1)
+        select(P("f6", 3, 515, 4), P("f6", 3, 515, 4), [[-1, 128]], A.not_equal, 1.0, 0, 1)
+        select(P("d3", 0, 16), P("d3", 0, 16), [[0, 2], [16, 8]], A.is_ge, 0.0, 15, -1)
+        select(P("d3", 0, 16), P("d3", 0, 16), [[0, 2], [-17, 8]], A.not_equal, 0.0, -2, 1)
+
+    def constants_lists():
+        for r in range(16):
+            act(P("f3", 4 * r + r // 4, 512, 64), P("d3", 0, 8))
+        for e in range(2):
+            quant("c2", 128 * e, 128 * e + 128, P("f2", 3 - e, 515 - e))
+        for b in range(4):
+            quant("c6", 128 * b, 128 * b + 128, P("f6", 3 - b, 515 - b))
 
     state = ["xa", "xb", "xc"]
 
     def new_state(t, a, b):
-        X, Z = state[t], state[t + 1]
-        for e in range(4):
-            i, y = P("offs", a // 16, b // 16), P("yt%d" % e, 0, 272)
-            do("v", lambda: g.vector.tensor_tensor(T[Z][:, 4 * a + e:4 * b:4], V(y).indirect(V(i)), T[X][:, 4 * a + e:4 * b:4], A.add),
-               [y, i, P(X, 4 * a + e, 4 * b, 4)], [P(Z, 4 * a + e, 4 * b, 4)])
+        i, y, x, z = P("offs", a // 4, b // 4), P("yt", 0, 528), P(state[t], 4 * a, 4 * b), P(state[t + 1], 4 * a, 4 * b)
+        do("v", lambda: g.vector.tensor_tensor(V(z), V(y).indirect(V(i)), V(x), A.add), [y, i, x], [z])
 
-    def spread():
-        do("v", lambda: g.vector.transpose(V(Q("row", 0, 32)), V(Q("tr", 0, 32))), [Q("tr", 0, 32)], [Q("row", 0, 32)])
-        for k in range(2):
-            first = 64 * (o & 1) + 32 * k
-            src, out = P("row", 0, 32, 1, first, first + 1), P("bc", 32 * k, 32 * k + 32)
-            do("g", lambda: g.partition_broadcast(V(out), V(src), 128), [src], [out])
-
-    def fold(dst, scale):
-        tt(P("mk", 0, 64), P("bc", 0, 64), P("d5", 0, 64), A.mult)
-        scan(P("fold", 0, 64), P("rs", 0, 64), P("mk", 0, 64), 0.0, A.mult, A.add)
-        ts(P(dst, 0, 4), P("fold", 15, 64, 16), scale, A.mult)
+    def by_pieces(t, then):
+        for k in range(-1, len(pieces)):
+            if t >= 0 and k + 1 < len(pieces):
+                new_state(t, *pieces[k + 1])
+            if k >= 0:
+                then(k, *pieces[k])
 
     for t in range(ROUNDS):
         N = lambda s: "%s%d" % (s, t)
         X, xq = state[t], N("xq")
         last = t == ROUNDS - 1
-        for k, (a, b) in enumerate(pieces):
-            if t:
-                new_state(t - 1, a, b)
+
+        def scores(k, a, b):
             more = 2 if b == 512 else 0
             quant(xq, a, b + more, P(X, 4 * a, 4 * (b + more)))
-            mm((1, 3)[k], b - a, "up", 0, xq, a)
-            mm((0, 4)[k], b - a, "uq", 0, xq, a)
-            act(P("sq", a, b), ps((1, 3)[k], 0, b - a))
-        if t == 0:
-            constants_early()
-        mm(2, 512, "up", 128, xq, 0)
-        for k, (a, b) in enumerate(pieces):
-            tt(P("wm", a, b), ps((0, 4)[k], 0, b - a), P("sq", a, b), A.is_le)
-        quant("pq", 0, 128, P("wm", 0, 512))
-        if t == 0:
-            constants_mid()
-        banks = ((5, 6, 7, 1), (3, 0, 4, 5))
-        st, cq, lq = N("st"), N("cq"), N("lq")
+            mm((1, 3, 5)[k], b - a, "up", 0, xq, a)
+            mm((0, 4, 6)[k], b - a, "uq", 0, xq, a)
+            act(P("sq", a, b), ps((1, 3, 5)[k], 0, b - a))
+
+        def marks(k):
+            a, b = pieces[k]
+            at = 512 * (a // 256) + 2 * (a % 256)
+            for e in range(2):
+                tt(P("wm", at + e, at + 2 * (b - a), 4), P("ps%d" % (0, 4, 6)[k], e, b - a, 2), P("sq", a + e, b, 2), A.is_le)
+
+        def missing(j):
+            quant("pq", 128 * j, 128 * j + 128, P("wm", 512 * j, 512 * j + 512))
+            for h in range(2):
+                for e in range(2):
+                    bank = ((7, 1, 0, 3), (5, 4, 6, 7))[j][2 * h + e]
+                    mm(bank, 128, "c1", 256 * e + 128 * h, "pq", 128 * j)
+                    act(P(("va", "vb")[h], 256 * j + e, 256 * j + 256, 2), ps(bank, 0, 128), scale=MISS)
+
+        def maxima(j):
+            a, b = 256 * j, 256 * j + 256
+            for h in range(2):
+                tt(P(("sa", "sb")[h], a, b), ps(2, a, b), P(("va", "vb")[h], a, b), A.add)
+            for h in range(2):
+                sa, run = P(("sa", "sb")[h], a, b + j), N(("ra", "rb")[h])
+                scan(P(run, HEAD + a, HEAD + b + j), sa, sa, P(run, HEAD + a - 1, HEAD + a), A.max, A.max)
+                if j:
+                    strongest(h, run)
+
+        def strongest(h, run):
+            send([(r, V(P(run, end, end + 1)), T[st][:, 4 * o:4 * o + 1], N("as")) for r in (far, near)[h]], [P(run, end, end + 1)])
+            for k, step in enumerate((64, 8, 1)):
+                if h and k == 2:
+                    act(digit(0, 2), P("k8", 0, 8), F.Relu, count(0, 1), count(0, 2))
+                below(count(h, k), run, step, 704 * h + (0, 16, 128)[k])
+
+        st, cq, lq, rr, se = N("st"), N("cq"), N("lq"), N("rr"), N("se")
         end = HEAD + 512
         count = lambda h, k: P("acc", 8 * h + k, 8 * h + k + 1)
         digit = lambda h, k: P("zb", 520 * h + k, 520 * h + 32, 4)
-        for h in range(2):
-            for b in range(4):
-                mm(banks[h][b], 128, "c1", 256 * b + 128 * h, "pq", 0)
-                act(P("vb", b, 512, 4) if h else P("va", 128 * b, 128 * b + 128), ps(banks[h][b], 0, 128), scale=MISS)
-        for h in range(2):
-            if h:
-                tt(P("sb", 0, 512), ps(2, 0, 512), P("vb", 0, 512), A.add)
-            else:
-                for b in range(4):
-                    tt(P("sa", b, 512, 4), P("ps2", b, 512, 4), P("va", 128 * b, 128 * b + 128), A.add)
-            sa, run = P(("sa", "sb")[h], 0, 513), N(("ra", "rb")[h])
-            scan(P(run, HEAD, end + 1), sa, sa, LOW, A.max, A.max)
-            send([(r, V(P(run, end, end + 1)), T[st][:, 4 * o:4 * o + 1]) for r in (far, near)[h]], N("as"), [P(run, end, end + 1)])
-            for k, step in enumerate((64, 8, 1)):
-                below(count(h, k), run, step, 704 * h + (0, 16, 128)[k])
-            if h == 0:
-                act(digit(0, 0), P("m8", 0, 8), scale=count(0, 0))
-                act(digit(0, 1), P("k8", 0, 8), F.Relu, count(0, 0), count(0, 1))
-            act(digit(h, 2), P("k8", 0, 8), F.Relu, count(h, 1), count(h, 2))
+        if t:
+            new_state(t - 1, *pieces[0])
+            new_state(t - 1, *pieces[1])
+        scores(0, *pieces[0])
+        if t:
+            new_state(t - 1, *pieces[2])
+        else:
+            pick("up", 128, 256, "uq", 128, "ulist", 8, 16)
+        scores(1, *pieces[1])
+        if t:
+            marks(0)
+        scores(2, *pieces[2])
+        if t == 0:
+            constants_early()
+            marks(0)
+            fill(P("zb", 0, 520), 0.0)
+        missing(0)
+        mm(2, 512, "up", 128, xq, 0)
+        marks(1)
+        marks(2)
+        missing(1)
+        if t == 0:
+            constants_mid()
+        maxima(0)
+        maxima(1)
+        act(digit(1, 2), P("k8", 0, 8), F.Relu, count(1, 1), count(1, 2))
         land(N("as"), from_mates, [P(st, 4 * (r % 4), 4 * (r % 4) + 1) for r in mates])
         slot = {r: 64 * (r & 1) for r in far}
         slot[near[0]] = 128
-        for h in range(2):
+        mine = 64 * o
+
+        def codes(to):
+            send([(r, U8(cq + "c", slot[r], slot[r] + 64), U8(lq + "c", mine, mine + 64), N("ac")) for r in to],
+                 [P(cq + "c", slot[r], slot[r] + 64) for r in to])
+
+        def product(h):
             quant("zq", 128 * h, 128 * h + 128, P("zb", 520 * h, 520 * h + 512))
             mm(6 + h, 128, "c5", 0, "zq", 128 * h)
-            if h == 0:
-                ts(digit(1, 0), P("m8", 0, 8), count(1, 0), A.mult)
-                ts(P("dg", 0, 8), P("k8", 0, 8), count(1, 0), A.mult, count(1, 1), A.add)
+
+        def places(h):
             ts(P("off", 8 * h, 8 * h + 8), ps(6 + h, 0, 8), -float(HEAD), A.add)
-            if h == 0:
-                pick(cq, 0, 128, xq, 514, "off", 0, 8)
-                ts(digit(1, 1), P("dg", 0, 8), 0.0, A.max)
+
+        def planes(to):
+            send([(r, T[cq + "s"][:, slot[r]:slot[r] + 64], T[lq + "s"][:, mine:mine + 64], N("ad")) for r in to],
+                 [P(cq + "s", slot[r], slot[r] + 64) for r in to])
+
+        def spread():
+            do("v", lambda: g.vector.transpose(V(Q("row", 0, 32)), V(Q("tr", 0, 32))), [Q("tr", 0, 32)], [Q("row", 0, 32)])
+
+        def broadcast(k):
+            first = 64 * (o & 1) + 32 * k
+            src, out = P("row", 0, 32, 1, first, first + 1), P("bc", 32 * k, 32 * k + 32)
+            do("g", lambda: g.partition_broadcast(V(out), V(src), 128), [src], [out], k == 1)
+
+        for h in range(2):
+            if h:
                 copy(P(st, 4 * o, 4 * o + 1), P(N("rb"), end, end + 1))
-            else:
-                there = 8 + 4 * (near[0] & 1)
-                pick(cq, 128, 192, xq, 514, "off", there, there + 4)
-            send([(r, U8(cq + "c", slot[r], slot[r] + 64), U8(lq + "c", 64 * o, 64 * o + 64)) for r in (far, near)[h]], N("ac"),
-                 [P(cq + "c", slot[r], slot[r] + 64) for r in (far, near)[h]])
-        send([(r, T[cq + "s"][:, slot[r]:slot[r] + 64], T[lq + "s"][:, 64 * o:64 * o + 64]) for r in mates], N("ac"),
-             [P(cq + "s", 0, 192)])
-        pick(lq, 64 * o, 64 * o + 64, xq, 514, "off", 8 + 4 * (o & 1), 12 + 4 * (o & 1))
-        land(N("ac"), 2 * from_mates, [P(lq + k, 64 * (r % 4), 64 * (r % 4) + 64) for r in mates for k in "cs"])
+            ts(P("dg", 8 * h, 8 * h + 8), P("k8", 0, 8), count(h, 0), A.mult, count(h, 1), A.add)
+            ts(digit(h, 0), P("m8", 0, 8), count(h, 0), A.mult)
+            if h:
+                product(0)
+            ts(digit(h, 1), P("dg", 8 * h, 8 * h + 8), 0.0, A.max)
+        places(0)
+        product(1)
+        pick(cq, 0, 128, xq, 514, "off", 0, 8)
+        codes(far)
+        if FOUR:
+            planes(far)
+        def compare():
+            scan(P(rr, 0, 4), P(st, 0, 16, 4), P(st, 0, 16, 4), LOW, A.max, A.max)
+            src, top, junk, out = Q(rr, 0, 3), Q(rr, 3, 4), Q("cm", 0, 3), Q("tr", 0, 1)
+            do("s", lambda: g.scalar.activation(V(junk), V(src), F.Sign, bias=V(top), scale=-1.0, accum_out=V(out)),
+               [src, top], [junk, out])
+
+        if AHEAD[t] == 2:
+            compare()
+        places(1)
+        if AHEAD[t] == 1:
+            compare()
+        there = 8 + 4 * (near[0] & 1)
+        pick(cq, 128, 192, xq, 514, "off", there, there + 4)
+        if AHEAD[t] == 0:
+            compare()
+        spread()
+        if FOUR:
+            codes(near)
+            planes(near)
+        else:
+            planes(mates)
+            codes(near)
+        pick(lq, mine, mine + 64, xq, 514, "off", 8 + 4 * (o & 1), 12 + 4 * (o & 1))
+        for k, s in (("c", "ac"), ("s", "ad")):
+            land(N(s), from_mates, [P(lq + k, 64 * (r % 4), 64 * (r % 4 + 1)) for r in mates])
+
+        def fold(mask):
+            for k in range(2):
+                tt(P("mk", 32 * k, 32 * k + 32), P("bc", 32 * k, 32 * k + 32), P(mask, 32 * k, 32 * k + 32), A.mult)
+
+        def wishes():
+            for j in range(2):
+                for e in range(2):
+                    mm(2 * j + e, 128, "c2", 128 * e, "pq", 128 * j)
+            for j in range(2):
+                for e in range(2):
+                    tt(P("nd", 256 * j + e, 256 * j + 256, 2), ps(2 * j + e, 0, 128), P("wm", 512 * j + e, 512 * j + 512, 4), A.max)
+
+        broadcast(0)
+        broadcast(1)
+        send([(partner, T[rr][:, 3:4], T[se][:, 3:4], N("bs"))], [P(rr, 3, 4)])
         if t == 0:
             constants_wait()
-        for b in range(4):
-            mm((3, 0, 4, 5)[b], 128, "c2", 128 * b, "pq", 0)
-        rr, se = N("rr"), N("se")
-        scan(P(rr, 0, 4), P(st, 0, 16, 4), P(st, 0, 16, 4), LOW, A.max, A.max)
-        send([(partner, T[rr][:, 3:4], T[se][:, 0:1])], N("bs"), [P(rr, 3, 4)])
-        land(N("bs"), from_partner, [P(se, 0, 1)])
-        ts(Q("cm", 0, 3), Q(rr, 0, 3), Q(rr, 3, 4), A.is_lt, 64.0, A.mult)
-        src, out = Q("cm", 0, 4), Q("tr", 0, 1)
-        do("v", lambda: g.vector.tensor_reduce(V(out), V(src), AxisListType.X, A.add), [src], [out])
-        spread()
-        if t == 0:
-            select(P("f6", 3, 515, 4), P("f6", 3, 515, 4), [[-1, 128]], A.not_equal, 1.0, 0, 1)
-        for b in range(4):
-            tt(P("nd", b, 512, 4), ps((3, 0, 4, 5)[b], 0, 128), P("wm", b, 512, 4), A.max)
-        fold("offm", 1.0)
-        mq, eq = N("mq"), N("eq")
-        pick(mq, 0, 64, lq, 256, "offm", 0, 4)
+        else:
+            wishes()
+        fold("d5")
+        scan(P("fold", 0, 64), P("kk", 0, 64), P("mk", 0, 64), 4096.0, A.min, A.add)
+        ts(P("offm", 0, 4), P("fold", 15, 64, 16), 64.0, A.mult, P("bcol", 2, 3), A.add)
+        eq = N("eq")
+        pick(eq, 0, 64, lq, 256, "offm", 0, 4)
         theirs = 1 - block
-        send([(partner, U8(mq + "c", 0, 64), U8(eq + "c", 64 * block, 64 * block + 64))], N("bc"), [P(mq + "c", 0, 64)])
-        send([(partner, T[mq + "s"][:, 0:64], T[eq + "s"][:, 64 * block:64 * block + 64])], N("bc"), [P(mq + "s", 0, 64)])
-        land(N("bc"), 2 * from_partner, [P(eq + k, 64 * theirs, 64 * theirs + 64) for k in "cs"])
-        pair = [Q(rr, 3, 4), Q(se, 0, 1)]
+        for k in "sc" if SC1[t] else "cs":
+            side = U8 if k == "c" else lambda name, a, b: T[name][:, a:b]
+            send([(partner, side(eq + k, 0, 64), side(eq + k, 192, 256), N("bc"))], [P(eq + k, 0, 64)])
+        land(N("bc"), 2 * from_partner, [P(eq + k, 192, 256) for k in "cs"])
+        land(N("bs"), from_partner, [P(se, 3, 4)])
+        if t == 0:
+            constants_weights()
+
+        def layer(whose, first, bank):
+            for b in range(4):
+                mm(bank + b, 128, "wq", 128 * b, eq, 2 * first)
+            for b in range(4):
+                out, src = P("hw", 256 * whose + b, 256 * whose + 256, 4), ps(bank + b, first, first + 64)
+                if b % 2 and first:
+                    ts(out, src, 0.03125, A.mult)
+                else:
+                    act(out, src, scale=0.03125)
+
+        layer(block, 0, 0)
+        pair = [Q(rr, 3, 4), Q(se, 3, 4)]
         ts(Q("tr", 0, 1), pair[theirs], pair[block], A.is_gt, Q("p2", 0, 1), A.add)
         spread()
-        pick(eq, 64 * block, 64 * block + 64, lq, 256, "offm", 0, 4)
-        quant("nq", 0, 128, P("nd", 0, 512))
-        fold("offe", 64.0)
-        tq, hq, tl = N("tq"), N("hq"), N("tl")
-        pick(tq, 0, 64, eq, 128, "offe", 0, 4)
-        for b in range(4):
-            mm(b, 128, "wq", 128 * b, tq, 0)
-        for b in range(4):
-            if b % 2:
-                ts(P("hb", 256 + b, 512, 4), ps(b, 0, 64), 0.03125, A.mult)
-            else:
-                act(P("hb", 256 + b, 512, 4), ps(b, 0, 64), scale=0.03125)
-        quant(hq, 0, 128, P("hb", 0, 512))
-        spot = {r: (tl, 64 * ((o ^ r) & 1)) for r in far}
-        spot[near[0]] = (hq, 128)
-        send([(r, U8(hq + "c", 64, 128), U8(spot[r][0] + "c", spot[r][1], spot[r][1] + 64)) for r in mates], N("gc"),
-             [P(hq + "c", 64, 128)], N("gn"))
-        send([(r, T[hq + "s"][:, 64:128], T[spot[r][0] + "s"][:, spot[r][1]:spot[r][1] + 64]) for r in mates], N("gc"),
-             [P(hq + "s", 64, 128)], N("gn"))
-        land(N("gc"), 2 * (from_mates - from_near), [P(tl + k, 0, 128) for k in "cs"])
-        land(N("gn"), 2 * from_near, [P(hq + k, 128, 192) for k in "cs"])
+        broadcast(0)
+        broadcast(1)
         if t == 0:
-            constants_swap()
-            constants_last()
-
-        def unpack(a, src, first, bank):
-            for b in range(4):
-                mm(bank + b, 128, "c6", 128 * b, src, first)
-            for b in range(4):
-                act(P("yt%d" % b, a, a + 128), ps(bank + b, 0, 128))
-
+            constants_hop()
+            constants_blocks()
+        else:
+            quant("nq", 0, 128, P("nd", 0, 512))
+        fold("part")
+        scan(P("fold", 0, 64), P("rs", 0, 64), P("mk", 0, 64), 0.0, A.mult, A.add)
+        ts(P("offe", 0, 8), P("fold", 7, 64, 8), 256.0, A.mult, P("bcol", 0, 1), A.add)
+        hq = N("hq")
+        layer(theirs, 64, 4)
+        win, lst, out = P("hw", 0, 512), P("offe", 0, 8), P("hb", 384, 512)
+        do("v", lambda: g.vector.tensor_copy(V(out), V(win).indirect(V(lst))), [win, lst], [out])
+        quant(hq, 0, 128, P("hb", 0, 512))
+        spot = {r: 96 + 32 * (o ^ r % 4) for r in mates}
+        send([(r, U8(hq + "c", 96, 128), U8(hq + "c", spot[r], spot[r] + 32), N("gc")) for r in mates], [P(hq + "c", 96, 128)])
+        send([(r, T[hq + "s"][:, 96:128], T[hq + "s"][:, spot[r]:spot[r] + 32], N("gc")) for r in mates], [P(hq + "s", 96, 128)])
+        land(N("gc"), 2 * from_mates, [P(hq + k, 128, 224) for k in "cs"])
+        if t == 0:
+            constants_lists()
+            wishes()
+            quant("c3", 0, 128, P("f3", 0, 512))
+            quant("nq", 0, 128, P("nd", 0, 512))
         mm(7, 128, "c3", 0, "nq", 0)
-        tt(P("lx", 0, 128), ps(7, 0, 128), P("lm", 0, 128), A.mult)
-        scan(P("ls", 0, 128), P("d0b", 0, 128), P("lx", 0, 128), 0.0, A.mult, A.add)
-        ts(P("offs", 0, 32), P("ls", 3, 128, 4), float(511 - 64 * o), A.add, 256.0, A.min)
+        if t == 0:
+            quant("eq1", 64, 192, P("zt", 0, 512))
+        act(P("la", 0, 128), ps(7, 0, 128), F.Abs, 2.0, 2.0 * (1023 - 64 * o))
+        ts(P("offs", 0, 128), P("la", 0, 128), P("bcol", 1, 2), A.add, 512.0, A.min)
         if last:
-            act(P("f4", 3, 35, 4), P("d4", 0, 8))
+            act(P("f4", 3, 35, 4), P("d3", 8, 16))
             for b in range(4):
                 quant("c4", 128 * b, 128 * b + 128, P("f4", 3 - b, 515 - b))
                 mm(4 + b, 128, "c4", 128 * b, "nq", 0)
@@ -495,18 +594,32 @@ def rank_program(g, core, T, topo):
             dma("y", T.wl[:, 0:512], T.wo[0:8, 0:512], "done", 0, [P("wo", 0, 512)], [])
         else:
             quant("vq", 0, 128, P("vt", 0, 512))
-            quant("tq%d" % (t + 1), 0, 128, P("zt", 0, 512))
-        unpack(0, hq, 64, 4)
-        unpack(128, tl, 0, 0)
-    for k, (a, b) in enumerate(pieces):
-        new_state(ROUNDS - 1, a, b)
+        for b in range(4):
+            mm(b, 128, "c6", 128 * b, hq, 96)
+        for b in range(4):
+            (copy if b % 2 else act)(P("yt", b, 512, 4), ps(b, 0, 128))
+
+    def results(k, a, b):
         quant("xq2", a, b, P(state[ROUNDS], 4 * a, 4 * b))
         mm(4 + k, b - a, "vq", 0, "xq2", a)
         act(P("yo", a, b), ps(4 + k, 0, b - a))
         dma("y", T.oc[:, 4 * a:4 * b], U8("xq2c", a, b), "done", 0, [P("xq2c", a, b)], [])
-        dma("ys"[k], T.y[:, a:b], V(P("yo", a, b)), "done", 0, [P("yo", a, b)], [])
-    for k in range(4):
-        dma("y", T.osc[4 * k:4 * k + 4, 0:512], T.xq2s[32 * k:32 * k + 4, 0:512], "done", 0, [P("xq2s", 0, 512)], [])
+        if b == 512:
+            scales("y", 0)
+            scales("y", 1)
+        dma("s", T.y[:, a:b], V(P("yo", a, b)), "done", 0, [P("yo", a, b)], [])
+
+    def scales(q, k):
+        dma(q, T.osc[4 * k:4 * k + 4, 0:512], T.xq2s[32 * k:32 * k + 4, 0:512], "done", 0, [P("xq2s", 0, 512)], [])
+
+    if TAIL:
+        for k, (a, b) in enumerate(TAIL):
+            new_state(ROUNDS - 1, a, b)
+            results(k, a, b)
+    else:
+        by_pieces(ROUNDS - 1, results)
+    scales("s", 2)
+    scales("s", 3)
     for s in total:
         if waited.get(s, 0) < total[s]:
             g.wait_ge(T.sem[s], total[s])

@@ -10,11 +10,13 @@ NONE = -float(2 ** 84)
 LOW = -float(2 ** 85)
 MISS = -float(2 ** 90)
 ROUNDS = 2
-FOUR = 1
-AHEAD = (0, 2)
-SC1 = (0, 0)
-NEAR = 8
-TAIL = ((0, 256), (256, 384), (384, 512))
+ORDER = ("y0 q0 y1 u y2 q1 y3 q2 t0 e z m0 y4 y5 y6 p0 m1 t1 m2 y7 y8 y9 p1 c w0 h005 h016 h021 h030 h103 h117 "
+         "a00 a01 w1 x00 x01 a10 a11 x10 n0 x11 l0 v125 l1 R00 R01 R02 D00 D01 D02 n1 v136 R10 R11 R12 C0 P0 A1 A0 D11 D12 D10 "
+         "F0 P1 K0 H00 H10 w2 F1 K1 C1 H01 C2 w3 K2 T0 H11 B0 w4 E W0 d f00 T1 f01 f02 B1 f03 M0 f11 i W1 f10 M1 W2 f12 f13",
+         "s08 s8c q0 h005 h016 scg q1 h027 m0 q2 p0 t0 m1 t1 m2 h035 p1 h106 h115 h121 "
+         "a00 a01 x00 x01 a10 a11 x10 x11 n0 l0 v130 R00 R01 R02 D00 D01 D02 n1 A0 l1 C0 P0 R12 R10 D10 R11 A1 F0 D11 D12 P1 "
+         "K0 H00 H10 F1 C1 K1 C2 H01 H11 T0 K2 B0 E W0 d f00 T1 f01 B1 f02 f03 M0 M1 W1 f10 f11 W2 f12 f13")
+TAIL = "s08 s8c r0 r1 scg r2"
 HEAD = 64
 
 SCRATCH = {}
@@ -40,38 +42,42 @@ def _parts(name, dtype, *parts):
 
 for _k in range(8):
     SCRATCH["ps%d" % _k] = ("psum", [128, 512], "float32")
-for _n, _c in (("xa", 2056), ("xb", 2056), ("xc", 2048), ("ut", 512), ("vt", 512), ("wm", 1024), ("nd", 512), ("zb", 1040),
-               ("hw", 512), ("hb", 512), ("zt", 520), ("junk", 1408), ("yt", 528),
-               ("f1", 1032), ("f2", 520), ("f3", 520), ("f4", 520), ("f5", 520), ("f6", 520)):
+for _n, _c in (("xa", 2048), ("xb", 2048), ("xc", 2048), ("ut", 512), ("vt", 512), ("wm", 1024), ("nd", 512), ("zb", 1040),
+               ("zt", 520), ("junk", 1408), ("yt", 1040), ("ha", 2056),
+               ("f1", 1032), ("f2", 520), ("f3", 520), ("f4", 520), ("f5", 520), ("f6", 520), ("f7", 520)):
     _sb(_n, _c, "bfloat16")
-for _n, _c in (("sq", 512), ("acc", 16), ("dg", 32), ("yo", 512), ("wo", 512)):
+for _n, _c in (("sq", 512), ("acc", 16), ("e8", 144), ("yo", 512), ("wo", 512)):
     _sb(_n, _c, "float32")
 _parts("work", "float32", ("va", 512), ("vb", 512), ("sa", 520), ("sb", 520))
-_parts("fixed", "float32", ("m8", 8), ("k8", 8), ("d5", 128), ("lm", 32), ("d3", 16), ("wr", 48), ("wx", 32), ("im", 128), ("uf", 16),
-       ("gcol", 8), ("rs", 64), ("kk", 64), ("has", 64), ("part", 64), ("bcol", 8), ("p2", 8))
-_parts("lists", "float32", ("la", 128))
-_parts("choose", "float32", ("cm", 8), ("tr", 32), ("row", 32), ("bc", 64), ("mk", 64), ("fold", 64))
-_parts("whole", "int32", ("ip", 128), ("ip2", 128), ("il", 32), ("il2", 32), ("bi", 128), ("bj", 128), ("ib", 8))
-for _n, _c in (("ulist", 16), ("off", 16), ("offs", 128), ("offm", 4), ("offe", 8)):
+_parts("fixed", "float32", ("m32", 64), ("k32", 64), ("d5", 128), ("dd", 32), ("d3", 8), ("im", 128), ("uf", 16), ("ir", 8),
+       ("key", 8), ("gcol", 8), ("kk", 192), ("mc", 192), ("cols", 8))
+_parts("choose", "float32", ("cm", 8), ("tr", 64), ("row", 64), ("bc", 128), ("mk", 192), ("fold", 192))
+_parts("whole", "int32", ("ip", 128), ("ip2", 128), ("bi", 128), ("bj", 128), ("ib", 8), ("uu", 8), ("uv", 8), ("wi", 192),
+       ("wj", 192))
+_parts("lists", "int32", ("la", 128), ("lb", 128), ("lc", 128), ("ld", 128), ("le", 128))
+for _n, _c in (("ulist", 16), ("off", 16), ("offs", 128), ("offm", 4), ("offe", 4)):
     _sb(_n, _c, "uint16")
-for _n, _c in (("uq", 128), ("up", 256), ("vq", 128), ("wq", 512), ("c1", 512), ("c2", 256), ("c3", 128), ("c4", 512),
+for _n, _c in (("uq", 128), ("up", 256), ("vq", 128), ("wq", 512), ("c1", 512), ("c2", 256), ("c3", 256), ("c4", 512),
                ("c5", 128), ("c6", 512), ("pq", 256), ("nq", 128), ("zq", 256), ("xq2", 512)):
     _mx(_n, _c)
 for _t in range(ROUNDS):
-    for _n, _c in (("xq", 544), ("cq", 192), ("lq", 256), ("eq", 256), ("hq", 224)):
+    for _n, _c in (("xq", 512), ("aq", 544), ("cq", 192), ("lq", 256), ("mq", 64), ("eq", 128), ("hq", 320)):
         _mx("%s%d" % (_n, _t), _c)
     _parts("run%d" % _t, "float32", ("ra%d" % _t, HEAD + 520), ("rb%d" % _t, HEAD + 520))
-    for _n, _c in (("st", 16), ("rr", 4), ("se", 4)):
+    for _n, _c in (("st", 16), ("rr", 4), ("se", 16)):
         _sb("%s%d" % (_n, _t), _c, "float32")
 SEMAPHORES = ["nv", "ns", "nt", "ng", "lu", "lx0", "lx1", "lx2", "lw", "lv", "done", "left"] + [
-    "%s%d" % (a, t) for t in range(ROUNDS) for a in ("ac", "ad", "as", "bc", "bs", "gc")]
+    "%s%d" % (a, t) for t in range(ROUNDS) for a in ("ac", "ad", "as", "bc", "bs", "gc", "gn")]
 
 
 def rank_program(g, core, T, topo):
     rank = T.rank_of(core)
     if rank is None:
         return
-    o, block, partner = rank % 4, rank // 4, rank ^ 4
+    blocks = [[0, 1, 2, 3], [4, 5, 6, 7]]
+    owner = {r: b.index(r) for b in blocks for r in b}
+    o, block = owner[rank], int(rank in blocks[1])
+    partner = blocks[1 - block][o]
     queue = {"v": g.vector, "s": g.scalar, "t": g.tensor, "g": g, "y": g.sync}
     counter = {"v": "nv", "s": "ns", "t": "nt", "g": "ng"}
     span = [set()]
@@ -169,9 +175,7 @@ def rank_program(g, core, T, topo):
         do("s", lambda: g.scalar.activation(V(out), V(a), func, **{k: V(x) if isinstance(x, tuple) else x for k, x in more.items()}),
            [a] + [x for x in more.values() if isinstance(x, tuple)], [out])
 
-    def below(out, r, step, at):
-        n = HEAD + 512
-        src, end, junk = P(r, step - 1, n, step), P(r, n, n + 1), P("junk", at, at + n // step)
+    def below(out, src, end, junk):
         do("s", lambda: g.scalar.activation(V(junk), V(src), F.Sign, bias=V(end), scale=-1.0, accum_out=V(out)),
            [src, end], [junk, out])
 
@@ -203,41 +207,40 @@ def rank_program(g, core, T, topo):
     def bitmask(engines):
         return sum(1 << e for e in engines)
 
-    mates = [4 * block + d for d in range(4) if d != o]
+    mates = [r for r in blocks[block] if r != rank]
     far = [r for r in mates if topo.chip(T.cores[r]) != topo.chip(core)]
     near = [r for r in mates if r not in far]
+    assert [owner[r] for r in near] == [o ^ 1]
     outside = topo.engines(core, T.cores[far[0]])
-    share = len(outside) // len(far)
-    masks = {r: bitmask(outside[k * share:(k + 1) * share]) for k, r in enumerate(far)}
     inside = [e for e in topo.engines(core, T.cores[near[0]]) if e not in outside]
-    masks[near[0]] = bitmask(inside[:NEAR])
-    assert [r % 4 for r in near] == [o ^ 1]
-    masks[partner] = topo.mask(core, T.cores[partner])
-    from_mates = sum(bin(masks[r]).count("1") for r in mates)
-    from_partner = bin(masks[partner]).count("1")
-    halves = [masks[r] for r in far]
+    share = len(outside) // len(far)
+    assert all(topo.engines(core, T.cores[r]) == outside for r in far + blocks[1 - block])
+    from_mates = len(outside) + len(inside)
 
     def send(moves, reads):
         wait("g", conflicts("g", reads, []))
-        moves = [m if len(m) == 5 else m + (masks[m[0]],) for m in moves]
-        g.remote_dma_fused([RemoteDMATransfer(dst_ids=[address(r)], dma_engine_mask=e, remote_sem=T.sem[s], src=a, dst=b)
-                            for r, a, b, s, e in moves], local_sem=T.sem.left)
-        total["left"] = total.get("left", 0) + sum(bin(m[4]).count("1") for m in moves)
+        away = [m[0] for m in moves if m[0] not in near]
+        n = len(outside) // max(len(away), 1)
+        engines = {r: inside if r in near else outside[n * away.index(r):n * away.index(r) + n] for r, a, b, s in moves}
+        g.remote_dma_fused([RemoteDMATransfer(dst_ids=[address(r)], dma_engine_mask=bitmask(engines[r]), remote_sem=T.sem[s], src=a, dst=b)
+                            for r, a, b, s in moves], local_sem=T.sem.left)
+        total["left"] = total.get("left", 0) + sum(len(e) for e in engines.values())
 
     def land(s, n, places):
         total[s] = n
         note("remote", [], places, (s, n))
 
-    def U8(name, a, b):
-        return T[name][:, a:b].bitcast(dt.uint8)
+    def side(name, a, b):
+        return T[name][:, a:b].bitcast(dt.uint8) if name[-1] == "c" else T[name][:, a:b]
 
     pieces = ((0, 256), (256, 384), (384, 512))
     dma("s", T.ut[:], T.u[:], "lu", 16, [], [P("ut", 0, 512)])
     for k, (a, b) in enumerate(pieces):
         dma("y", T.xa[:, 4 * a:4 * b], T.x[:, 4 * a:4 * b], "lx%d" % k, 16, [], [P("xa", 4 * a, 4 * b)])
-    wait("y", {"lx%d" % k: 16 for k in range(3)})
-    dma("y", U8("wqc", 0, 512), T.wc[:], "lw", 32, [], [P("wqc", 0, 512)])
+    wait("y", {"lx0": 16})
+    dma("y", side("wqc", 0, 512), T.wc[:], "lw", 32, [], [P("wqc", 0, 512)])
     dma("y", T.wqs[:], T.ws[:], "lw", 32, [], [P("wqs", 0, 512)])
+    wait("y", {"lw": 32})
     dma("y", T.vt[:], T.v[:], "lv", 16, [], [P("vt", 0, 512)])
 
     def iota(p, pattern, base, ch, f=False):
@@ -250,26 +253,30 @@ def rank_program(g, core, T, topo):
         do("g", lambda: g.affine_select(V(out), V(src), pattern, op, value, base, ch), [src], [out])
 
     iota(P("ip", 0, 128), [[0, 8], [-1, 16]], 16, 1)
-    iota(P("im", 0, 128), [[128 - 256 * (1 - (o >> 1)), 2], [2, 64]], 128 * (1 - (o >> 1)), 0, True)
+    for e in range(2):
+        iota(P("im", 64 * e, 64 * e + 64), [[4369, 4], [256, 4], [16, 4]], 4096 * e, 0, True)
     iota(P("uf", 0, 16), [[16, 16]], 1, 0, True)
+    iota(P("uu", 0, 1), [[0, 1]], 0, 1)
     select(P("uf", 0, 16), P("uf", 0, 16), [[-1, 16]], A.is_ge, 15.0, 7, 0)
     fill(P("zt", 0, 520), 0.0)
     act(P("f1", 0, 516), P("zt", 0, 516))
     act(P("f1", 516, 1032), P("zt", 0, 516))
     act(P("f2", 0, 520), P("zt", 0, 520))
     for k in range(4):
-        fill(P("gcol", 0, 1, 1, 32 * k, 32 * k + 32), 2.0 ** (6 - 2 * k))
+        fill(P("gcol", 0, 1, 1, 32 * k, 32 * k + 32), 2.0 ** (12 - 4 * k))
     for k in range(4):
-        fill(P("gcol", 0, 1, 1, 32 * k, 32 * k + 16), 2.0 ** (7 - 2 * k))
+        fill(P("gcol", 0, 1, 1, 32 * k, 32 * k + 16), 2.0 ** (13 - 4 * k))
     ts(P("ip2", 0, 128), P("ip", 0, 128), 15, A.bitwise_and)
-    fill(P("xa", 2048, 2056), 0.0)
+    fill(P("ha", 2048, 2056), 0.0)
     ts(P("bi", 0, 128), P("im", 0, 128), P("gcol", 0, 1), A.mult)
     ts(P("d5", 0, 128), P("ip2", 0, 128), 0.0, A.is_equal)
     fill(P("wm", 2, 1024, 4), 0.0)
-    ts(P("bj", 0, 128), P("bi", 0, 128), 128, A.bitwise_and)
+    ts(P("bj", 0, 128), P("bi", 0, 128), 8192, A.bitwise_and)
+    ts(P("cols", 3, 4), P("gcol", 0, 1), 1.0, A.is_equal, 8192.0, A.mult)
     fill(P("wm", 3, 1024, 4), 0.0)
-    ts(P("f1", 3, 1027, 8), P("bj", 0, 128), P("d5", 0, 1), A.mult)
-    ts(P("f1", 7, 1031, 8), P("bj", 0, 128), 0.0, A.is_equal, P("d5", 0, 1), A.mult)
+    top = 512 * (o >> 1)
+    ts(P("f1", 515 - top, 1027 - top, 4), P("bj", 0, 128), P("d5", 0, 1), A.mult)
+    ts(P("f1", 3 + top, 515 + top, 4), P("bj", 0, 128), P("cols", 3, 4), A.not_equal, P("d5", 0, 1), A.mult)
     copy(P("ulist", 0, 16), P("uf", 0, 16))
     for e, w in ((0, 64.0), (1, 8.0), (2, 1.0), (3, 0.0)):
         act(P("f5", e, 512, 4), P("d5", 0, 128), scale=w)
@@ -279,347 +286,365 @@ def rank_program(g, core, T, topo):
     quant("uq", 0, 128, P("ut", 0, 512))
     quant("c1", 256, 512, P("f1", 2, 1026))
     pick("up", 0, 128, "uq", 128, "ulist", 0, 8)
-    iota(P("m8", 0, 8), [[0, 8]], 1, 0, True)
-    iota(P("il", 0, 32), [[4, 32]], 259, -1)
-    select(P("m8", 0, 8), P("m8", 0, 8), [[-64, 2], [16, 4]], A.is_ge, 0.0, -48, 1)
+    act(P("zb", 0, 520), P("zt", 0, 520))
+    iota(P("cols", 5, 6), [[0, 1]], 0, 1, True)
+    iota(P("uu", 1, 2), [[0, 1]], 0, 17)
+    iota(P("ir", 0, 8), [[4, 2], [-1, 4]], 3, 0, True)
+    for e in range(2):
+        iota(P("uu", 3, 5, 1, 64 * e, 64 * e + 64), [[64 * (o >> 1) - 32, 2]], 32 * (1 - (o >> 1)) + 80 * e, 1)
+        iota(P("cols", 4, 5, 1, 64 * e, 64 * e + 64), [[0, 1]], 4 * e, 0, True)
+    iota(P("dd", 0, 32), [[0, 32]], 0, 0, True)
     select(P("f2", 3, 515, 4), P("f2", 3, 515, 4), [[0, 8], [16, 16]], A.not_equal, 1.0, -32, -1)
-    select(P("m8", 0, 8), P("m8", 0, 8), [[64, 2], [-16, 4]], A.is_ge, 0.0, 63, -1)
+    iota(P("wi", 0, 192), [[-16, 3], [16, 4], [1, 16]], 240, 0)
     select(P("f2", 3, 515, 4), P("f2", 3, 515, 4), [[16, 8], [1000, 16]], A.not_equal, 1.0, 0, -1)
-    iota(Q("cm", 3, 4), [[0, 1]], 0, 1, True)
+
+    def weigh(at, row, w, pattern=((-16, 8),)):
+        select(P("dd", at, at + 8), P("dd", at, at + 8), [list(p) for p in pattern], A.not_equal, float(w), -row, 1)
+
+    for k in range(6):
+        weigh(0, 2 + k, (9, 18, -1, -2, -8, -16)[k])
+        if k < 5:
+            weigh(8, (2, 3, 8, 9, 0)[k], (64, 128, -64, -128, -1024)[k])
+        if k < 2:
+            weigh(16, 2 + k, 16 << k, ((-34, 4), (-16, 2)))
+    select(P("dd", 0, 24), P("dd", 0, 24), [[0, 3], [-17, 8]], A.not_equal, 0.0, -2, 1)
 
     def constants_early():
         for r in ("ra0", "rb0"):
             fill(P(r, 0, HEAD), LOW)
-        fill(Q("tr", 0, 32), 0.0)
-        ts(P("k8", 0, 8), P("m8", 0, 8), 1016.0, A.mult, -1024.0, A.add)
+        fill(Q("tr", 0, 64), 0.0)
 
     def constants_mid():
-        act(P("zb", 520, 1040), P("zt", 0, 520))
         quant("c5", 0, 128, P("f5", 0, 512))
 
-    def constants_wait():
-        for f in ("f6", "f3", "f4"):
-            act(P(f, 0, 520), P("zt", 0, 520))
-        act(Q("p2", 0, 1), Q("cm", 3, 4), scale=1.0 / 64)
-        fill(P("kk", 0, 64), 4096.0)
-        fill(P("rs", 0, 64), 1.0)
-        copy(P("bcol", 2, 3), P("ip2", 0, 1))
-        ts(P("il2", 0, 32), P("il", 0, 32), 12, A.bitwise_and)
-        for s in range(4):
-            fill(P("kk", 16 * s, 16 * s + 1), 0.75 - 0.25 * s)
-        quant("eq0", 64, 192, P("zt", 0, 512))
-        own = 64 + 32 * (o & 1)
-        ts(P("has", 0, 32), P("bj", own, own + 32), 0.0, A.not_equal)
-        ts(P("has", 32, 64), P("bj", own, own + 32), 0.0, A.is_equal)
-        ts(P("lm", 0, 32), P("il2", 0, 32), 0.0, A.is_equal)
+    def constants_places(k):
+        if k == 0:
+            ts(P("ib", 1, 2), P("uu", 0, 1), 124, A.bitwise_and)
+        elif k == 1:
+            ts(P("uu", 2, 3), P("ib", 1, 2), 4.0, A.mult, P("cols", 5, 6), A.add)
+        elif k == 2:
+            ts(P("uv", 0, 5), P("uu", 0, 5), 4, A.logical_shift_right, 3, A.bitwise_and)
+        elif k == 3:
+            ts(P("key", 0, 5), P("uv", 0, 5), P("cols", 4, 5), A.add)
+        elif k < 9:
+            c = k - 4
+            at = 8 * c if c < 4 else 56
+            ts(P("m32", at, at + 8), P("ir", 0, 8), P("key", c, c + 1), A.is_equal)
+        else:
+            act(P("m32", 32, 56), P("m32", 0, 24))
+            act(P("k32", 0, 32), P("m32", 0, 32), F.Identity, 1016.0, -1024.0)
+            act(P("k32", 32, 64), P("m32", 32, 64), F.Identity, 1016.0, -1024.0)
 
-    def constants_weights():
-        fill(P("wr", 0, 32), 0.0)
-        fill(P("wr", 32, 48), 2.0)
-        fill(P("rs", 0, 64, 8), 0.0)
+    def constants_choices(k):
+        if k == 0:
+            copy(P("cols", 2, 3), P("ip2", 0, 1))
+            fill(P("ib", 2, 3, 1, 0, 32), 0)
+            ts(P("ib", 2, 3, 1, 32, 64), P("ip2", 0, 1, 1, 32, 64), 3, A.bitwise_and)
+            ts(P("ib", 2, 3, 1, 64, 96), P("ip2", 0, 1, 1, 64, 96), 2, A.logical_shift_right)
+            fill(P("ib", 2, 3, 1, 96, 128), o)
+        elif k == 1:
+            ts(P("cols", 6, 7), P("ib", 2, 3), 16.0, A.mult, P("cols", 2, 3), A.subtract)
+        elif k == 2:
+            ts(P("wj", 0, 192), P("wi", 0, 192), P("cols", 6, 7), A.add)
+        elif k == 3:
+            ts(P("wi", 0, 192), P("wj", 0, 192), 63, A.bitwise_and)
+        else:
+            ts(P("mc", 0, 192), P("wi", 0, 192), 0.0, A.is_equal)
+
+    def constants_wait():
+        act(P("kk", 0, 192), P("zt", 0, 192), F.Identity, 1.0, 4096.0)
+        act(P("f6", 0, 520), P("zt", 0, 520))
+        act(P("kk", 0, 192, 64), P("ir", 1, 4), scale=0.25)
+        for f in ("f3", "f7"):
+            act(P(f, 0, 520), P("zt", 0, 520))
         ts(P("ib", 0, 1), P("ip", 0, 1), 3, A.bitwise_and)
-        scan(P("wr", 18, 26), P("wr", 32, 40), P("wr", 0, 8), 0.5, A.mult, A.add)
-        for s in range(2):
-            tt(P("part", s, 64, 2), P("has", 32 * s, 32 * s + 32), P("lm", 0, 32), A.mult)
-        copy(P("bcol", 0, 1), P("ib", 0, 1))
-        ts(P("wr", 3, 8), P("wr", 19, 24), -1.0, A.mult)
-        for at, w in ((0, -1024.0), (2, 256.0), (8, 64.0 if o & 1 else -64.0), (9, 128.0 if o & 2 else -128.0)):
-            fill(P("wr", at, at + 1), w)
+        tt(P("d3", 0, 8), P("dd", 8, 16), P("dd", 16, 24), A.add)
+        quant("hq0", 0, 128, P("zt", 0, 512))
+        copy(P("cols", 1, 2), P("ib", 0, 1))
 
     def constants_hop():
-        fill(P("hb", 0, 384), 0.0)
-        tt(P("wx", 0, 32), P("wr", 0, 32), P("d5", 0, 32), A.mult)
-        ts(P("bcol", 1, 2), P("ib", 0, 1), -2.0, A.add)
-        fill(P("yt", 512, 528), 0.0)
-        fill(P("xb", 2048, 2056), 0.0)
-        for k in range(2):
-            src, out = P("wx", 16 * k, 16 * k + 16), P("bcol", 4 + k, 5 + k)
-            do("v", lambda: g.vector.tensor_reduce(V(out), V(src), AxisListType.X, A.add), [src], [out])
-        for r in ("ra1", "rb1"):
-            fill(P(r, 0, HEAD), LOW)
-        for k in range(2):
-            ts(P("d3", 8 * k, 8 * k + 8), P("wr", 32, 40), P("bcol", 4 + k, 5 + k), A.mult, 0.5, A.mult)
-
-    def constants_blocks():
-        select(P("d3", 0, 16), P("d3", 0, 16), [[0, 2], [-16, 8]], A.is_ge, 0.0, 0, 1)
-        select(P("f6", 3, 515, 4), P("f6", 3, 515, 4), [[-1, 128]], A.not_equal, 1.0, 0, 1)
-        select(P("d3", 0, 16), P("d3", 0, 16), [[0, 2], [16, 8]], A.is_ge, 0.0, 15, -1)
-        select(P("d3", 0, 16), P("d3", 0, 16), [[0, 2], [-17, 8]], A.not_equal, 0.0, -2, 1)
-
-    def constants_lists():
         for r in range(16):
-            act(P("f3", 4 * r + r // 4, 512, 64), P("d3", 0, 8))
+            act(P("f3", 4 * r + r // 4, 512, 64), P("dd", 0, 8), scale=4.0)
+            act(P("f7", 4 * r + r // 4, 512, 64), P("d3", 0, 8), scale=4.0)
         for e in range(2):
             quant("c2", 128 * e, 128 * e + 128, P("f2", 3 - e, 515 - e))
-        for b in range(4):
-            quant("c6", 128 * b, 128 * b + 128, P("f6", 3 - b, 515 - b))
+
+    def constants_last():
+        quant("c3", 0, 128, P("f3", 0, 512))
+        quant("c3", 128, 256, P("f7", 0, 512))
+        act(P("yt", 0, 520), P("zt", 0, 520))
+        act(P("yt", 520, 1040), P("zt", 0, 520))
+        act(P("f4", 0, 520), P("zt", 0, 520))
+        for k in range(8):
+            weigh(24, 2 + k, 1 << k)
+        weigh(24, 2, 0, ((-17, 8),))
 
     state = ["xa", "xb", "xc"]
+    end = HEAD + 512
+    mine, theirs = 64 * o, 1 - block
+    slot = {r: 64 * (owner[r] & 1) for r in far}
+    slot[near[0]] = 128
 
     def new_state(t, a, b):
-        i, y, x, z = P("offs", a // 4, b // 4), P("yt", 0, 528), P(state[t], 4 * a, 4 * b), P(state[t + 1], 4 * a, 4 * b)
+        i, y, x, z = P("offs", a // 4, b // 4), P("yt", 0, 1040), P(state[t], 4 * a, 4 * b), P(state[t + 1], 4 * a, 4 * b)
         do("v", lambda: g.vector.tensor_tensor(V(z), V(y).indirect(V(i)), V(x), A.add), [y, i, x], [z])
 
-    def by_pieces(t, then):
-        for k in range(-1, len(pieces)):
-            if t >= 0 and k + 1 < len(pieces):
-                new_state(t, *pieces[k + 1])
-            if k >= 0:
-                then(k, *pieces[k])
+    def count(h, k):
+        return P("acc", 8 * h + k, 8 * h + k + 1)
+
+    def digit(h, k):
+        return P("zb", 520 * h + k, 520 * h + 128, 4)
+
+    def marks(k):
+        a, b = pieces[k]
+        at = 512 * (a // 256) + 2 * (a % 256)
+        for e in range(2):
+            tt(P("wm", at + e, at + 2 * (b - a), 4), P("ps%d" % (0, 4, 6)[k], e, b - a, 2), P("sq", a + e, b, 2), A.is_le)
+
+    def missing(j):
+        quant("pq", 128 * j, 128 * j + 128, P("wm", 512 * j, 512 * j + 512))
+        for h in range(2):
+            for e in range(2):
+                bank = (1, 0, 3, 7)[2 * h + e]
+                mm(bank, 128, "c1", 256 * e + 128 * h, "pq", 128 * j)
+                act(P(("va", "vb")[h], 256 * j + e, 256 * j + 256, 2), ps(bank, 0, 128), scale=MISS)
+
+    def product(h):
+        quant("zq", 128 * h, 128 * h + 128, P("zb", 520 * h, 520 * h + 512))
+        mm(6 + h, 128, "c5", 0, "zq", 128 * h)
+
+    def places(h):
+        for a in range(4):
+            ts(P("off", 8 * h, 8 * h + 8, 1, 32 * a, 32 * a + 32), P("ps%d" % (6 + h), 8 * a, 8 * a + 8, 1, 32 * a, 32 * a + 32),
+               -float(HEAD), A.add)
+
+    def turn(n):
+        src, out = Q("tr", 32 * n, 32 * n + 32), Q("row", 32 * n, 32 * n + 32)
+        do("v", lambda: g.vector.transpose(V(out), V(src)), [src], [out])
+
+    def spread(n):
+        for k in range(2):
+            first = 64 * (o & 1) + 32 * k
+            src, out = P("row", 32 * n, 32 * n + 32, 1, first, first + 1), P("bc", 64 * n + 32 * k, 64 * n + 32 * k + 32)
+            do("g", lambda: g.partition_broadcast(V(out), V(src), 128), [src], [out], k == 1)
+
+    def fold(n, k):
+        if k < 2:
+            for c in range(3):
+                at, row = 64 * (2 - c if n else c) + 32 * k, 64 * n + 32 * k
+                tt(P("mk", at, at + 32), P("bc", row, row + 32), P("mc", 64 * c + 32 * k, 64 * c + 32 * k + 32), A.mult)
+        elif k == 2:
+            scan(P("fold", 0, 192), P("kk", 0, 192), P("mk", 0, 192), 4096.0, A.min, A.add)
+        else:
+            ts(P(("offm", "offe")[n], 0, 3), P("fold", 63, 192, 64), 64.0, A.mult, P("cols", 2, 3), A.add)
+
+    def offsets(k):
+        if k == 0:
+            quant("nq", 0, 128, P("nd", 0, 512))
+            for j in range(2):
+                mm(6 + j, 128, "c3", 128 * j, "nq", 0)
+        elif k == 1:
+            ts(P("la", 0, 128), ps(6, 0, 128), 4.0 * 36, A.add)
+            ts(P("lb", 0, 128), ps(7, 0, 128), 4.0 * 1280, A.add)
+        elif k == 2:
+            ts(P("lc", 0, 128), P("la", 0, 128), 12, A.bitwise_and)
+            ts(P("ld", 0, 128), P("la", 0, 128), 1, A.logical_shift_right, 48, A.bitwise_and)
+            ts(P("le", 0, 128), P("lb", 0, 128), 4 * (1024 + 240), A.bitwise_and)
+            tt(P("la", 0, 128), P("lc", 0, 128), P("ld", 0, 128), A.add)
+        elif k == 3:
+            tt(P("lb", 0, 128), P("la", 0, 128), P("le", 0, 128), A.add)
+        else:
+            ts(P("offs", 0, 128), P("lb", 0, 128), P("cols", 1, 2), A.add, 1024.0, A.min)
+
+    def wishes():
+        for j in range(2):
+            for e in range(2):
+                mm(2 * j + e, 128, "c2", 128 * e, "pq", 128 * j)
+        for j in range(2):
+            for e in range(2):
+                tt(P("nd", 256 * j + e, 256 * j + 256, 2), ps(2 * j + e, 0, 128), P("wm", 512 * j + e, 512 * j + 512, 4), A.max)
 
     for t in range(ROUNDS):
-        N = lambda s: "%s%d" % (s, t)
-        X, xq = state[t], N("xq")
-        last = t == ROUNDS - 1
+        X, last = state[t], t == ROUNDS - 1
+        xq, aq, cq, lq, mq, eq, hq, st, rr, se, ra, rb = [
+            "%s%d" % (s, t) for s in ("xq", "aq", "cq", "lq", "mq", "eq", "hq", "st", "rr", "se", "ra", "rb")]
+        sem = {s: "%s%d" % (s, t) for s in ("ac", "ad", "as", "bc", "bs", "gc", "gn")}
 
-        def scores(k, a, b):
-            more = 2 if b == 512 else 0
-            quant(xq, a, b + more, P(X, 4 * a, 4 * (b + more)))
+        def scores(k):
+            a, b = pieces[k]
+            quant(xq, a, b, P(X, 4 * a, 4 * b))
             mm((1, 3, 5)[k], b - a, "up", 0, xq, a)
             mm((0, 4, 6)[k], b - a, "uq", 0, xq, a)
             act(P("sq", a, b), ps((1, 3, 5)[k], 0, b - a))
 
-        def marks(k):
-            a, b = pieces[k]
-            at = 512 * (a // 256) + 2 * (a % 256)
-            for e in range(2):
-                tt(P("wm", at + e, at + 2 * (b - a), 4), P("ps%d" % (0, 4, 6)[k], e, b - a, 2), P("sq", a + e, b, 2), A.is_le)
+        def strengths(j):
+            mm(2 + 2 * j, 256, "up", 128, xq, 256 * j)
 
-        def missing(j):
-            quant("pq", 128 * j, 128 * j + 128, P("wm", 512 * j, 512 * j + 512))
-            for h in range(2):
-                for e in range(2):
-                    bank = ((7, 1, 0, 3), (5, 4, 6, 7))[j][2 * h + e]
-                    mm(bank, 128, "c1", 256 * e + 128 * h, "pq", 128 * j)
-                    act(P(("va", "vb")[h], 256 * j + e, 256 * j + 256, 2), ps(bank, 0, 128), scale=MISS)
+        def layer(j, b, bank, vector=False):
+            mm(bank, 256, "wq", 128 * b, xq, 256 * j)
+            out = P("ha", 1024 * j + b, 1024 * j + 1024, 4)
+            if vector:
+                ts(out, ps(bank, 0, 256), 0.03125, A.mult)
+            else:
+                act(out, ps(bank, 0, 256), scale=0.03125)
 
-        def maxima(j):
+        def masked(j, h):
             a, b = 256 * j, 256 * j + 256
-            for h in range(2):
-                tt(P(("sa", "sb")[h], a, b), ps(2, a, b), P(("va", "vb")[h], a, b), A.add)
-            for h in range(2):
-                sa, run = P(("sa", "sb")[h], a, b + j), N(("ra", "rb")[h])
-                scan(P(run, HEAD + a, HEAD + b + j), sa, sa, P(run, HEAD + a - 1, HEAD + a), A.max, A.max)
-                if j:
-                    strongest(h, run)
+            tt(P(("sa", "sb")[h], a, b), ps(2 + 2 * j, 0, 256), P(("va", "vb")[h], a, b), A.add)
+
+        def maxima(j, h):
+            a, b = 256 * j, 256 * j + 256
+            sa, run = P(("sa", "sb")[h], a, b + j), (ra, rb)[h]
+            scan(P(run, HEAD + a, HEAD + b + j), sa, sa, P(run, HEAD + a - 1, HEAD + a), A.max, A.max)
+            if j:
+                strongest(h, run)
 
         def strongest(h, run):
-            send([(r, V(P(run, end, end + 1)), T[st][:, 4 * o:4 * o + 1], N("as")) for r in (far, near)[h]], [P(run, end, end + 1)])
-            for k, step in enumerate((64, 8, 1)):
-                if h and k == 2:
-                    act(digit(0, 2), P("k8", 0, 8), F.Relu, count(0, 1), count(0, 2))
-                below(count(h, k), run, step, 704 * h + (0, 16, 128)[k])
-
-        st, cq, lq, rr, se = N("st"), N("cq"), N("lq"), N("rr"), N("se")
-        end = HEAD + 512
-        count = lambda h, k: P("acc", 8 * h + k, 8 * h + k + 1)
-        digit = lambda h, k: P("zb", 520 * h + k, 520 * h + 32, 4)
-        if t:
-            new_state(t - 1, *pieces[0])
-            new_state(t - 1, *pieces[1])
-        scores(0, *pieces[0])
-        if t:
-            new_state(t - 1, *pieces[2])
-        else:
-            pick("up", 128, 256, "uq", 128, "ulist", 8, 16)
-        scores(1, *pieces[1])
-        if t:
-            marks(0)
-        scores(2, *pieces[2])
-        if t == 0:
-            constants_early()
-            marks(0)
-            fill(P("zb", 0, 520), 0.0)
-        missing(0)
-        mm(2, 512, "up", 128, xq, 0)
-        marks(1)
-        marks(2)
-        missing(1)
-        if t == 0:
-            constants_mid()
-        maxima(0)
-        maxima(1)
-        act(digit(1, 2), P("k8", 0, 8), F.Relu, count(1, 1), count(1, 2))
-        land(N("as"), from_mates, [P(st, 4 * (r % 4), 4 * (r % 4) + 1) for r in mates])
-        slot = {r: 64 * (r & 1) for r in far}
-        slot[near[0]] = 128
-        mine = 64 * o
-
-        def codes(to):
-            send([(r, U8(cq + "c", slot[r], slot[r] + 64), U8(lq + "c", mine, mine + 64), N("ac")) for r in to],
-                 [P(cq + "c", slot[r], slot[r] + 64) for r in to])
-
-        def product(h):
-            quant("zq", 128 * h, 128 * h + 128, P("zb", 520 * h, 520 * h + 512))
-            mm(6 + h, 128, "c5", 0, "zq", 128 * h)
-
-        def places(h):
-            ts(P("off", 8 * h, 8 * h + 8), ps(6 + h, 0, 8), -float(HEAD), A.add)
-
-        def planes(to):
-            send([(r, T[cq + "s"][:, slot[r]:slot[r] + 64], T[lq + "s"][:, mine:mine + 64], N("ad")) for r in to],
-                 [P(cq + "s", slot[r], slot[r] + 64) for r in to])
-
-        def spread():
-            do("v", lambda: g.vector.transpose(V(Q("row", 0, 32)), V(Q("tr", 0, 32))), [Q("tr", 0, 32)], [Q("row", 0, 32)])
-
-        def broadcast(k):
-            first = 64 * (o & 1) + 32 * k
-            src, out = P("row", 0, 32, 1, first, first + 1), P("bc", 32 * k, 32 * k + 32)
-            do("g", lambda: g.partition_broadcast(V(out), V(src), 128), [src], [out], k == 1)
-
-        for h in range(2):
+            top = P(run, end, end + 1)
+            beyond = [[(r, V(P((ra, rb)[k], end, end + 1)), T[se][:, 4 * o:4 * o + 1], sem["bs"]) for r in blocks[theirs]
+                       if (owner[r] >> 1 == o >> 1) == (k == 1)] for k in range(2)]
+            send([(r, V(top), T[st][:, 4 * o:4 * o + 1], sem["as"]) for r in (far, near)[h]] + beyond[1] * h, [top])
             if h:
-                copy(P(st, 4 * o, 4 * o + 1), P(N("rb"), end, end + 1))
-            ts(P("dg", 8 * h, 8 * h + 8), P("k8", 0, 8), count(h, 0), A.mult, count(h, 1), A.add)
-            ts(digit(h, 0), P("m8", 0, 8), count(h, 0), A.mult)
-            if h:
-                product(0)
-            ts(digit(h, 1), P("dg", 8 * h, 8 * h + 8), 0.0, A.max)
-        places(0)
-        product(1)
-        pick(cq, 0, 128, xq, 514, "off", 0, 8)
-        codes(far)
-        if FOUR:
-            planes(far)
-        def compare():
-            scan(P(rr, 0, 4), P(st, 0, 16, 4), P(st, 0, 16, 4), LOW, A.max, A.max)
-            src, top, junk, out = Q(rr, 0, 3), Q(rr, 3, 4), Q("cm", 0, 3), Q("tr", 0, 1)
-            do("s", lambda: g.scalar.activation(V(junk), V(src), F.Sign, bias=V(top), scale=-1.0, accum_out=V(out)),
-               [src, top], [junk, out])
+                send(beyond[0], [P(ra, end, end + 1)])
+                land(sem["as"], from_mates, [P(st, 4 * owner[r], 4 * owner[r] + 1) for r in mates])
+                land(sem["bs"], 4 * share, [P(se, 0, 16, 4)])
 
-        if AHEAD[t] == 2:
-            compare()
-        places(1)
-        if AHEAD[t] == 1:
-            compare()
-        there = 8 + 4 * (near[0] & 1)
-        pick(cq, 128, 192, xq, 514, "off", there, there + 4)
-        if AHEAD[t] == 0:
-            compare()
-        spread()
-        if FOUR:
-            codes(near)
-            planes(near)
-        else:
-            planes(mates)
-            codes(near)
-        pick(lq, mine, mine + 64, xq, 514, "off", 8 + 4 * (o & 1), 12 + 4 * (o & 1))
-        for k, s in (("c", "ac"), ("s", "ad")):
-            land(N(s), from_mates, [P(lq + k, 64 * (r % 4), 64 * (r % 4 + 1)) for r in mates])
+        def every(h):
+            run = (ra, rb)[h]
+            below(count(h, 3), P(run, HEAD - 8, end), P(run, end, end + 1), P("junk", 520 * h, 520 * h + 520))
 
-        def fold(mask):
-            for k in range(2):
-                tt(P("mk", 32 * k, 32 * k + 32), P("bc", 32 * k, 32 * k + 32), P(mask, 32 * k, 32 * k + 32), A.mult)
+        def eighth(h):
+            run = (ra, rb)[h]
+            ts(P("e8", 72 * h, 72 * h + 72), P(run, 7, end, 8), P(run, end, end + 1), A.is_lt)
 
-        def wishes():
-            for j in range(2):
-                for e in range(2):
-                    mm(2 * j + e, 128, "c2", 128 * e, "pq", 128 * j)
-            for j in range(2):
-                for e in range(2):
-                    tt(P("nd", 256 * j + e, 256 * j + 256, 2), ps(2 * j + e, 0, 128), P("wm", 512 * j + e, 512 * j + 512, 4), A.max)
+        def sums(h, k):
+            src, out = P("e8", 72 * h + (7, 0, 7)[k], 72 * h + 72, (8, 1, 1)[k]), count(h, k)
+            do("v", lambda: g.vector.tensor_reduce(V(out), V(src), AxisListType.X, A.add), [src], [out])
 
-        broadcast(0)
-        broadcast(1)
-        send([(partner, T[rr][:, 3:4], T[se][:, 3:4], N("bs"))], [P(rr, 3, 4)])
+        def digits(h, k):
+            if k == 0:
+                act(digit(h, 0), P("m32", 32 * h, 32 * h + 32), scale=count(h, 0))
+            else:
+                act(digit(h, k), P("k32", 32 * h, 32 * h + 32), F.Relu, count(h, 2 * k - 2), count(h, 2 * k - 1))
+
+        def candidates(k):
+            if k == 0:
+                pick(cq, 0, 128, aq, 514, "off", 0, 8)
+            elif k == 1:
+                pick(cq, 128, 176, aq, 514, "off", 12 - 4 * (o & 1), 15 - 4 * (o & 1))
+            else:
+                pick(lq, mine, mine + 48, aq, 514, "off", 8 + 4 * (o & 1), 11 + 4 * (o & 1))
+
+        def hop1(k, to):
+            k, to = "cs"[k], (far, near)[to]
+            send([(r, side(cq + k, slot[r], slot[r] + 48), side(lq + k, mine, mine + 48), sem["ac" if k == "c" else "ad"]) for r in to],
+                 [P(cq + k, slot[r], slot[r] + 48) for r in to])
+
+        def compare(k):
+            if k == 0:
+                copy(P(st, 4 * o, 4 * o + 1), P(rb, end, end + 1))
+            elif k == 1:
+                scan(P(rr, 0, 4), P(st, 0, 16, 4), P(st, 0, 16, 4), LOW, A.max, A.max)
+            else:
+                below(Q("tr", 0, 1), Q(rr, 0, 3), Q(rr, 3, 4), Q("cm", 0, 3))
+
+        def swap():
+            scan(Q("cm", 4, 8), Q(se, 0, 16, 4), Q(se, 0, 16, 4), LOW, A.max, A.max)
+
+        def meanwhile(k):
+            if t == 0:
+                (constants_wait, constants_hop, wishes)[k]()
+            elif k == 0:
+                wishes()
+            elif k == 1:
+                offsets(0)
+                act(P("f4", 3, 35, 4), P("dd", 24, 32))
+            else:
+                for b in range(2):
+                    quant("c4", 128 * b, 128 * b + 128, P("f4", 3 - b, 515 - b))
+
+        def stronger():
+            pair = (Q(rr, 3, 4), Q("cm", 7, 8))
+            ts(Q("tr", 32, 33), pair[theirs], pair[block], A.is_gt)
+
+        def hop2(k):
+            if k == 0:
+                for c, s in (("c", "ac"), ("s", "ad")):
+                    land(sem[s], from_mates, [P(lq + c, 64 * owner[r], 64 * owner[r] + 64) for r in mates])
+                pick(mq, 0, 48, lq, 256, "offm", 0, 3)
+                for c in "cs":
+                    send([(partner, side(mq + c, 0, 48), side(eq + c, 64 * block, 64 * block + 48), sem["bc"])], [P(mq + c, 0, 48)])
+                land(sem["bc"], 2 * len(outside), [P(eq + c, 64 * theirs, 64 * theirs + 48) for c in "cs"])
+            else:
+                pick(eq, 64 * block, 64 * block + 48, lq, 256, "offm", 0, 3)
+
+        steps = {"s": lambda a, b: new_state(t - 1, 32 * a, 32 * b), "q": scores, "m": marks, "p": missing, "t": strengths,
+                 "h": layer, "v": lambda j, b, bank: layer(j, b, bank, True), "a": masked, "x": maxima,
+                 "u": lambda: pick("up", 128, 256, "uq", 128, "ulist", 8, 16), "z": lambda: act(P("zb", 520, 1040), P("zt", 0, 520)),
+                 "e": constants_early, "c": constants_mid, "y": constants_places, "w": constants_choices,
+                 "n": every, "l": eighth, "R": sums, "D": digits, "P": product, "F": places, "K": candidates, "H": hop1,
+                 "A": lambda j: quant(aq, 256 * j, 256 + 258 * j, P("ha", 1024 * j, 1024 + 1032 * j)),
+                 "C": compare, "T": turn, "B": spread, "E": swap, "W": meanwhile, "f": fold, "d": stronger, "M": hop2,
+                 "i": lambda: select(P("f6", 3, 515, 4), P("f6", 3, 515, 4), [[-1, 128]], A.not_equal, 1.0, 0, 1)}
+        for step in ORDER[min(t, 1)].split():
+            steps[step[0]](*[int(c, 17) for c in step[1:]])
+        pick(hq, 128, 176, eq, 128, "offe", 0, 3)
+        spot = {r: 128 + 48 * (o ^ owner[r]) for r in mates}
+        for k in "cs":
+            send([(r, side(hq + k, 128, 176), side(hq + k, spot[r], spot[r] + 48), sem["gn" if r in near else "gc"]) for r in mates],
+                 [P(hq + k, 128, 176)])
+        land(sem["gn"], 2 * len(inside), [P(hq + k, 176, 224) for k in "cs"])
+        land(sem["gc"], 2 * len(outside), [P(hq + k, 224, 320) for k in "cs"])
         if t == 0:
-            constants_wait()
-        else:
-            wishes()
-        fold("d5")
-        scan(P("fold", 0, 64), P("kk", 0, 64), P("mk", 0, 64), 4096.0, A.min, A.add)
-        ts(P("offm", 0, 4), P("fold", 15, 64, 16), 64.0, A.mult, P("bcol", 2, 3), A.add)
-        eq = N("eq")
-        pick(eq, 0, 64, lq, 256, "offm", 0, 4)
-        theirs = 1 - block
-        for k in "sc" if SC1[t] else "cs":
-            side = U8 if k == "c" else lambda name, a, b: T[name][:, a:b]
-            send([(partner, side(eq + k, 0, 64), side(eq + k, 192, 256), N("bc"))], [P(eq + k, 0, 64)])
-        land(N("bc"), 2 * from_partner, [P(eq + k, 192, 256) for k in "cs"])
-        land(N("bs"), from_partner, [P(se, 3, 4)])
-        if t == 0:
-            constants_weights()
-
-        def layer(whose, first, bank):
+            constants_last()
+            offsets(0)
             for b in range(4):
-                mm(bank + b, 128, "wq", 128 * b, eq, 2 * first)
-            for b in range(4):
-                out, src = P("hw", 256 * whose + b, 256 * whose + 256, 4), ps(bank + b, first, first + 64)
-                if b % 2 and first:
-                    ts(out, src, 0.03125, A.mult)
-                else:
-                    act(out, src, scale=0.03125)
-
-        layer(block, 0, 0)
-        pair = [Q(rr, 3, 4), Q(se, 3, 4)]
-        ts(Q("tr", 0, 1), pair[theirs], pair[block], A.is_gt, Q("p2", 0, 1), A.add)
-        spread()
-        broadcast(0)
-        broadcast(1)
-        if t == 0:
-            constants_hop()
-            constants_blocks()
-        else:
-            quant("nq", 0, 128, P("nd", 0, 512))
-        fold("part")
-        scan(P("fold", 0, 64), P("rs", 0, 64), P("mk", 0, 64), 0.0, A.mult, A.add)
-        ts(P("offe", 0, 8), P("fold", 7, 64, 8), 256.0, A.mult, P("bcol", 0, 1), A.add)
-        hq = N("hq")
-        layer(theirs, 64, 4)
-        win, lst, out = P("hw", 0, 512), P("offe", 0, 8), P("hb", 384, 512)
-        do("v", lambda: g.vector.tensor_copy(V(out), V(win).indirect(V(lst))), [win, lst], [out])
-        quant(hq, 0, 128, P("hb", 0, 512))
-        spot = {r: 96 + 32 * (o ^ r % 4) for r in mates}
-        send([(r, U8(hq + "c", 96, 128), U8(hq + "c", spot[r], spot[r] + 32), N("gc")) for r in mates], [P(hq + "c", 96, 128)])
-        send([(r, T[hq + "s"][:, 96:128], T[hq + "s"][:, spot[r]:spot[r] + 32], N("gc")) for r in mates], [P(hq + "s", 96, 128)])
-        land(N("gc"), 2 * from_mates, [P(hq + k, 128, 224) for k in "cs"])
-        if t == 0:
-            constants_lists()
-            wishes()
-            quant("c3", 0, 128, P("f3", 0, 512))
-            quant("nq", 0, 128, P("nd", 0, 512))
-        mm(7, 128, "c3", 0, "nq", 0)
-        if t == 0:
-            quant("eq1", 64, 192, P("zt", 0, 512))
-        act(P("la", 0, 128), ps(7, 0, 128), F.Abs, 2.0, 2.0 * (1023 - 64 * o))
-        ts(P("offs", 0, 128), P("la", 0, 128), P("bcol", 1, 2), A.add, 512.0, A.min)
+                quant("c6", 128 * b, 128 * b + 128, P("f6", 3 - b, 515 - b))
+        fillers = [lambda b=b: quant("c4", 128 * b, 128 * b + 128, P("f4", 3 - b, 515 - b)) for b in range(2, 4)] if last else [
+            lambda: quant("hq1", 0, 128, P("zt", 0, 512)), lambda: quant("vq", 0, 128, P("vt", 0, 512))]
+        offsets(1)
+        fillers[0]()
+        offsets(2)
+        fillers[1]()
+        offsets(3)
         if last:
-            act(P("f4", 3, 35, 4), P("d3", 8, 16))
             for b in range(4):
-                quant("c4", 128 * b, 128 * b + 128, P("f4", 3 - b, 515 - b))
                 mm(4 + b, 128, "c4", 128 * b, "nq", 0)
+        else:
+            for r in ("ra1", "rb1"):
+                fill(P(r, 0, HEAD), LOW)
+        offsets(4)
+        if last:
             for b in range(4):
                 ts(P("wo", b, 512, 4, 0, 8), ps(4 + b, 0, 128, 8), -1.0, A.mult, 255.0, A.add)
             dma("y", T.wl[:, 0:512], T.wo[0:8, 0:512], "done", 0, [P("wo", 0, 512)], [])
-        else:
-            quant("vq", 0, 128, P("vt", 0, 512))
-        for b in range(4):
-            mm(b, 128, "c6", 128 * b, hq, 96)
-        for b in range(4):
-            (copy if b % 2 else act)(P("yt", b, 512, 4), ps(b, 0, 128))
-
-    def results(k, a, b):
-        quant("xq2", a, b, P(state[ROUNDS], 4 * a, 4 * b))
-        mm(4 + k, b - a, "vq", 0, "xq2", a)
-        act(P("yo", a, b), ps(4 + k, 0, b - a))
-        dma("y", T.oc[:, 4 * a:4 * b], U8("xq2c", a, b), "done", 0, [P("xq2c", a, b)], [])
-        if b == 512:
-            scales("y", 0)
-            scales("y", 1)
-        dma("s", T.y[:, a:b], V(P("yo", a, b)), "done", 0, [P("yo", a, b)], [])
+        for j in range(2):
+            for b in range(4):
+                mm(4 * j + b, 128, "c6", 128 * b, hq, 96 + 96 * j)
+            for b in range(4):
+                for k in range(2):
+                    at = 256 * (o ^ (2 * j + k)) + b
+                    (copy if j and b % 2 else act)(P("yt", at, at + 192, 4), ps(4 * j + b, 32 + 48 * k, 80 + 48 * k))
 
     def scales(q, k):
         dma(q, T.osc[4 * k:4 * k + 4, 0:512], T.xq2s[32 * k:32 * k + 4, 0:512], "done", 0, [P("xq2s", 0, 512)], [])
 
-    if TAIL:
-        for k, (a, b) in enumerate(TAIL):
-            new_state(ROUNDS - 1, a, b)
-            results(k, a, b)
-    else:
-        by_pieces(ROUNDS - 1, results)
-    scales("s", 2)
-    scales("s", 3)
+    def results(k):
+        a, b = pieces[k]
+        quant("xq2", a, b, P(state[ROUNDS], 4 * a, 4 * b))
+        mm(k, b - a, "vq", 0, "xq2", a)
+        act(P("yo", a, b), ps(k, 0, b - a))
+        dma("y", T.oc[:, 4 * a:4 * b], side("xq2c", a, b), "done", 0, [P("xq2c", a, b)], [])
+        if b == 512:
+            for j in range(4):
+                scales("y", j)
+        dma("s", T.y[:, a:b], V(P("yo", a, b)), "done", 0, [P("yo", a, b)], [])
+
+    for step in TAIL.split():
+        if step[0] == "s":
+            new_state(ROUNDS - 1, 32 * int(step[1], 17), 32 * int(step[2], 17))
+        else:
+            results(int(step[1]))
     for s in total:
         if waited.get(s, 0) < total[s]:
             g.wait_ge(T.sem[s], total[s])

@@ -1,23 +1,27 @@
 import math
 from concourse.bass import DstId, RemoteDMATransfer
-from concourse.mybir import dt, AluOpType, ActivationFunctionType, AxisListType
+from concourse.mybir import dt, AluOpType, ActivationFunctionType
+from concourse.mybir import AxisListType
 import comms_topo
 
 A = AluOpType
 F = ActivationFunctionType
 CODE = "float8_e4m3fn_x4"
-NONE = -float(2 ** 84)
-LOW = -float(2 ** 85)
-MISS = -float(2 ** 90)
+SMALL = 2.0 ** -42
+MISS = -2.0 ** 30
+NONE = -2.0 ** 29
+LOW = -2.0 ** 40
 ROUNDS = 2
-ORDER = ("y0 q0 y1 u y2 q1 y3 q2 t0 e z m0 y4 y5 y6 p0 m1 t1 m2 y7 y8 y9 p1 c w0 h005 h016 h021 h030 h103 h117 "
-         "a00 a01 w1 x00 x01 a10 a11 x10 n0 x11 l0 v125 l1 R00 R01 R02 D00 D01 D02 n1 v136 R10 R11 R12 C0 P0 A1 A0 D11 D12 D10 "
-         "F0 P1 K0 H00 H10 w2 F1 K1 C1 H01 C2 w3 K2 T0 H11 B0 w4 E W0 d f00 T1 f01 f02 B1 f03 M0 f11 i W1 f10 M1 W2 f12 f13",
-         "s08 s8c q0 h005 h016 scg q1 h027 m0 q2 p0 t0 m1 t1 m2 h035 p1 h106 h115 h121 "
-         "a00 a01 x00 x01 a10 a11 x10 x11 n0 l0 v130 R00 R01 R02 D00 D01 D02 n1 A0 l1 C0 P0 R12 R10 D10 R11 A1 F0 D11 D12 P1 "
-         "K0 H00 H10 F1 C1 K1 C2 H01 H11 T0 K2 B0 E W0 d f00 T1 f01 B1 f02 f03 M0 M1 W1 f10 f11 W2 f12 f13")
-TAIL = "s08 s8c r0 r1 scg r2"
-HEAD = 64
+BANKS = 8
+ORDER = ("b2 z0 b0 b4 b3 u0 z3 z4 b5 z2 r5 u1 r1 b6 r2 b1 j4 j5 z1 b7 c0 r0 zb u2 b8 b9 r4 u3 bb ba i0 u4 r3 q0 l0 u5 w5 q1 w0 r9 e0 l2 "
+         "bd t00 q2 c1 bc e1 l1 t10 j0 m0 m1 z5 l3 t01 r6 r8 p0 h00 w1 t20 w6 j2 r7 p1 w2 e2 y00 t11 w7 N00 w3 N10 ra m2 h30 a00 p2 t21 "
+         "a10 z8 j3 x00 z7 N01 N11 la N20 j1 w4 a01 j8 w8 x10 y30 c2 a20 h01 h31 a11 j6 N21 x20 y01 x01 h33 a21 w9 l4 y31 n0 h02 x11 i2 "
+         "D00 h03 y03 j7 l6 D01 x21 v33 C0 h32 y02 v32 n1 P0 wa A3 D10 D11 A0 wb F0 l7 i9 P1 K0 l5 l8 wc wd H00 H10 F1 C1 C2 K1 H01 H11 "
+         "K2 l9 T0 i7 f00 E we i1 c6 f01 c3 d i3 f02 i4 ia M T1 i6 f10 c5 c4 i5 f11 f12 i8 z6 c7 W0 c8 G W1 O0 O1 U0 O2 O3 U1",
+         "s08 q0 s8c t00 e0 h01 h00 h03 h02 scg t01 q1 m0 t10 y00 y01 q2 p0 e1 t11 m1 e2 p1 N00 t20 a00 m2 L0 h33 t21 N10 a10 p2 x00 "
+         "N01 y33 h32 y03 N11 y02 N20 h31 a01 x10 y32 y31 a20 a11 h30 y30 x20 x01 N21 n0 a21 x11 D00 x21 D01 C0 z9 n1 P0 D10 A0 A3 F0 "
+         "D11 P1 K0 H00 H10 F1 C1 C2 K1 H01 H11 K2 T0 L1 f00 za W1 f01 E W0 L2 f02 d M T1 f10 O0 f11 L3 f12 G O1 O2 O3 L4 U0 L5 U1")
+TAIL = "s8c s08 r8c r08 scg rcg"
 
 SCRATCH = {}
 PLACES = {}
@@ -40,34 +44,34 @@ def _parts(name, dtype, *parts):
     _sb(name, at, dtype)
 
 
-for _k in range(8):
+for _k in range(BANKS):
     SCRATCH["ps%d" % _k] = ("psum", [128, 512], "float32")
-for _n, _c in (("xa", 2048), ("xb", 2048), ("xc", 2048), ("ut", 512), ("vt", 512), ("wm", 1024), ("nd", 512), ("zb", 1040),
-               ("zt", 520), ("junk", 1408), ("yt", 1040), ("ha", 2056),
-               ("f1", 1032), ("f2", 520), ("f3", 520), ("f4", 520), ("f5", 520), ("f6", 520), ("f7", 520)):
+for _n, _c in (("xa", 2048), ("xb", 2048), ("xc", 2048), ("ut", 512), ("vt", 512), ("wm", 1024), ("nd", 512), ("junk", 1088),
+               ("yt", 1040), ("ha", 2056), ("f1", 1032), ("f2", 520), ("f3", 512), ("f4", 608), ("f5", 512), ("f6", 520), ("f7", 512)):
     _sb(_n, _c, "bfloat16")
-for _n, _c in (("sq", 512), ("acc", 16), ("e8", 144), ("yo", 512), ("wo", 512)):
+_parts("zb", "bfloat16", ("digits", 128), ("zt", 520))
+for _n, _c in (("sq", 512), ("sp", 512), ("acc", 8), ("yo", 512), ("wo", 512), ("bc", 128)):
     _sb(_n, _c, "float32")
-_parts("work", "float32", ("va", 512), ("vb", 512), ("sa", 520), ("sb", 520))
-_parts("fixed", "float32", ("m32", 64), ("k32", 64), ("d5", 128), ("dd", 32), ("d3", 8), ("im", 128), ("uf", 16), ("ir", 8),
-       ("key", 8), ("gcol", 8), ("kk", 192), ("mc", 192), ("cols", 8))
-_parts("choose", "float32", ("cm", 8), ("tr", 64), ("row", 64), ("bc", 128), ("mk", 192), ("fold", 192))
-_parts("whole", "int32", ("ip", 128), ("ip2", 128), ("bi", 128), ("bj", 128), ("ib", 8), ("uu", 8), ("uv", 8), ("wi", 192),
-       ("wj", 192))
-_parts("lists", "int32", ("la", 128), ("lb", 128), ("lc", 128), ("ld", 128), ("le", 128))
-for _n, _c in (("ulist", 16), ("off", 16), ("offs", 128), ("offm", 4), ("offe", 4)):
+_parts("work", "float32", ("sa", 520), ("sb", 520))
+_parts("fixed", "float32", ("m1", 64), ("pm", 8), ("dd", 24), ("im", 128), ("uf", 16), ("pw", 16), ("gd", 8), ("cols", 8),
+       ("pat", 64), ("jq", 96))
+_parts("choose", "float32", ("cm", 8), ("tr", 64), ("slots", 96), ("fold", 96))
+_parts("whole", "int32", ("bi", 128), ("bj", 128), ("ci", 128), ("cj", 128), ("mi", 64), ("mj", 64), ("gl", 24))
+_parts("lists", "int32", ("la", 128), ("lb", 128))
+for _n, _c in (("ulist", 16), ("glist", 8), ("off", 16), ("offs", 128), ("offm", 4), ("offe", 4)):
     _sb(_n, _c, "uint16")
-for _n, _c in (("uq", 128), ("up", 256), ("vq", 128), ("wq", 512), ("c1", 512), ("c2", 256), ("c3", 256), ("c4", 512),
-               ("c5", 128), ("c6", 512), ("pq", 256), ("nq", 128), ("zq", 256), ("xq2", 512)):
+for _n, _c in (("uq", 128), ("up", 256), ("vq", 128), ("wq", 512), ("c1", 512), ("c2", 256), ("c3", 256), ("c4", 152),
+               ("c5", 128), ("c6", 512), ("pq", 384), ("nq", 128), ("zq", 272), ("xq2", 512)):
     _mx(_n, _c)
 for _t in range(ROUNDS):
-    for _n, _c in (("xq", 512), ("aq", 544), ("cq", 192), ("lq", 256), ("mq", 64), ("eq", 128), ("hq", 320)):
+    for _n, _c in (("xq", 512), ("aq", 544), ("cq", 192), ("lq", 256), ("eq", 128), ("hq", 320)):
         _mx("%s%d" % (_n, _t), _c)
-    _parts("run%d" % _t, "float32", ("ra%d" % _t, HEAD + 520), ("rb%d" % _t, HEAD + 520))
+    _parts("run%d" % _t, "float32", ("ra%d" % _t, 520), ("rb%d" % _t, 520))
     for _n, _c in (("st", 16), ("rr", 4), ("se", 16)):
         _sb("%s%d" % (_n, _t), _c, "float32")
-SEMAPHORES = ["nv", "ns", "nt", "ng", "lu", "lx0", "lx1", "lx2", "lw", "lv", "done", "left"] + [
-    "%s%d" % (a, t) for t in range(ROUNDS) for a in ("ac", "ad", "as", "bc", "bs", "gc", "gn")]
+LANDINGS = ("am", "ac", "as", "bm", "bc", "bs", "gn", "gc")
+SEMAPHORES = ["nv", "ns", "nt", "ng", "lu", "lx0", "lx1", "lx2", "lw0", "lw1", "lv", "done", "left"] + [
+    "%s%d" % (a, t) for t in range(ROUNDS) for a in LANDINGS]
 
 
 def rank_program(g, core, T, topo):
@@ -81,6 +85,7 @@ def rank_program(g, core, T, topo):
     queue = {"v": g.vector, "s": g.scalar, "t": g.tensor, "g": g, "y": g.sync}
     counter = {"v": "nv", "s": "ns", "t": "nt", "g": "ng"}
     span = [set()]
+    banks, free = {}, list(range(BANKS))
     total, known, snaps, seen, waited = {}, {q: {} for q in queue}, {}, {}, {}
 
     def P(name, a, b, step=1, r0=0, r1=128):
@@ -130,8 +135,11 @@ def rank_program(g, core, T, topo):
             seen.setdefault(p[0], []).append((p, True, q, tok))
 
     def do(q, call, reads, writes, alike=False):
-        wait(q, conflicts(q, reads, writes))
         s = counter[q]
+        deps = conflicts(q, reads, writes)
+        if q == "t" and alike:
+            deps.pop(s)
+        wait(q, deps)
         if q == "g":
             rows = {p[4:6] for p in reads + writes}
             if total.get(s) and rows | span[0] != {(0, 128)} and not alike:
@@ -170,10 +178,19 @@ def rank_program(g, core, T, topo):
         do("v", lambda: g.vector.tensor_tensor_scan(V(out), V(d0), V(d1), V(initial) if held else initial, op0, op1),
            [d0, d1] + [initial] * held, [out])
 
+    def flip(out, src):
+        do("v", lambda: g.vector.transpose(V(out), V(src)), [src], [out])
+
+    def gather(out, win, lst, other):
+        do("v", lambda: g.vector.tensor_tensor(V(out), V(win).indirect(V(lst)), V(other), A.add), [win, lst, other], [out])
+
     def act(out, a, func=F.Copy, scale=None, bias=None):
         more = {k: x for k, x in (("scale", scale), ("bias", bias)) if x is not None}
         do("s", lambda: g.scalar.activation(V(out), V(a), func, **{k: V(x) if isinstance(x, tuple) else x for k, x in more.items()}),
            [a] + [x for x in more.values() if isinstance(x, tuple)], [out])
+
+    def zero(p):
+        act(p, P("zt", 0, len(range(*p[1:4])), 1, p[4], p[5]))
 
     def below(out, src, end, junk):
         do("s", lambda: g.scalar.activation(V(junk), V(src), F.Sign, bias=V(end), scale=-1.0, accum_out=V(out)),
@@ -183,11 +200,14 @@ def rank_program(g, core, T, topo):
         do("v", lambda: g.vector.quantize_mx(T[q + "c"][:, a:b], T[q + "s"][:, a:b], V(src)), [src],
            [P(q + "c", a, b), P(q + "s", a, b)])
 
-    def mm(bank, n, w, wa, x, xa):
+    def mm(name, n, w, wa, x, xa, start=True, stop=True):
+        if start:
+            banks[name] = free.pop(0)
+        bank = banks[name]
         do("t", lambda: g.tensor.matmul_mx(T["ps%d" % bank][:, 0:n], T[w + "c"][:, wa:wa + 128], T[w + "s"][:, wa:wa + 128],
-                                           T[x + "c"][:, xa:xa + n], T[x + "s"][:, xa:xa + n], True, True),
+                                           T[x + "c"][:, xa:xa + n], T[x + "s"][:, xa:xa + n], start, stop),
            [P(w + "c", wa, wa + 128), P(w + "s", wa, wa + 128), P(x + "c", xa, xa + n), P(x + "s", xa, xa + n)],
-           [P("ps%d" % bank, 0, n)])
+           [P("ps%d" % bank, 0, n)], not start)
 
     def pick(out, c, d, win, b, lst, e, f):
         i = P(lst, e, f)
@@ -197,8 +217,20 @@ def rank_program(g, core, T, topo):
         do("s", lambda: g.scalar.activation(T[out + "s"][:, c:d], T[win + "s"][:, 0:b].indirect(V(i)), F.Copy),
            [P(win + "s", 0, b), i], [P(out + "s", c, d)])
 
-    def ps(k, a, b, r1=128):
-        return P("ps%d" % k, a, b, 1, 0, r1)
+    def ps(name, a, b, step=1, r1=128):
+        return P("ps%d" % banks[name], a, b, step, 0, r1)
+
+    def drop(name):
+        free.append(banks.pop(name))
+
+    def iota(p, pattern, base, ch, f=False):
+        if f:
+            do("g", lambda: g.iota(V(p), pattern, base, ch, allow_small_or_imprecise_dtypes=True), [], [p])
+        else:
+            do("g", lambda: g.iota(V(p), pattern, base, ch), [], [p])
+
+    def select(out, src, pattern, op, value, base, ch):
+        do("g", lambda: g.affine_select(V(out), V(src), pattern, op, value, base, ch), [src], [out])
 
     def address(r):
         rid, pid = topo.addr(T.cores[r])[:2]
@@ -213,7 +245,6 @@ def rank_program(g, core, T, topo):
     assert [owner[r] for r in near] == [o ^ 1]
     outside = topo.engines(core, T.cores[far[0]])
     inside = [e for e in topo.engines(core, T.cores[near[0]]) if e not in outside]
-    share = len(outside) // len(far)
     assert all(topo.engines(core, T.cores[r]) == outside for r in far + blocks[1 - block])
     from_mates = len(outside) + len(inside)
 
@@ -237,312 +268,318 @@ def rank_program(g, core, T, topo):
     dma("s", T.ut[:], T.u[:], "lu", 16, [], [P("ut", 0, 512)])
     for k, (a, b) in enumerate(pieces):
         dma("y", T.xa[:, 4 * a:4 * b], T.x[:, 4 * a:4 * b], "lx%d" % k, 16, [], [P("xa", 4 * a, 4 * b)])
-    wait("y", {"lx0": 16})
-    dma("y", side("wqc", 0, 512), T.wc[:], "lw", 32, [], [P("wqc", 0, 512)])
-    dma("y", T.wqs[:], T.ws[:], "lw", 32, [], [P("wqs", 0, 512)])
-    wait("y", {"lw": 32})
+    dma("y", T.wqs[:], T.ws[:], "lw0", 32, [], [P("wqs", 0, 512)])
+    dma("y", side("wqc", 0, 256), T.wc[:, 0:1024], "lw0", 32, [], [P("wqc", 0, 256)])
+    dma("y", side("wqc", 256, 512), T.wc[:, 1024:2048], "lw1", 16, [], [P("wqc", 256, 512)])
+    wait("y", {"lw1": 16})
     dma("y", T.vt[:], T.v[:], "lv", 16, [], [P("vt", 0, 512)])
 
-    def iota(p, pattern, base, ch, f=False):
-        if f:
-            do("g", lambda: g.iota(V(p), pattern, base, ch, allow_small_or_imprecise_dtypes=True), [], [p])
+    pair = (1 - (o >> 1), o >> 1)
+    shift, seventh, half, place, element, mixed = [P("cols", k, k + 1) for k in range(6)]
+
+    def columns_of_u(k):
+        (lambda: iota(P("uf", 0, 16), [[16, 16]], 1, 0, True),
+         lambda: select(P("uf", 0, 16), P("uf", 0, 16), [[-1, 16]], A.is_ge, 15.0, 7, 0),
+         lambda: copy(P("ulist", 0, 16), P("uf", 0, 16)),
+         lambda: quant("uq", 0, 128, P("ut", 0, 512)),
+         lambda: pick("up", 0, 128, "uq", 128, "ulist", 0, 8),
+         lambda: pick("up", 128, 256, "uq", 128, "ulist", 8, 16))[k]()
+
+    def blanks(k):
+        (lambda: fill(P("zt", 0, 520), 0.0),
+         lambda: fill(P("work", 512, 1040, 520), NONE),
+         lambda: fill(P("wm", 2, 1024, 4), 0.0),
+         lambda: fill(P("wm", 3, 1024, 4), 0.0),
+         lambda: fill(P("ha", 2048, 2056), 0.0),
+         lambda: zero(Q("tr", 0, 64)),
+         lambda: quant("hq0", 0, 128, P("zt", 0, 512)),
+         lambda: [zero(P("yt", 256 * w + 192, 256 * w + 256)) for w in range(4)],
+         lambda: zero(P("yt", 1024, 1040)),
+         lambda: quant("hq1", 0, 128, P("zt", 0, 512)),
+         lambda: quant("vq", 0, 128, P("vt", 0, 512)),
+         lambda: fill(P("wm", 513, 1024, 4), 0.0))[k]()
+
+    def bits(k):
+        (lambda: zero(P("f1", 0, 516)),
+         lambda: zero(P("f1", 516, 1032)),
+         lambda: fill(P("pw", 0, 8), 0.5),
+         lambda: scan(P("pw", 8, 16), P("pw", 0, 8), P("pw", 0, 8), 16384.0, A.mult, A.max),
+         lambda: iota(P("im", 0, 128), [[64, 2], [-48, 4], [1, 16]], 256, 0, True),
+         lambda: select(P("gd", 0, 8), P("pw", 8, 16), [[-16, 8]], A.is_equal, 0.0, 0, 1),
+         lambda: do("v", lambda: g.vector.tensor_reduce(V(shift), V(P("gd", 0, 8)), AxisListType.X, A.add), [P("gd", 0, 8)], [shift]),
+         lambda: ts(P("bi", 0, 128), P("im", 0, 128), shift, A.mult),
+         lambda: ts(seventh, shift, 64.0, A.is_equal, 8192.0, A.mult),
+         lambda: ts(P("bj", 0, 128), P("bi", 0, 128), 8192, A.bitwise_and),
+         lambda: ts(P("f1", 3 + 512 * pair[0], 515 + 512 * pair[0], 4), P("bj", 0, 128), 0.0, A.not_equal, MISS, A.mult),
+         lambda: ts(P("f1", 3 + 512 * pair[1], 515 + 512 * pair[1], 4), P("bj", 0, 128), seventh, A.not_equal, MISS, A.mult),
+         lambda: quant("c1", 0, 256, P("f1", 3, 1027)),
+         lambda: quant("c1", 256, 512, P("f1", 2, 1026)))[k]()
+
+    def rows(k):
+        if k < 3:
+            a, b, pattern, step = ((0, 32, [[0, 2], [-16, 4], [-1, 4]], 1), (32, 64, [[0, 2], [-4, 16]], 1), (64, 128, [[0, 4], [-4, 16]], 4))[k]
+            iota(P("ci", a, b), pattern, 64, step)
+        elif k < 5:
+            a, b, mask = ((0, 32, 51), (32, 128, 60))[k - 3]
+            ts(P("cj", a, b), P("ci", a, b), mask, A.bitwise_and)
+        elif k == 5:
+            fill(P("f5", 0, 512), 0.0)
+        elif k < 10:
+            a, at = k - 6, (32, 0, 64, 96)[k - 6]
+            ts(P("f5", 129 * a, 128 * a + 128, 4), P("cj", at, at + 32), 0.0, A.is_equal)
         else:
-            do("g", lambda: g.iota(V(p), pattern, base, ch), [], [p])
+            quant("c5", 0, 128, P("f5", 0, 512))
 
-    def select(out, src, pattern, op, value, base, ch):
-        do("g", lambda: g.affine_select(V(out), V(src), pattern, op, value, base, ch), [src], [out])
+    def pairs(k):
+        if k < 3:
+            iota(P("mi", k, 64, 4), [[0, 2], [4096, 2], [-16, 4]], 48, 16 >> 2 * k)
+        elif k == 3:
+            iota(P("mi", 3, 64, 4), [[32 * (pair[1] - pair[0]), 2], [4112, 2], [-16, 4]], 255 + 32 * pair[0], -1)
+        elif k < 6:
+            fill(P("cols", 2, 3, 1, 64 * k - 256, 64 * k - 192), 4096.0 * (k - 4))
+        elif k == 6:
+            ts(P("mj", 0, 64), P("mi", 0, 64), 4096 + 48, A.bitwise_and)
+        elif k == 7:
+            ts(P("m1", 0, 64), P("mj", 0, 64), half, A.is_equal)
+        else:
+            iota(P("pm", 0, 2), [[64, 2]], -32, 0, True)
 
-    iota(P("ip", 0, 128), [[0, 8], [-1, 16]], 16, 1)
-    for e in range(2):
-        iota(P("im", 64 * e, 64 * e + 64), [[4369, 4], [256, 4], [16, 4]], 4096 * e, 0, True)
-    iota(P("uf", 0, 16), [[16, 16]], 1, 0, True)
-    iota(P("uu", 0, 1), [[0, 1]], 0, 1)
-    select(P("uf", 0, 16), P("uf", 0, 16), [[-1, 16]], A.is_ge, 15.0, 7, 0)
-    fill(P("zt", 0, 520), 0.0)
-    act(P("f1", 0, 516), P("zt", 0, 516))
-    act(P("f1", 516, 1032), P("zt", 0, 516))
-    act(P("f2", 0, 520), P("zt", 0, 520))
-    for k in range(4):
-        fill(P("gcol", 0, 1, 1, 32 * k, 32 * k + 32), 2.0 ** (12 - 4 * k))
-    for k in range(4):
-        fill(P("gcol", 0, 1, 1, 32 * k, 32 * k + 16), 2.0 ** (13 - 4 * k))
-    ts(P("ip2", 0, 128), P("ip", 0, 128), 15, A.bitwise_and)
-    fill(P("ha", 2048, 2056), 0.0)
-    ts(P("bi", 0, 128), P("im", 0, 128), P("gcol", 0, 1), A.mult)
-    ts(P("d5", 0, 128), P("ip2", 0, 128), 0.0, A.is_equal)
-    fill(P("wm", 2, 1024, 4), 0.0)
-    ts(P("bj", 0, 128), P("bi", 0, 128), 8192, A.bitwise_and)
-    ts(P("cols", 3, 4), P("gcol", 0, 1), 1.0, A.is_equal, 8192.0, A.mult)
-    fill(P("wm", 3, 1024, 4), 0.0)
-    top = 512 * (o >> 1)
-    ts(P("f1", 515 - top, 1027 - top, 4), P("bj", 0, 128), P("d5", 0, 1), A.mult)
-    ts(P("f1", 3 + top, 515 + top, 4), P("bj", 0, 128), P("cols", 3, 4), A.not_equal, P("d5", 0, 1), A.mult)
-    copy(P("ulist", 0, 16), P("uf", 0, 16))
-    for e, w in ((0, 64.0), (1, 8.0), (2, 1.0), (3, 0.0)):
-        act(P("f5", e, 512, 4), P("d5", 0, 128), scale=w)
-    fill(P("sa", 512, 516), NONE)
-    fill(P("sb", 512, 516), NONE)
-    quant("c1", 0, 256, P("f1", 3, 1027))
-    quant("uq", 0, 128, P("ut", 0, 512))
-    quant("c1", 256, 512, P("f1", 2, 1026))
-    pick("up", 0, 128, "uq", 128, "ulist", 0, 8)
-    act(P("zb", 0, 520), P("zt", 0, 520))
-    iota(P("cols", 5, 6), [[0, 1]], 0, 1, True)
-    iota(P("uu", 1, 2), [[0, 1]], 0, 17)
-    iota(P("ir", 0, 8), [[4, 2], [-1, 4]], 3, 0, True)
-    for e in range(2):
-        iota(P("uu", 3, 5, 1, 64 * e, 64 * e + 64), [[64 * (o >> 1) - 32, 2]], 32 * (1 - (o >> 1)) + 80 * e, 1)
-        iota(P("cols", 4, 5, 1, 64 * e, 64 * e + 64), [[0, 1]], 4 * e, 0, True)
-    iota(P("dd", 0, 32), [[0, 32]], 0, 0, True)
-    select(P("f2", 3, 515, 4), P("f2", 3, 515, 4), [[0, 8], [16, 16]], A.not_equal, 1.0, -32, -1)
-    iota(P("wi", 0, 192), [[-16, 3], [16, 4], [1, 16]], 240, 0)
-    select(P("f2", 3, 515, 4), P("f2", 3, 515, 4), [[16, 8], [1000, 16]], A.not_equal, 1.0, 0, -1)
+    def slots(k):
+        (lambda: iota(P("gl", 6, 12), [[4, 3], [0, 2]], 4, 0),
+         lambda: iota(P("gl", 0, 6), [[1, 3], [0, 2]], 1, 4),
+         lambda: iota(P("gl", 12, 18), [[16, 3], [0, 2]], 16, 1),
+         lambda: iota(P("gl", 18, 24), [[-16, 3], [0, 2]], 16 * (o + 3), 1),
+         lambda: ts(element, P("mj", 12, 13), 0.0625, A.mult),
+         lambda: ts(place, P("cj", 64, 65), 0.25, A.mult),
+         lambda: ts(mixed, P("mj", 5, 6), element, A.add),
+         lambda: ts(P("gl", 0, 24), P("gl", 0, 24), 63, A.bitwise_and),
+         lambda: [copy(P("glist", 0, 6, 1, 32 * a, 32 * a + 32), P("gl", 6 * a, 6 * a + 6, 1, 32 * a, 32 * a + 32)) for a in (0, 2, 3)],
+         lambda: ts(P("glist", 0, 6, 1, 32, 64), P("gl", 6, 12, 1, 32, 64), P("cols", 5, 6, 1, 32, 64), A.add),
+         lambda: [act(P("jq", 32 * j, 32 * j + 32), P("zt", 0, 32), F.Identity, 1.0, 0.25 * j) for j in range(3)])[k]()
 
-    def weigh(at, row, w, pattern=((-16, 8),)):
-        select(P("dd", at, at + 8), P("dd", at, at + 8), [list(p) for p in pattern], A.not_equal, float(w), -row, 1)
-
-    for k in range(6):
-        weigh(0, 2 + k, (9, 18, -1, -2, -8, -16)[k])
-        if k < 5:
-            weigh(8, (2, 3, 8, 9, 0)[k], (64, 128, -64, -128, -1024)[k])
+    def units(k):
         if k < 2:
-            weigh(16, 2 + k, 16 << k, ((-34, 4), (-16, 2)))
-    select(P("dd", 0, 24), P("dd", 0, 24), [[0, 3], [-17, 8]], A.not_equal, 0.0, -2, 1)
-
-    def constants_early():
-        for r in ("ra0", "rb0"):
-            fill(P(r, 0, HEAD), LOW)
-        fill(Q("tr", 0, 64), 0.0)
-
-    def constants_mid():
-        quant("c5", 0, 128, P("f5", 0, 512))
-
-    def constants_places(k):
-        if k == 0:
-            ts(P("ib", 1, 2), P("uu", 0, 1), 124, A.bitwise_and)
-        elif k == 1:
-            ts(P("uu", 2, 3), P("ib", 1, 2), 4.0, A.mult, P("cols", 5, 6), A.add)
+            zero(P(("f6", "f2")[k], 0, 520))
         elif k == 2:
-            ts(P("uv", 0, 5), P("uu", 0, 5), 4, A.logical_shift_right, 3, A.bitwise_and)
+            select(P("f6", 3, 515, 4), P("f6", 3, 515, 4), [[-1, 128]], A.not_equal, 1.0, 0, 1)
         elif k == 3:
-            ts(P("key", 0, 5), P("uv", 0, 5), P("cols", 4, 5), A.add)
-        elif k < 9:
-            c = k - 4
-            at = 8 * c if c < 4 else 56
-            ts(P("m32", at, at + 8), P("ir", 0, 8), P("key", c, c + 1), A.is_equal)
+            select(P("f2", 3, 515, 4), P("f6", 3, 515, 4), [[0, 8], [16, 16]], A.not_equal, 1.0, -32, -1)
+        elif k == 4:
+            select(P("f2", 3, 515, 4), P("f2", 3, 515, 4), [[-1, 8], [1, 16]], A.not_equal, 0.0, -2, 0)
+        elif k < 7:
+            quant("c2", 128 * k - 640, 128 * k - 512, P("f2", 8 - k, 520 - k))
         else:
-            act(P("m32", 32, 56), P("m32", 0, 24))
-            act(P("k32", 0, 32), P("m32", 0, 32), F.Identity, 1016.0, -1024.0)
-            act(P("k32", 32, 64), P("m32", 32, 64), F.Identity, 1016.0, -1024.0)
+            quant("c6", 128 * k - 896, 128 * k - 768, P("f6", 10 - k, 522 - k))
 
-    def constants_choices(k):
+    def weigh(at, row, w, groups=8, step=-128):
+        p = P("dd", at, at + 8)
+        select(p, p, [[step, 8 // groups], [-16, groups]], A.not_equal, float(w), -row, 1)
+
+    def weights(k):
+        if k < 4:
+            weigh(0, 6 + k, -256 << (k & 1))
+        elif k == 4:
+            weigh(0, 0, -4096)
+        else:
+            x, e = divmod(k - 5, 2)
+            if x < 4:
+                weigh(8, (2, 4, 4, 6)[x] + e, (-4, -16, -4, -16)[x] << e, (8, 8, 2, 4)[x])
+            else:
+                weigh(8, 2 + e, -64 << e, 2, -34)
+
+    def tiles(k):
         if k == 0:
-            copy(P("cols", 2, 3), P("ip2", 0, 1))
-            fill(P("ib", 2, 3, 1, 0, 32), 0)
-            ts(P("ib", 2, 3, 1, 32, 64), P("ip2", 0, 1, 1, 32, 64), 3, A.bitwise_and)
-            ts(P("ib", 2, 3, 1, 64, 96), P("ip2", 0, 1, 1, 64, 96), 2, A.logical_shift_right)
-            fill(P("ib", 2, 3, 1, 96, 128), o)
+            iota(P("dd", 0, 24), [[0, 24]], 0, 0, True)
         elif k == 1:
-            ts(P("cols", 6, 7), P("ib", 2, 3), 16.0, A.mult, P("cols", 2, 3), A.subtract)
+            iota(P("pat", 0, 64), [[0, 64]], 1, 0, True)
         elif k == 2:
-            ts(P("wj", 0, 192), P("wi", 0, 192), P("cols", 6, 7), A.add)
-        elif k == 3:
-            ts(P("wi", 0, 192), P("wj", 0, 192), 63, A.bitwise_and)
+            select(P("pat", 0, 64), P("pat", 0, 64), [[-1, 4], [0, 4], [1, 4]], A.is_equal, 0.0, 0, 0)
+        elif k < 7:
+            j, e = divmod(k - 3, 2)
+            for r in range(4 * e, 4 * e + 4):
+                act(P(("f3", "f7")[j], 64 * r, 64 * r + 64), P("pat", 0, 64), scale=P("dd", 8 * j + r, 8 * j + r + 1))
         else:
-            ts(P("mc", 0, 192), P("wi", 0, 192), 0.0, A.is_equal)
-
-    def constants_wait():
-        act(P("kk", 0, 192), P("zt", 0, 192), F.Identity, 1.0, 4096.0)
-        act(P("f6", 0, 520), P("zt", 0, 520))
-        act(P("kk", 0, 192, 64), P("ir", 1, 4), scale=0.25)
-        for f in ("f3", "f7"):
-            act(P(f, 0, 520), P("zt", 0, 520))
-        ts(P("ib", 0, 1), P("ip", 0, 1), 3, A.bitwise_and)
-        tt(P("d3", 0, 8), P("dd", 8, 16), P("dd", 16, 24), A.add)
-        quant("hq0", 0, 128, P("zt", 0, 512))
-        copy(P("cols", 1, 2), P("ib", 0, 1))
-
-    def constants_hop():
-        for r in range(16):
-            act(P("f3", 4 * r + r // 4, 512, 64), P("dd", 0, 8), scale=4.0)
-            act(P("f7", 4 * r + r // 4, 512, 64), P("d3", 0, 8), scale=4.0)
-        for e in range(2):
-            quant("c2", 128 * e, 128 * e + 128, P("f2", 3 - e, 515 - e))
-
-    def constants_last():
-        quant("c3", 0, 128, P("f3", 0, 512))
-        quant("c3", 128, 256, P("f7", 0, 512))
-        act(P("yt", 0, 520), P("zt", 0, 520))
-        act(P("yt", 520, 1040), P("zt", 0, 520))
-        act(P("f4", 0, 520), P("zt", 0, 520))
-        for k in range(8):
-            weigh(24, 2 + k, 1 << k)
-        weigh(24, 2, 0, ((-17, 8),))
+            quant("c3", 128 * k - 896, 128 * k - 768, P(("f3", "f7")[k - 7], 0, 512))
 
     state = ["xa", "xb", "xc"]
-    end = HEAD + 512
     mine, theirs = 64 * o, 1 - block
     slot = {r: 64 * (owner[r] & 1) for r in far}
     slot[near[0]] = 128
+    runs = (((0, 0, 2), (1, 1, 2)), ((0, 256, 1),), ((1, 384, 1),))
+    spans = pieces + ((256, 512),)
 
     def new_state(t, a, b):
-        i, y, x, z = P("offs", a // 4, b // 4), P("yt", 0, 1040), P(state[t], 4 * a, 4 * b), P(state[t + 1], 4 * a, 4 * b)
-        do("v", lambda: g.vector.tensor_tensor(V(z), V(y).indirect(V(i)), V(x), A.add), [y, i, x], [z])
-
-    def count(h, k):
-        return P("acc", 8 * h + k, 8 * h + k + 1)
-
-    def digit(h, k):
-        return P("zb", 520 * h + k, 520 * h + 128, 4)
+        gather(P(state[t + 1], 4 * a, 4 * b), P("yt", 0, 1040), P("offs", a // 4, b // 4), P(state[t], 4 * a, 4 * b))
 
     def marks(k):
-        a, b = pieces[k]
-        at = 512 * (a // 256) + 2 * (a % 256)
-        for e in range(2):
-            tt(P("wm", at + e, at + 2 * (b - a), 4), P("ps%d" % (0, 4, 6)[k], e, b - a, 2), P("sq", a + e, b, 2), A.is_le)
+        for e, a, step in runs[k]:
+            at = 512 * min(k, 1)
+            tt(P("wm", at + e, at + 512, 4), ps(("scores", k), a - pieces[k][0], pieces[k][1] - pieces[k][0], step),
+               P("sq", a, pieces[k][1], step), A.is_le)
+        drop(("scores", k))
 
-    def missing(j):
-        quant("pq", 128 * j, 128 * j + 128, P("wm", 512 * j, 512 * j + 512))
-        for h in range(2):
-            for e in range(2):
-                bank = (1, 0, 3, 7)[2 * h + e]
-                mm(bank, 128, "c1", 256 * e + 128 * h, "pq", 128 * j)
-                act(P(("va", "vb")[h], 256 * j + e, 256 * j + 256, 2), ps(bank, 0, 128), scale=MISS)
+    def missing(k, h):
+        for e, a, step in runs[k]:
+            mm(("missing", a, h), 128, "c1", 256 * e + 128 * h, "pq", 128 * k)
+
+    def masked(k, h):
+        for e, a, step in runs[k]:
+            b = pieces[k][1]
+            tt(P(("sa", "sb")[h], a, b, step), ps(("missing", a, h), 0, 128), P("sp", a, b, step), A.add)
+            drop(("missing", a, h))
+
+    def digits(h, k):
+        c, n, less, more = [P("acc", 4 * h + i, 4 * h + i + 1) for i in range(4)]
+        at = 64 - 64 * h
+        if k == 0:
+            ts(P("acc", 4 * h + 2, 4 * h + 4), P("pm", 0, 2), c, A.mult)
+        else:
+            act(P("digits", at, at + 32), P("zt", 0, 32), F.Identity, 1.0, more)
+            act(P("digits", at + 32, at + 64), P("m1", 32 * h, 32 * h + 32), F.Identity, n, less)
 
     def product(h):
-        quant("zq", 128 * h, 128 * h + 128, P("zb", 520 * h, 520 * h + 512))
-        mm(6 + h, 128, "c5", 0, "zq", 128 * h)
+        quant("zq", 136 * h, 136 * h + 136, P("zb", 64 - 64 * h, 608 - 64 * h))
+        for k in range(2):
+            mm(("places", h), 128, "c5", 0, "zq", 136 * h + 8 * k, k == 0, k == 1)
 
     def places(h):
-        for a in range(4):
-            ts(P("off", 8 * h, 8 * h + 8, 1, 32 * a, 32 * a + 32), P("ps%d" % (6 + h), 8 * a, 8 * a + 8, 1, 32 * a, 32 * a + 32),
-               -float(HEAD), A.add)
+        copy(P("off", 8 * h, 8 * h + 8), ps(("places", h), 0, 8))
+        drop(("places", h))
 
     def turn(n):
-        src, out = Q("tr", 32 * n, 32 * n + 32), Q("row", 32 * n, 32 * n + 32)
-        do("v", lambda: g.vector.transpose(V(out), V(src)), [src], [out])
-
-    def spread(n):
-        for k in range(2):
-            first = 64 * (o & 1) + 32 * k
-            src, out = P("row", 32 * n, 32 * n + 32, 1, first, first + 1), P("bc", 64 * n + 32 * k, 64 * n + 32 * k + 32)
-            do("g", lambda: g.partition_broadcast(V(out), V(src), 128), [src], [out], k == 1)
+        for first in (0, 64):
+            flip(P("bc", 64 * n, 64 * n + 32, 1, first, first + 64), Q("tr", 32 * n, 32 * n + 32))
+        for a in range(4):
+            first = 64 * (o & 1) + 32 * (1 - a % 2)
+            flip(P("bc", 64 * n + 32, 64 * n + 64, 1, 32 * a, 32 * a + 32), P("tr", 32 * n, 32 * n + 32, 1, first, first + 32))
 
     def fold(n, k):
-        if k < 2:
-            for c in range(3):
-                at, row = 64 * (2 - c if n else c) + 32 * k, 64 * n + 32 * k
-                tt(P("mk", at, at + 32), P("bc", row, row + 32), P("mc", 64 * c + 32 * k, 64 * c + 32 * k + 32), A.mult)
-        elif k == 2:
-            scan(P("fold", 0, 192), P("kk", 0, 192), P("mk", 0, 192), 4096.0, A.min, A.add)
+        if k == 0:
+            gather(P("slots", 0, 96), P("bc", 64 * n, 64 * n + 64), P("glist", 0, 6), P("jq", 0, 96))
+        elif k == 1:
+            flip(P("fold", 0, 96), P("slots", 0, 96))
         else:
-            ts(P(("offm", "offe")[n], 0, 3), P("fold", 63, 192, 64), 64.0, A.mult, P("cols", 2, 3), A.add)
+            ts(P(("offm", "offe")[n], 0, 3), P("fold", 0, 96, 32), 64.0, A.mult, place, A.add)
+
+    def wishes(j):
+        for e in range(2):
+            a, step = (runs[0] + runs[1] + runs[2])[2 * j + e][1:]
+            mm("wishes", 128, "c2", 128 * e, "pq", 256 * j)
+            act(P("nd", a, a - a % step + 128 * step, step), ps("wishes", 0, 128), F.Sign)
+            drop("wishes")
 
     def offsets(k):
         if k == 0:
             quant("nq", 0, 128, P("nd", 0, 512))
             for j in range(2):
-                mm(6 + j, 128, "c3", 128 * j, "nq", 0)
+                mm("offsets", 128, "c3", 128 * j, "nq", 0, j == 0, j == 1)
         elif k == 1:
-            ts(P("la", 0, 128), ps(6, 0, 128), 4.0 * 36, A.add)
-            ts(P("lb", 0, 128), ps(7, 0, 128), 4.0 * 1280, A.add)
+            ts(P("la", 0, 128), ps("offsets", 0, 128), element, A.add, 4.0 * (6 * 64 + 63 - 16) + 4096.0, A.add)
+            drop("offsets")
         elif k == 2:
-            ts(P("lc", 0, 128), P("la", 0, 128), 12, A.bitwise_and)
-            ts(P("ld", 0, 128), P("la", 0, 128), 1, A.logical_shift_right, 48, A.bitwise_and)
-            ts(P("le", 0, 128), P("lb", 0, 128), 4 * (1024 + 240), A.bitwise_and)
-            tt(P("la", 0, 128), P("lc", 0, 128), P("ld", 0, 128), A.add)
-        elif k == 3:
-            tt(P("lb", 0, 128), P("la", 0, 128), P("le", 0, 128), A.add)
+            ts(P("lb", 0, 128), P("la", 0, 128), 4096 + 1023, A.bitwise_and)
         else:
-            ts(P("offs", 0, 128), P("lb", 0, 128), P("cols", 1, 2), A.add, 1024.0, A.min)
+            ts(P("offs", 0, 128), P("lb", 0, 128), 1024.0, A.min)
 
-    def wishes():
-        for j in range(2):
-            for e in range(2):
-                mm(2 * j + e, 128, "c2", 128 * e, "pq", 128 * j)
-        for j in range(2):
-            for e in range(2):
-                tt(P("nd", 256 * j + e, 256 * j + 256, 2), ps(2 * j + e, 0, 128), P("wm", 512 * j + e, 512 * j + 512, 4), A.max)
+    def numbers(k):
+        if k == 0:
+            for k in range(8):
+                weigh(16, 2 + k, 1 << k)
+        elif k == 1:
+            zero(P("f4", 0, 304))
+            zero(P("f4", 304, 608))
+        elif k == 2:
+            for b in range(4):
+                act(P("f4", 33 * b, 32 * b + 32, 4), P("dd", 16, 24))
+        elif k == 3:
+            quant("c4", 0, 152, P("f4", 0, 608))
+        elif k == 4:
+            for b in range(4):
+                mm("numbers", 128, "c4", 8 * b, "nq", 0)
+                act(P("wo", b, 512, 4, 0, 8), ps("numbers", 0, 128, 1, 8), F.Identity, -1.0, 255.0)
+                drop("numbers")
+        else:
+            dma("y", T.wl[:, 0:512], T.wo[0:8, 0:512], "done", 0, [P("wo", 0, 512)], [])
 
     for t in range(ROUNDS):
-        X, last = state[t], t == ROUNDS - 1
-        xq, aq, cq, lq, mq, eq, hq, st, rr, se, ra, rb = [
-            "%s%d" % (s, t) for s in ("xq", "aq", "cq", "lq", "mq", "eq", "hq", "st", "rr", "se", "ra", "rb")]
-        sem = {s: "%s%d" % (s, t) for s in ("ac", "ad", "as", "bc", "bs", "gc", "gn")}
+        X = state[t]
+        xq, aq, cq, lq, eq, hq, st, rr, se, ra, rb = [
+            "%s%d" % (s, t) for s in ("xq", "aq", "cq", "lq", "eq", "hq", "st", "rr", "se", "ra", "rb")]
+        sem = {s: "%s%d" % (s, t) for s in LANDINGS}
 
         def scores(k):
             a, b = pieces[k]
             quant(xq, a, b, P(X, 4 * a, 4 * b))
-            mm((1, 3, 5)[k], b - a, "up", 0, xq, a)
-            mm((0, 4, 6)[k], b - a, "uq", 0, xq, a)
-            act(P("sq", a, b), ps((1, 3, 5)[k], 0, b - a))
+            mm(("edges", k), b - a, "up", 0, xq, a)
+            mm(("scores", k), b - a, "uq", 0, xq, a)
 
-        def strengths(j):
-            mm(2 + 2 * j, 256, "up", 128, xq, 256 * j)
+        def edges(k):
+            a, b = pieces[k]
+            act(P("sq", a, b), ps(("edges", k), 0, b - a))
+            drop(("edges", k))
 
-        def layer(j, b, bank, vector=False):
-            mm(bank, 256, "wq", 128 * b, xq, 256 * j)
-            out = P("ha", 1024 * j + b, 1024 * j + 1024, 4)
+        def strengths(k, done):
+            a, b = spans[k]
+            if done:
+                act(P("sp", a, b), ps(("strengths", k), 0, b - a), scale=SMALL)
+                drop(("strengths", k))
+            else:
+                mm(("strengths", k), b - a, "up", 128, xq, a)
+
+        def layer(k, e):
+            a, b = spans[k]
+            mm(("layer", k, e), b - a, "wq", 128 * e, xq, a)
+
+        def scaled(k, e, vector=False):
+            a, b = spans[k]
+            out, src = P("ha", 4 * a + e, 4 * b, 4), ps(("layer", k, e), 0, b - a)
             if vector:
-                ts(out, ps(bank, 0, 256), 0.03125, A.mult)
+                ts(out, src, 0.03125, A.mult)
             else:
-                act(out, ps(bank, 0, 256), scale=0.03125)
+                act(out, src, scale=0.03125)
+            drop(("layer", k, e))
 
-        def masked(j, h):
-            a, b = 256 * j, 256 * j + 256
-            tt(P(("sa", "sb")[h], a, b), ps(2 + 2 * j, 0, 256), P(("va", "vb")[h], a, b), A.add)
+        def maxima(k, h):
+            a, b = pieces[k][0], pieces[k][1] + k // 2
+            sa, run = P(("sa", "sb")[h], a, b), (ra, rb)[h]
+            scan(P(run, a, b), sa, sa, P(run, a - 1, a) if k else LOW, A.max, A.max)
+            if k == 2:
+                strongest(h)
 
-        def maxima(j, h):
-            a, b = 256 * j, 256 * j + 256
-            sa, run = P(("sa", "sb")[h], a, b + j), (ra, rb)[h]
-            scan(P(run, HEAD + a, HEAD + b + j), sa, sa, P(run, HEAD + a - 1, HEAD + a), A.max, A.max)
-            if j:
-                strongest(h, run)
-
-        def strongest(h, run):
-            top = P(run, end, end + 1)
-            beyond = [[(r, V(P((ra, rb)[k], end, end + 1)), T[se][:, 4 * o:4 * o + 1], sem["bs"]) for r in blocks[theirs]
-                       if (owner[r] >> 1 == o >> 1) == (k == 1)] for k in range(2)]
-            send([(r, V(top), T[st][:, 4 * o:4 * o + 1], sem["as"]) for r in (far, near)[h]] + beyond[1] * h, [top])
+        def strongest(h):
+            top = [P(run, 512, 513) for run in (ra, rb)]
+            send([(r, V(top[h]), T[st][:, 4 * o:4 * o + 1], sem["am"]) for r in (far, near)[h]]
+                 + [(r, V(top[pair.index(owner[r] >> 1)]), T[se][:, 4 * o:4 * o + 1], sem["bm"]) for r in blocks[theirs] if h],
+                 top[:h + 1])
             if h:
-                send(beyond[0], [P(ra, end, end + 1)])
-                land(sem["as"], from_mates, [P(st, 4 * owner[r], 4 * owner[r] + 1) for r in mates])
-                land(sem["bs"], 4 * share, [P(se, 0, 16, 4)])
+                land(sem["am"], from_mates, [P(st, 4 * owner[r], 4 * owner[r] + 1) for r in mates])
+                land(sem["bm"], len(outside), [P(se, 0, 16, 4)])
 
-        def every(h):
+        def counts(h):
             run = (ra, rb)[h]
-            below(count(h, 3), P(run, HEAD - 8, end), P(run, end, end + 1), P("junk", 520 * h, 520 * h + 520))
+            below(P("acc", 4 * h, 4 * h + 1), P(run, 15, 512, 32), P(run, 512, 513), P("junk", 544 * h, 544 * h + 16))
+            below(P("acc", 4 * h + 1, 4 * h + 2), P(run, 0, 512), P(run, 512, 513), P("junk", 544 * h + 32, 544 * h + 544))
 
-        def eighth(h):
-            run = (ra, rb)[h]
-            ts(P("e8", 72 * h, 72 * h + 72), P(run, 7, end, 8), P(run, end, end + 1), A.is_lt)
-
-        def sums(h, k):
-            src, out = P("e8", 72 * h + (7, 0, 7)[k], 72 * h + 72, (8, 1, 1)[k]), count(h, k)
-            do("v", lambda: g.vector.tensor_reduce(V(out), V(src), AxisListType.X, A.add), [src], [out])
-
-        def digits(h, k):
-            if k == 0:
-                act(digit(h, 0), P("m32", 32 * h, 32 * h + 32), scale=count(h, 0))
-            else:
-                act(digit(h, k), P("k32", 32 * h, 32 * h + 32), F.Relu, count(h, 2 * k - 2), count(h, 2 * k - 1))
+        def packed(k):
+            a, b = spans[k][0], spans[k][1] + 2 * (spans[k][1] // 512)
+            quant(aq, a, b, P("ha", 4 * a, 4 * b))
 
         def candidates(k):
             if k == 0:
-                pick(cq, 0, 128, aq, 514, "off", 0, 8)
+                pick(cq, 0, 112, aq, 514, "off", 0, 7)
             elif k == 1:
                 pick(cq, 128, 176, aq, 514, "off", 12 - 4 * (o & 1), 15 - 4 * (o & 1))
             else:
                 pick(lq, mine, mine + 48, aq, 514, "off", 8 + 4 * (o & 1), 11 + 4 * (o & 1))
 
         def hop1(k, to):
-            k, to = "cs"[k], (far, near)[to]
-            send([(r, side(cq + k, slot[r], slot[r] + 48), side(lq + k, mine, mine + 48), sem["ac" if k == "c" else "ad"]) for r in to],
-                 [P(cq + k, slot[r], slot[r] + 48) for r in to])
+            k = "cs"[k]
+            send([(r, side(cq + k, slot[r], slot[r] + 48), side(lq + k, mine, mine + 48), sem["a" + k]) for r in (far, near)[to]],
+                 [P(cq + k, slot[r], slot[r] + 48) for r in (far, near)[to]])
 
         def compare(k):
             if k == 0:
-                copy(P(st, 4 * o, 4 * o + 1), P(rb, end, end + 1))
+                copy(P(st, 4 * o, 4 * o + 1), P(rb, 512, 513))
             elif k == 1:
                 scan(P(rr, 0, 4), P(st, 0, 16, 4), P(st, 0, 16, 4), LOW, A.max, A.max)
             else:
@@ -551,100 +588,66 @@ def rank_program(g, core, T, topo):
         def swap():
             scan(Q("cm", 4, 8), Q(se, 0, 16, 4), Q(se, 0, 16, 4), LOW, A.max, A.max)
 
-        def meanwhile(k):
-            if t == 0:
-                (constants_wait, constants_hop, wishes)[k]()
-            elif k == 0:
-                wishes()
-            elif k == 1:
-                offsets(0)
-                act(P("f4", 3, 35, 4), P("dd", 24, 32))
-            else:
-                for b in range(2):
-                    quant("c4", 128 * b, 128 * b + 128, P("f4", 3 - b, 515 - b))
-
         def stronger():
-            pair = (Q(rr, 3, 4), Q("cm", 7, 8))
-            ts(Q("tr", 32, 33), pair[theirs], pair[block], A.is_gt)
+            both = (Q(rr, 3, 4), Q("cm", 7, 8))
+            ts(Q("tr", 32, 33), both[theirs], both[block], A.is_gt)
 
-        def hop2(k):
-            if k == 0:
-                for c, s in (("c", "ac"), ("s", "ad")):
-                    land(sem[s], from_mates, [P(lq + c, 64 * owner[r], 64 * owner[r] + 64) for r in mates])
-                pick(mq, 0, 48, lq, 256, "offm", 0, 3)
-                for c in "cs":
-                    send([(partner, side(mq + c, 0, 48), side(eq + c, 64 * block, 64 * block + 48), sem["bc"])], [P(mq + c, 0, 48)])
-                land(sem["bc"], 2 * len(outside), [P(eq + c, 64 * theirs, 64 * theirs + 48) for c in "cs"])
-            else:
-                pick(eq, 64 * block, 64 * block + 48, lq, 256, "offm", 0, 3)
+        def hop2():
+            a, b = 64 * block, 64 * block + 48
+            for k in "cs":
+                land(sem["a" + k], from_mates, [P(lq + k, 64 * owner[r], 64 * owner[r] + 64) for r in mates])
+            pick(eq, a, b, lq, 256, "offm", 0, 3)
+            for k in "cs":
+                send([(partner, side(eq + k, a, b), side(eq + k, a, b), sem["b" + k])], [P(eq + k, a, b)])
+                land(sem["b" + k], len(outside), [P(eq + k, 64 * theirs, 64 * theirs + 48)])
 
-        steps = {"s": lambda a, b: new_state(t - 1, 32 * a, 32 * b), "q": scores, "m": marks, "p": missing, "t": strengths,
-                 "h": layer, "v": lambda j, b, bank: layer(j, b, bank, True), "a": masked, "x": maxima,
-                 "u": lambda: pick("up", 128, 256, "uq", 128, "ulist", 8, 16), "z": lambda: act(P("zb", 520, 1040), P("zt", 0, 520)),
-                 "e": constants_early, "c": constants_mid, "y": constants_places, "w": constants_choices,
-                 "n": every, "l": eighth, "R": sums, "D": digits, "P": product, "F": places, "K": candidates, "H": hop1,
-                 "A": lambda j: quant(aq, 256 * j, 256 + 258 * j, P("ha", 1024 * j, 1024 + 1032 * j)),
-                 "C": compare, "T": turn, "B": spread, "E": swap, "W": meanwhile, "f": fold, "d": stronger, "M": hop2,
-                 "i": lambda: select(P("f6", 3, 515, 4), P("f6", 3, 515, 4), [[-1, 128]], A.not_equal, 1.0, 0, 1)}
-        for step in ORDER[min(t, 1)].split():
-            steps[step[0]](*[int(c, 17) for c in step[1:]])
-        pick(hq, 128, 176, eq, 128, "offe", 0, 3)
-        spot = {r: 128 + 48 * (o ^ owner[r]) for r in mates}
-        for k in "cs":
-            send([(r, side(hq + k, 128, 176), side(hq + k, spot[r], spot[r] + 48), sem["gn" if r in near else "gc"]) for r in mates],
-                 [P(hq + k, 128, 176)])
-        land(sem["gn"], 2 * len(inside), [P(hq + k, 176, 224) for k in "cs"])
-        land(sem["gc"], 2 * len(outside), [P(hq + k, 224, 320) for k in "cs"])
-        if t == 0:
-            constants_last()
-            offsets(0)
+        def hop3():
+            pick(hq, 128, 176, eq, 128, "offe", 0, 3)
+            spot = {r: 128 + 48 * (o ^ owner[r]) for r in mates}
+            for k in "cs":
+                send([(r, side(hq + k, 128, 176), side(hq + k, spot[r], spot[r] + 48), sem["gn" if r in near else "gc"]) for r in mates],
+                     [P(hq + k, 128, 176)])
+            land(sem["gn"], 2 * len(inside), [P(hq + k, 176, 224) for k in "cs"])
+            land(sem["gc"], 2 * len(outside), [P(hq + k, 224, 320) for k in "cs"])
+
+        def unpack(j):
             for b in range(4):
-                quant("c6", 128 * b, 128 * b + 128, P("f6", 3 - b, 515 - b))
-        fillers = [lambda b=b: quant("c4", 128 * b, 128 * b + 128, P("f4", 3 - b, 515 - b)) for b in range(2, 4)] if last else [
-            lambda: quant("hq1", 0, 128, P("zt", 0, 512)), lambda: quant("vq", 0, 128, P("vt", 0, 512))]
-        offsets(1)
-        fillers[0]()
-        offsets(2)
-        fillers[1]()
-        offsets(3)
-        if last:
-            for b in range(4):
-                mm(4 + b, 128, "c4", 128 * b, "nq", 0)
-        else:
-            for r in ("ra1", "rb1"):
-                fill(P(r, 0, HEAD), LOW)
-        offsets(4)
-        if last:
-            for b in range(4):
-                ts(P("wo", b, 512, 4, 0, 8), ps(4 + b, 0, 128, 8), -1.0, A.mult, 255.0, A.add)
-            dma("y", T.wl[:, 0:512], T.wo[0:8, 0:512], "done", 0, [P("wo", 0, 512)], [])
-        for j in range(2):
-            for b in range(4):
-                mm(4 * j + b, 128, "c6", 128 * b, hq, 96 + 96 * j)
+                mm(("table", b), 128, "c6", 128 * b, hq, 96 + 96 * j)
             for b in range(4):
                 for k in range(2):
                     at = 256 * (o ^ (2 * j + k)) + b
-                    (copy if j and b % 2 else act)(P("yt", at, at + 192, 4), ps(4 * j + b, 32 + 48 * k, 80 + 48 * k))
+                    (copy if j and b % 2 else act)(P("yt", at, at + 192, 4), ps(("table", b), 32 + 48 * k, 80 + 48 * k))
+                drop(("table", b))
+
+        steps = {"s": lambda a, b: new_state(t - 1, 32 * a, 32 * b), "q": scores, "m": marks, "t": strengths, "h": layer,
+                 "p": lambda k: quant("pq", 128 * k, 128 * k + 128, P("wm", 512 * min(k, 1), 512 * min(k, 1) + 512)),
+                 "e": edges, "N": missing, "a": masked, "x": maxima, "u": columns_of_u, "z": blanks, "b": bits, "r": rows,
+                 "j": pairs, "l": slots, "i": units, "w": weights, "c": tiles, "y": scaled, "v": lambda k, e: scaled(k, e, True),
+                 "n": counts, "D": digits, "P": product, "F": places, "K": candidates, "H": hop1, "A": packed, "C": compare,
+                 "T": turn, "W": wishes, "f": fold, "E": swap, "d": stronger, "M": hop2, "G": hop3, "O": offsets, "L": numbers, "U": unpack}
+        for step in ORDER[min(t, 1)].split():
+            steps[step[0]](*[int(c, 17) for c in step[1:]])
 
     def scales(q, k):
         dma(q, T.osc[4 * k:4 * k + 4, 0:512], T.xq2s[32 * k:32 * k + 4, 0:512], "done", 0, [P("xq2s", 0, 512)], [])
 
-    def results(k):
-        a, b = pieces[k]
+    def results(a, b):
         quant("xq2", a, b, P(state[ROUNDS], 4 * a, 4 * b))
-        mm(k, b - a, "vq", 0, "xq2", a)
-        act(P("yo", a, b), ps(k, 0, b - a))
+        mm("results", b - a, "vq", 0, "xq2", a)
         dma("y", T.oc[:, 4 * a:4 * b], side("xq2c", a, b), "done", 0, [P("xq2c", a, b)], [])
         if b == 512:
             for j in range(4):
-                scales("y", j)
+                scales("ys"[j // 2], j)
+        act(P("yo", a, b), ps("results", 0, b - a))
+        drop("results")
         dma("s", T.y[:, a:b], V(P("yo", a, b)), "done", 0, [P("yo", a, b)], [])
 
     for step in TAIL.split():
+        a, b = [32 * int(c, 17) for c in step[1:]]
         if step[0] == "s":
-            new_state(ROUNDS - 1, 32 * int(step[1], 17), 32 * int(step[2], 17))
+            new_state(ROUNDS - 1, a, b)
         else:
-            results(int(step[1]))
+            results(a, b)
     for s in total:
         if waited.get(s, 0) < total[s]:
             g.wait_ge(T.sem[s], total[s])

@@ -13,15 +13,17 @@ NONE = -2.0 ** 29
 LOW = -2.0 ** 40
 ROUNDS = 2
 BANKS = 8
-ORDER = ("b2 z0 b0 b4 b3 u0 z3 z4 b5 z2 r5 u1 r1 b6 r2 b1 j4 j5 z1 b7 c0 r0 zb u2 b8 b9 r4 u3 bb ba i0 u4 r3 q0 l0 u5 w5 q1 w0 r9 e0 l2 "
-         "bd t00 q2 c1 bc e1 l1 t10 j0 m0 m1 z5 l3 t01 r6 r8 p0 h00 w1 t20 w6 j2 r7 p1 w2 e2 y00 t11 w7 N00 w3 N10 ra m2 h30 a00 p2 t21 "
-         "a10 z8 j3 x00 z7 N01 N11 la N20 j1 w4 a01 j8 w8 x10 y30 c2 a20 h01 h31 a11 j6 N21 x20 y01 x01 h33 a21 w9 l4 y31 n0 h02 x11 i2 "
-         "D00 h03 y03 j7 l6 D01 x21 v33 C0 h32 y02 v32 n1 P0 wa A3 D10 D11 A0 wb F0 l7 i9 P1 K0 l5 l8 wc wd H00 H10 F1 C1 C2 K1 H01 H11 "
-         "K2 l9 T0 i7 f00 E we i1 c6 f01 c3 d i3 f02 i4 ia M T1 i6 f10 c5 c4 i5 f11 f12 i8 z6 c7 W0 c8 G W1 O0 O1 U0 O2 O3 U1",
-         "s08 q0 s8c t00 e0 h01 h00 h03 h02 scg t01 q1 m0 t10 y00 y01 q2 p0 e1 t11 m1 e2 p1 N00 t20 a00 m2 L0 h33 t21 N10 a10 p2 x00 "
-         "N01 y33 h32 y03 N11 y02 N20 h31 a01 x10 y32 y31 a20 a11 h30 y30 x20 x01 N21 n0 a21 x11 D00 x21 D01 C0 z9 n1 P0 D10 A0 A3 F0 "
-         "D11 P1 K0 H00 H10 F1 C1 C2 K1 H01 H11 K2 T0 L1 f00 za W1 f01 E W0 L2 f02 d M T1 f10 O0 f11 L3 f12 G O1 O2 O3 L4 U0 L5 U1")
-TAIL = "s8c s08 r8c r08 scg rcg"
+ORDER = ("b2 z0 b4 u0 b3 j5 b5 r1 r5 z4 z8 z3 z2 b6 zb j4 b0 b1 u1 b7 r2 b8 c1 u2 z1 b9 r4 u3 ba bb u4 i0 c0 j1 q0 u5 q1 bc e0 c2 e1 r0 "
+         "t40 q2 j2 bd m0 w5 m1 w6 q3 l3 r3 p0 e2 w7 N00 l1 t41 e3 m2 t50 p1 w0 w1 j0 N10 t51 r7 p2 z5 w2 N11 N20 a00 r9 N01 j3 m3 h40 a10 "
+         "x00 h50 la w8 p3 N30 y40 a20 x10 h51 a01 r6 y50 j8 y51 h41 x20 N31 w3 a30 w9 x01 wa j6 x30 N21 h42 a11 l0 l2 a31 a21 x11 y41 n0 "
+         "w4 wb r8 D00 h53 y42 j7 x21 v53 h52 h43 x31 wc ra C0 D01 y43 n1 P0 v52 D10 A4 D11 A5 F0 i2 l7 P1 wd K0 l4 c4 H00 H10 l8 l6 F1 C1 "
+         "C2 K1 K2 l5 l9 H01 H11 T0 i1 f00 E z7 we i3 f01 i7 c6 f02 i4 d M T1 c3 i6 f10 i5 f11 c5 f12 z6 W0 ia G W1 i8 c7 c8 i9 O0 O1 U0 "
+         "O2 O3 U1",
+         "g24 s46 s02 g68 o24 o68 q0 gac s8a geg q1 oac t40 e0 sce h43 q2 h40 e1 m0 oeg p0 t41 N00 L0 q3 m1 e2 t50 y40 m2 e3 p1 a00 p2 x00 "
+         "m3 N10 N01 N20 t51 a10 a01 N21 p3 x10 y43 h41 a20 h42 x01 N30 N11 h52 a21 N31 h53 h50 x20 y41 a30 a11 x30 y42 x11 a31 x21 y52 "
+         "v53 h51 n0 D00 x31 v50 D01 v51 P0 n1 D10 C0 D11 A4 A5 F0 P1 K0 H00 H10 C1 F1 C2 K1 H01 H11 T0 K2 E f00 W0 L1 d L2 f01 T1 f02 W1 "
+         "M f10 f11 O0 f12 L3 za O1 G z9 L4 O2 L5 O3 U0 U1")
+TAIL = "s04 s8a g48 gac gcg o48 r04 oac r48 r8c v04 ocg v48 rcg v8c ycg"
 
 SCRATCH = {}
 PLACES = {}
@@ -46,7 +48,7 @@ def _parts(name, dtype, *parts):
 
 for _k in range(BANKS):
     SCRATCH["ps%d" % _k] = ("psum", [128, 512], "float32")
-for _n, _c in (("xa", 2048), ("xb", 2048), ("xc", 2048), ("ut", 512), ("vt", 512), ("wm", 1024), ("nd", 512), ("junk", 1088),
+for _n, _c in (("xa", 2048), ("xb", 2048), ("xc", 2048), ("yg", 2048), ("ut", 512), ("vt", 512), ("wm", 1024), ("nd", 512), ("junk", 1088),
                ("yt", 1040), ("ha", 2056), ("f1", 1032), ("f2", 520), ("f3", 512), ("f4", 608), ("f5", 512), ("f6", 520), ("f7", 512)):
     _sb(_n, _c, "bfloat16")
 _parts("zb", "bfloat16", ("digits", 128), ("zt", 520))
@@ -61,7 +63,7 @@ _parts("lists", "int32", ("la", 128), ("lb", 128))
 for _n, _c in (("ulist", 16), ("glist", 8), ("off", 16), ("offs", 128), ("offm", 4), ("offe", 4)):
     _sb(_n, _c, "uint16")
 for _n, _c in (("uq", 128), ("up", 256), ("vq", 128), ("wq", 512), ("c1", 512), ("c2", 256), ("c3", 256), ("c4", 152),
-               ("c5", 128), ("c6", 512), ("pq", 384), ("nq", 128), ("zq", 272), ("xq2", 512)):
+               ("c5", 128), ("c6", 512), ("pq", 512), ("nq", 128), ("zq", 272), ("xq2", 512)):
     _mx(_n, _c)
 for _t in range(ROUNDS):
     for _n, _c in (("xq", 512), ("aq", 544), ("cq", 192), ("lq", 256), ("eq", 128), ("hq", 320)):
@@ -70,7 +72,7 @@ for _t in range(ROUNDS):
     for _n, _c in (("st", 16), ("rr", 4), ("se", 16)):
         _sb("%s%d" % (_n, _t), _c, "float32")
 LANDINGS = ("am", "ac", "as", "bm", "bc", "bs", "gn", "gc")
-SEMAPHORES = ["nv", "ns", "nt", "ng", "lu", "lx0", "lx1", "lx2", "lw0", "lw1", "lv", "done", "left"] + [
+SEMAPHORES = ["nv", "ns", "nt", "ng", "lu", "lx0", "lx1", "lx2", "lx3", "lw0", "lw1", "lv", "done", "left"] + [
     "%s%d" % (a, t) for t in range(ROUNDS) for a in LANDINGS]
 
 
@@ -264,7 +266,7 @@ def rank_program(g, core, T, topo):
     def side(name, a, b):
         return T[name][:, a:b].bitcast(dt.uint8) if name[-1] == "c" else T[name][:, a:b]
 
-    pieces = ((0, 256), (256, 384), (384, 512))
+    pieces = tuple((a, a + 128) for a in range(0, 512, 128))
     dma("s", T.ut[:], T.u[:], "lu", 16, [], [P("ut", 0, 512)])
     for k, (a, b) in enumerate(pieces):
         dma("y", T.xa[:, 4 * a:4 * b], T.x[:, 4 * a:4 * b], "lx%d" % k, 16, [], [P("xa", 4 * a, 4 * b)])
@@ -297,7 +299,7 @@ def rank_program(g, core, T, topo):
          lambda: zero(P("yt", 1024, 1040)),
          lambda: quant("hq1", 0, 128, P("zt", 0, 512)),
          lambda: quant("vq", 0, 128, P("vt", 0, 512)),
-         lambda: fill(P("wm", 513, 1024, 4), 0.0))[k]()
+         lambda: fill(P("wm", 1, 1024, 4), 0.0))[k]()
 
     def bits(k):
         (lambda: zero(P("f1", 0, 516)),
@@ -405,28 +407,29 @@ def rank_program(g, core, T, topo):
     mine, theirs = 64 * o, 1 - block
     slot = {r: 64 * (owner[r] & 1) for r in far}
     slot[near[0]] = 128
-    runs = (((0, 0, 2), (1, 1, 2)), ((0, 256, 1),), ((1, 384, 1),))
-    spans = pieces + ((256, 512),)
+    spans = pieces + ((0, 256), (256, 512))
 
     def new_state(t, a, b):
         gather(P(state[t + 1], 4 * a, 4 * b), P("yt", 0, 1040), P("offs", a // 4, b // 4), P(state[t], 4 * a, 4 * b))
 
+    def looked_up(a, b):
+        y, i, out = P("yt", 0, 1040), P("offs", a // 4, b // 4), P("yg", 4 * a, 4 * b)
+        do("s", lambda: g.scalar.activation(V(out), V(y).indirect(V(i)), F.Copy), [y, i], [out])
+
+    def added(t, a, b):
+        tt(P(state[t + 1], 4 * a, 4 * b), P("yg", 4 * a, 4 * b), P(state[t], 4 * a, 4 * b), A.add)
+
     def marks(k):
-        for e, a, step in runs[k]:
-            at = 512 * min(k, 1)
-            tt(P("wm", at + e, at + 512, 4), ps(("scores", k), a - pieces[k][0], pieces[k][1] - pieces[k][0], step),
-               P("sq", a, pieces[k][1], step), A.is_le)
+        at = 512 * (k // 2)
+        tt(P("wm", at + k % 2, at + 512, 4), ps(("scores", k), 0, 128), P("sq", *pieces[k]), A.is_le)
         drop(("scores", k))
 
     def missing(k, h):
-        for e, a, step in runs[k]:
-            mm(("missing", a, h), 128, "c1", 256 * e + 128 * h, "pq", 128 * k)
+        mm(("missing", k, h), 128, "c1", 256 * (k % 2) + 128 * h, "pq", 128 * k)
 
     def masked(k, h):
-        for e, a, step in runs[k]:
-            b = pieces[k][1]
-            tt(P(("sa", "sb")[h], a, b, step), ps(("missing", a, h), 0, 128), P("sp", a, b, step), A.add)
-            drop(("missing", a, h))
+        tt(P(("sa", "sb")[h], *pieces[k]), ps(("missing", k, h), 0, 128), P("sp", *pieces[k]), A.add)
+        drop(("missing", k, h))
 
     def digits(h, k):
         c, n, less, more = [P("acc", 4 * h + i, 4 * h + i + 1) for i in range(4)]
@@ -463,9 +466,8 @@ def rank_program(g, core, T, topo):
 
     def wishes(j):
         for e in range(2):
-            a, step = (runs[0] + runs[1] + runs[2])[2 * j + e][1:]
-            mm("wishes", 128, "c2", 128 * e, "pq", 256 * j)
-            act(P("nd", a, a - a % step + 128 * step, step), ps("wishes", 0, 128), F.Sign)
+            mm("wishes", 128, "c2", 128 * e, "pq", 256 * j + 128)
+            act(P("nd", *pieces[2 * j + e]), ps("wishes", 0, 128), F.Sign)
             drop("wishes")
 
     def offsets(k):
@@ -540,10 +542,10 @@ def rank_program(g, core, T, topo):
             drop(("layer", k, e))
 
         def maxima(k, h):
-            a, b = pieces[k][0], pieces[k][1] + k // 2
+            a, b = pieces[k][0], pieces[k][1] + k // 3
             sa, run = P(("sa", "sb")[h], a, b), (ra, rb)[h]
             scan(P(run, a, b), sa, sa, P(run, a - 1, a) if k else LOW, A.max, A.max)
-            if k == 2:
+            if k == 3:
                 strongest(h)
 
         def strongest(h):
@@ -619,8 +621,9 @@ def rank_program(g, core, T, topo):
                     (copy if j and b % 2 else act)(P("yt", at, at + 192, 4), ps(("table", b), 32 + 48 * k, 80 + 48 * k))
                 drop(("table", b))
 
-        steps = {"s": lambda a, b: new_state(t - 1, 32 * a, 32 * b), "q": scores, "m": marks, "t": strengths, "h": layer,
-                 "p": lambda k: quant("pq", 128 * k, 128 * k + 128, P("wm", 512 * min(k, 1), 512 * min(k, 1) + 512)),
+        steps = {"s": lambda a, b: new_state(t - 1, 32 * a, 32 * b), "g": lambda a, b: looked_up(32 * a, 32 * b),
+                 "o": lambda a, b: added(t - 1, 32 * a, 32 * b), "q": scores, "m": marks, "t": strengths, "h": layer,
+                 "p": lambda k: quant("pq", 128 * k, 128 * k + 128, P("wm", 512 * (k // 2), 512 * (k // 2) + 512)),
                  "e": edges, "N": missing, "a": masked, "x": maxima, "u": columns_of_u, "z": blanks, "b": bits, "r": rows,
                  "j": pairs, "l": slots, "i": units, "w": weights, "c": tiles, "y": scaled, "v": lambda k, e: scaled(k, e, True),
                  "n": counts, "D": digits, "P": product, "F": places, "K": candidates, "H": hop1, "A": packed, "C": compare,
@@ -633,21 +636,21 @@ def rank_program(g, core, T, topo):
 
     def results(a, b):
         quant("xq2", a, b, P(state[ROUNDS], 4 * a, 4 * b))
-        mm("results", b - a, "vq", 0, "xq2", a)
+        mm(("results", a), b - a, "vq", 0, "xq2", a)
         dma("y", T.oc[:, 4 * a:4 * b], side("xq2c", a, b), "done", 0, [P("xq2c", a, b)], [])
         if b == 512:
             for j in range(4):
                 scales("ys"[j // 2], j)
-        act(P("yo", a, b), ps("results", 0, b - a))
-        drop("results")
-        dma("s", T.y[:, a:b], V(P("yo", a, b)), "done", 0, [P("yo", a, b)], [])
+
+    def products(a, b, vector=False):
+        (copy if vector else act)(P("yo", a, b), ps(("results", a), 0, b - a))
+        drop(("results", a))
+        dma("y" if vector else "s", T.y[:, a:b], V(P("yo", a, b)), "done", 0, [P("yo", a, b)], [])
 
     for step in TAIL.split():
         a, b = [32 * int(c, 17) for c in step[1:]]
-        if step[0] == "s":
-            new_state(ROUNDS - 1, a, b)
-        else:
-            results(a, b)
+        {"s": lambda: new_state(ROUNDS - 1, a, b), "g": lambda: looked_up(a, b), "o": lambda: added(ROUNDS - 1, a, b),
+         "r": lambda: results(a, b), "y": lambda: products(a, b), "v": lambda: products(a, b, True)}[step[0]]()
     for s in total:
         if waited.get(s, 0) < total[s]:
             g.wait_ge(T.sem[s], total[s])

import math
from concourse.bass import DstId, RemoteDMATransfer
from concourse.mybir import dt, AluOpType, ActivationFunctionType
from concourse.mybir import AxisListType
import comms_topo

A = AluOpType
F = ActivationFunctionType
CODE = "float8_e4m3fn_x4"
SMALL = 2.0 ** -42
MISS = -2.0 ** 30
NONE = -2.0 ** 29
LOW = -2.0 ** 40
ROUNDS = 2
BANKS = 8
ORDER = ("b2 z0 b4 u0 b3 j5 b5 r1 r5 z4 z8 z3 z2 b6 zb j4 b0 b1 u1 b7 r2 b8 c1 u2 z1 b9 r4 u3 ba bb u4 i0 c0 j1 q0 u5 q1 bc e0 c2 e1 r0 "
         "t40 q2 j2 bd m0 w5 m1 w6 q3 l3 r3 p0 e2 w7 N00 l1 t41 e3 m2 t50 p1 w0 w1 j0 N10 t51 r7 p2 z5 w2 N11 N20 a00 r9 N01 j3 m3 h40 a10 "
         "x00 h50 la w8 p3 N30 y40 a20 x10 h51 a01 r6 y50 j8 y51 h41 x20 N31 w3 a30 w9 x01 wa j6 x30 N21 h42 a11 l0 l2 a31 a21 x11 y41 n0 "
         "w4 wb r8 D00 h53 y42 j7 x21 v53 h52 h43 x31 wc ra C0 D01 y43 n1 P0 v52 D10 A4 D11 A5 F0 i2 l7 P1 wd K0 l4 c4 H00 H10 l8 l6 F1 C1 "
         "C2 K1 K2 l5 l9 H01 H11 T0 i1 f00 E z7 we i3 f01 i7 c6 f02 i4 d M T1 c3 i6 f10 i5 f11 c5 f12 z6 W0 ia G W1 i8 c7 c8 i9 O0 O1 U0 "
         "O2 O3 U1",
         "g24 s46 s02 g68 o24 o68 q0 gac s8a geg q1 oac t40 e0 sce h43 q2 h40 e1 m0 oeg p0 t41 N00 L0 q3 m1 e2 t50 y40 m2 e3 p1 a00 p2 x00 "
         "m3 N10 N01 N20 t51 a10 a01 N21 p3 x10 y43 h41 a20 h42 x01 N30 N11 h52 a21 N31 h53 h50 x20 y41 a30 a11 x30 y42 x11 a31 x21 y52 "
         "v53 h51 n0 D00 x31 v50 D01 v51 P0 n1 D10 C0 D11 A4 A5 F0 P1 K0 H00 H10 C1 F1 C2 K1 H01 H11 T0 K2 E f00 W0 L1 d L2 f01 T1 f02 W1 "
         "M f10 f11 O0 f12 L3 za O1 G z9 L4 O2 L5 O3 U0 U1")
TAIL = "s04 s8a g48 gac gcg o48 r04 oac r48 r8c v04 ocg v48 rcg v8c ycg"

SCRATCH = {}
PLACES = {}


def _sb(name, cols, dtype):
    SCRATCH[name] = ("sbuf", [128, cols], dtype)


def _mx(name, cols):
    _sb(name + "c", cols, CODE)
    _sb(name + "s", cols, "uint8")


def _parts(name, dtype, *parts):
    at = 0
    for n, c in parts:
        PLACES[n] = (name, at)
        at += c
    _sb(name, at, dtype)


for _k in range(BANKS):
    SCRATCH["ps%d" % _k] = ("psum", [128, 512], "float32")
for _n, _c in (("xa", 2048), ("xb", 2048), ("xc", 2048), ("yg", 2048), ("ut", 512), ("vt", 512), ("wm", 1024), ("nd", 512), ("junk", 1088),
               ("yt", 1040), ("ha", 2056), ("f1", 1032), ("f2", 520), ("f3", 512), ("f4", 608), ("f5", 512), ("f6", 520), ("f7", 512)):
    _sb(_n, _c, "bfloat16")
_parts("zb", "bfloat16", ("digits", 128), ("zt", 520))
for _n, _c in (("sq", 512), ("sp", 512), ("acc", 8), ("yo", 512), ("wo", 512), ("bc", 128)):
    _sb(_n, _c, "float32")
_parts("work", "float32", ("sa", 520), ("sb", 520))
_parts("fixed", "float32", ("m1", 64), ("pm", 8), ("dd", 24), ("im", 128), ("uf", 16), ("pw", 16), ("gd", 8), ("cols", 8),
       ("pat", 64), ("jq", 96))
_parts("choose", "float32", ("cm", 8), ("tr", 64), ("slots", 96), ("fold", 96))
_parts("whole", "int32", ("bi", 128), ("bj", 128), ("ci", 128), ("cj", 128), ("mi", 64), ("mj", 64), ("gl", 24))
_parts("lists", "int32", ("la", 128), ("lb", 128))
for _n, _c in (("ulist", 16), ("glist", 8), ("off", 16), ("offs", 128), ("offm", 4), ("offe", 4)):
    _sb(_n, _c, "uint16")
for _n, _c in (("uq", 128), ("up", 256), ("vq", 128), ("wq", 512), ("c1", 512), ("c2", 256), ("c3", 256), ("c4", 152),
               ("c5", 128), ("c6", 512), ("pq", 512), ("nq", 128), ("zq", 272), ("xq2", 512)):
    _mx(_n, _c)
for _t in range(ROUNDS):
    for _n, _c in (("xq", 512), ("aq", 544), ("cq", 192), ("lq", 256), ("eq", 128), ("hq", 320)):
        _mx("%s%d" % (_n, _t), _c)
    _parts("run%d" % _t, "float32", ("ra%d" % _t, 520), ("rb%d" % _t, 520))
    for _n, _c in (("st", 16), ("rr", 4), ("se", 16)):
        _sb("%s%d" % (_n, _t), _c, "float32")
LANDINGS = ("am", "ac", "as", "bm", "bc", "bs", "gn", "gc")
SEMAPHORES = ["nv", "ns", "nt", "ng", "lu", "lx0", "lx1", "lx2", "lx3", "lw0", "lw1", "lv", "done", "left"] + [
    "%s%d" % (a, t) for t in range(ROUNDS) for a in LANDINGS]


def rank_program(g, core, T, topo):
    rank = T.rank_of(core)
    if rank is None:
        return
    blocks = [[0, 1, 2, 3], [4, 5, 6, 7]]
    owner = {r: b.index(r) for b in blocks for r in b}
    o, block = owner[rank], int(rank in blocks[1])
    partner = blocks[1 - block][o]
    queue = {"v": g.vector, "s": g.scalar, "t": g.tensor, "g": g, "y": g.sync}
    counter = {"v": "nv", "s": "ns", "t": "nt", "g": "ng"}
    span = [set()]
    banks, free = {}, list(range(BANKS))
    total, known, snaps, seen, waited = {}, {q: {} for q in queue}, {}, {}, {}

    def P(name, a, b, step=1, r0=0, r1=128):
        name, at = PLACES.get(name, (name, 0))
        return (name, at + a, at + b, step, r0, r1)

    def Q(name, a, b, step=1):
        return P(name, a, b, step, 64 * (o & 1), 64 * (o & 1) + 64)

    def V(p):
        rows = slice(None) if (p[4], p[5]) == (0, 128) else slice(p[4], p[5])
        return T[p[0]][rows, p[1]:p[2]:p[3]] if p[3] > 1 else T[p[0]][rows, p[1]:p[2]]

    def meet(a, b):
        if max(a[4], b[4]) >= min(a[5], b[5]) or max(a[1], b[1]) >= min(a[2], b[2]):
            return False
        step = math.gcd(*[0 if p[2] - p[1] == 1 else p[3] for p in (a, b)])
        return step == 0 or (a[1] - b[1]) % step == 0

    def conflicts(q, reads, writes):
        out = {}
        for p, w in [(p, False) for p in reads] + [(p, True) for p in writes]:
            bank = p[0][:2] == "ps"
            for p2, w2, q2, tok in seen.get(p[0], []):
                if bank:
                    if q2 == q and not (w or w2):
                        continue
                else:
                    if not (w or w2) or not meet(p, p2):
                        continue
                out[tok[0]] = max(out.get(tok[0], 0), tok[1])
        return out

    def wait(q, deps):
        deps = {s: n for s, n in deps.items() if known[q].get(s, 0) < n}
        keep = [s for s in deps if not any(e != s and snaps.get((e, deps[e]), {}).get(s, 0) >= deps[s] for e in deps)]
        for s in keep:
            queue[q].wait_ge(T.sem[s], deps[s])
            waited[s] = max(waited.get(s, 0), deps[s])
            for e, n in [(s, deps[s])] + list(snaps.get((s, deps[s]), {}).items()):
                known[q][e] = max(known[q].get(e, 0), n)

    def note(q, reads, writes, tok):
        for p in reads:
            seen.setdefault(p[0], []).append((p, False, q, tok))
        for p in writes:
            seen.setdefault(p[0], []).append((p, True, q, tok))

    def do(q, call, reads, writes, alike=False):
        s = counter[q]
        deps = conflicts(q, reads, writes)
        if q == "t" and alike:
            deps.pop(s)
        wait(q, deps)
        if q == "g":
            rows = {p[4:6] for p in reads + writes}
            if total.get(s) and rows | span[0] != {(0, 128)} and not alike:
                wait(q, {s: total[s]})
            span[0] = rows
        total[s] = total.get(s, 0) + 1
        call().then_inc(T.sem[s], 1)
        snaps[(s, total[s])] = dict(known[q])
        note(q, reads, writes, (s, total[s]))

    def dma(q, out, src, s, full, reads, writes):
        wait(q, conflicts("dma", reads, []))
        total[s] = total.get(s, 0) + 16
        queue[q].dma_start(out, src).then_inc(T.sem[s], 16)
        note("dma", reads, writes, (s, full))

    def fill(p, c):
        do("v", lambda: g.vector.memset(V(p), c), [], [p])

    def tt(out, a, b, op):
        do("v", lambda: g.vector.tensor_tensor(V(out), V(a), V(b), op), [a, b], [out])

    def ts(out, a, s1, op0, s2=None, op1=None):
        sc = [s for s in (s1, s2) if isinstance(s, tuple)]
        x1, x2 = [V(s) if isinstance(s, tuple) else s for s in (s1, s2)]
        if op1 is None:
            do("v", lambda: g.vector.tensor_scalar(V(out), V(a), x1, None, op0), [a] + sc, [out])
        else:
            do("v", lambda: g.vector.tensor_scalar(V(out), V(a), x1, x2, op0, op1), [a] + sc, [out])

    def copy(out, a):
        do("v", lambda: g.vector.tensor_copy(V(out), V(a)), [a], [out])

    def scan(out, d0, d1, initial, op0, op1):
        held = isinstance(initial, tuple)
        do("v", lambda: g.vector.tensor_tensor_scan(V(out), V(d0), V(d1), V(initial) if held else initial, op0, op1),
           [d0, d1] + [initial] * held, [out])

    def flip(out, src):
        do("v", lambda: g.vector.transpose(V(out), V(src)), [src], [out])

    def gather(out, win, lst, other):
        do("v", lambda: g.vector.tensor_tensor(V(out), V(win).indirect(V(lst)), V(other), A.add), [win, lst, other], [out])

    def act(out, a, func=F.Copy, scale=None, bias=None):
        more = {k: x for k, x in (("scale", scale), ("bias", bias)) if x is not None}
        do("s", lambda: g.scalar.activation(V(out), V(a), func, **{k: V(x) if isinstance(x, tuple) else x for k, x in more.items()}),
           [a] + [x for x in more.values() if isinstance(x, tuple)], [out])

    def zero(p):
        act(p, P("zt", 0, len(range(*p[1:4])), 1, p[4], p[5]))

    def below(out, src, end, junk):
        do("s", lambda: g.scalar.activation(V(junk), V(src), F.Sign, bias=V(end), scale=-1.0, accum_out=V(out)),
           [src, end], [junk, out])

    def quant(q, a, b, src):
        do("v", lambda: g.vector.quantize_mx(T[q + "c"][:, a:b], T[q + "s"][:, a:b], V(src)), [src],
           [P(q + "c", a, b), P(q + "s", a, b)])

    def mm(name, n, w, wa, x, xa, start=True, stop=True):
        if start:
            banks[name] = free.pop(0)
        bank = banks[name]
        do("t", lambda: g.tensor.matmul_mx(T["ps%d" % bank][:, 0:n], T[w + "c"][:, wa:wa + 128], T[w + "s"][:, wa:wa + 128],
                                           T[x + "c"][:, xa:xa + n], T[x + "s"][:, xa:xa + n], start, stop),
           [P(w + "c", wa, wa + 128), P(w + "s", wa, wa + 128), P(x + "c", xa, xa + n), P(x + "s", xa, xa + n)],
           [P("ps%d" % bank, 0, n)], not start)

    def pick(out, c, d, win, b, lst, e, f):
        i = P(lst, e, f)
        do("v", lambda: g.vector.tensor_copy(T[out + "c"][:, c:d].bitcast(dt.uint32),
                                             T[win + "c"][:, 0:b].bitcast(dt.uint32).indirect(V(i))),
           [P(win + "c", 0, b), i], [P(out + "c", c, d)])
        do("s", lambda: g.scalar.activation(T[out + "s"][:, c:d], T[win + "s"][:, 0:b].indirect(V(i)), F.Copy),
           [P(win + "s", 0, b), i], [P(out + "s", c, d)])

    def ps(name, a, b, step=1, r1=128):
        return P("ps%d" % banks[name], a, b, step, 0, r1)

    def drop(name):
        free.append(banks.pop(name))

    def iota(p, pattern, base, ch, f=False):
        if f:
            do("g", lambda: g.iota(V(p), pattern, base, ch, allow_small_or_imprecise_dtypes=True), [], [p])
        else:
            do("g", lambda: g.iota(V(p), pattern, base, ch), [], [p])

    def select(out, src, pattern, op, value, base, ch):
        do("g", lambda: g.affine_select(V(out), V(src), pattern, op, value, base, ch), [src], [out])

    def address(r):
        rid, pid = topo.addr(T.cores[r])[:2]
        return DstId(rid=rid, pnc=pid)

    def bitmask(engines):
        return sum(1 << e for e in engines)

    mates = [r for r in blocks[block] if r != rank]
    far = [r for r in mates if topo.chip(T.cores[r]) != topo.chip(core)]
    near = [r for r in mates if r not in far]
    assert [owner[r] for r in near] == [o ^ 1]
    outside = topo.engines(core, T.cores[far[0]])
    inside = [e for e in topo.engines(core, T.cores[near[0]]) if e not in outside]
    assert all(topo.engines(core, T.cores[r]) == outside for r in far + blocks[1 - block])
    from_mates = len(outside) + len(inside)

    def send(moves, reads):
        wait("g", conflicts("g", reads, []))
        away = [m[0] for m in moves if m[0] not in near]
        n = len(outside) // max(len(away), 1)
        engines = {r: inside if r in near else outside[n * away.index(r):n * away.index(r) + n] for r, a, b, s in moves}
        g.remote_dma_fused([RemoteDMATransfer(dst_ids=[address(r)], dma_engine_mask=bitmask(engines[r]), remote_sem=T.sem[s], src=a, dst=b)
                            for r, a, b, s in moves], local_sem=T.sem.left)
        total["left"] = total.get("left", 0) + sum(len(e) for e in engines.values())

    def land(s, n, places):
        total[s] = n
        note("remote", [], places, (s, n))

    def side(name, a, b):
        return T[name][:, a:b].bitcast(dt.uint8) if name[-1] == "c" else T[name][:, a:b]

    pieces = tuple((a, a + 128) for a in range(0, 512, 128))
    dma("s", T.ut[:], T.u[:], "lu", 16, [], [P("ut", 0, 512)])
    for k, (a, b) in enumerate(pieces):
        dma("y", T.xa[:, 4 * a:4 * b], T.x[:, 4 * a:4 * b], "lx%d" % k, 16, [], [P("xa", 4 * a, 4 * b)])
    dma("y", T.wqs[:], T.ws[:], "lw0", 32, [], [P("wqs", 0, 512)])
    dma("y", side("wqc", 0, 256), T.wc[:, 0:1024], "lw0", 32, [], [P("wqc", 0, 256)])
    dma("y", side("wqc", 256, 512), T.wc[:, 1024:2048], "lw1", 16, [], [P("wqc", 256, 512)])
    wait("y", {"lw1": 16})
    dma("y", T.vt[:], T.v[:], "lv", 16, [], [P("vt", 0, 512)])

    pair = (1 - (o >> 1), o >> 1)
    shift, seventh, half, place, element, mixed = [P("cols", k, k + 1) for k in range(6)]

    def columns_of_u(k):
        (lambda: iota(P("uf", 0, 16), [[16, 16]], 1, 0, True),
         lambda: select(P("uf", 0, 16), P("uf", 0, 16), [[-1, 16]], A.is_ge, 15.0, 7, 0),
         lambda: copy(P("ulist", 0, 16), P("uf", 0, 16)),
         lambda: quant("uq", 0, 128, P("ut", 0, 512)),
         lambda: pick("up", 0, 128, "uq", 128, "ulist", 0, 8),
         lambda: pick("up", 128, 256, "uq", 128, "ulist", 8, 16))[k]()

    def blanks(k):
        (lambda: fill(P("zt", 0, 520), 0.0),
         lambda: fill(P("work", 512, 1040, 520), NONE),
         lambda: fill(P("wm", 2, 1024, 4), 0.0),
         lambda: fill(P("wm", 3, 1024, 4), 0.0),
         lambda: fill(P("ha", 2048, 2056), 0.0),
         lambda: zero(Q("tr", 0, 64)),
         lambda: quant("hq0", 0, 128, P("zt", 0, 512)),
         lambda: [zero(P("yt", 256 * w + 192, 256 * w + 256)) for w in range(4)],
         lambda: zero(P("yt", 1024, 1040)),
         lambda: quant("hq1", 0, 128, P("zt", 0, 512)),
         lambda: quant("vq", 0, 128, P("vt", 0, 512)),
         lambda: fill(P("wm", 1, 1024, 4), 0.0))[k]()

    def bits(k):
        (lambda: zero(P("f1", 0, 516)),
         lambda: zero(P("f1", 516, 1032)),
         lambda: fill(P("pw", 0, 8), 0.5),
         lambda: scan(P("pw", 8, 16), P("pw", 0, 8), P("pw", 0, 8), 16384.0, A.mult, A.max),
         lambda: iota(P("im", 0, 128), [[64, 2], [-48, 4], [1, 16]], 256, 0, True),
         lambda: select(P("gd", 0, 8), P("pw", 8, 16), [[-16, 8]], A.is_equal, 0.0, 0, 1),
         lambda: do("v", lambda: g.vector.tensor_reduce(V(shift), V(P("gd", 0, 8)), AxisListType.X, A.add), [P("gd", 0, 8)], [shift]),
         lambda: ts(P("bi", 0, 128), P("im", 0, 128), shift, A.mult),
         lambda: ts(seventh, shift, 64.0, A.is_equal, 8192.0, A.mult),
         lambda: ts(P("bj", 0, 128), P("bi", 0, 128), 8192, A.bitwise_and),
         lambda: ts(P("f1", 3 + 512 * pair[0], 515 + 512 * pair[0], 4), P("bj", 0, 128), 0.0, A.not_equal, MISS, A.mult),
         lambda: ts(P("f1", 3 + 512 * pair[1], 515 + 512 * pair[1], 4), P("bj", 0, 128), seventh, A.not_equal, MISS, A.mult),
         lambda: quant("c1", 0, 256, P("f1", 3, 1027)),
         lambda: quant("c1", 256, 512, P("f1", 2, 1026)))[k]()

    def rows(k):
        if k < 3:
            a, b, pattern, step = ((0, 32, [[0, 2], [-16, 4], [-1, 4]], 1), (32, 64, [[0, 2], [-4, 16]], 1), (64, 128, [[0, 4], [-4, 16]], 4))[k]
            iota(P("ci", a, b), pattern, 64, step)
        elif k < 5:
            a, b, mask = ((0, 32, 51), (32, 128, 60))[k - 3]
            ts(P("cj", a, b), P("ci", a, b), mask, A.bitwise_and)
        elif k == 5:
            fill(P("f5", 0, 512), 0.0)
        elif k < 10:
            a, at = k - 6, (32, 0, 64, 96)[k - 6]
            ts(P("f5", 129 * a, 128 * a + 128, 4), P("cj", at, at + 32), 0.0, A.is_equal)
        else:
            quant("c5", 0, 128, P("f5", 0, 512))

    def pairs(k):
        if k < 3:
            iota(P("mi", k, 64, 4), [[0, 2], [4096, 2], [-16, 4]], 48, 16 >> 2 * k)
        elif k == 3:
            iota(P("mi", 3, 64, 4), [[32 * (pair[1] - pair[0]), 2], [4112, 2], [-16, 4]], 255 + 32 * pair[0], -1)
        elif k < 6:
            fill(P("cols", 2, 3, 1, 64 * k - 256, 64 * k - 192), 4096.0 * (k - 4))
        elif k == 6:
            ts(P("mj", 0, 64), P("mi", 0, 64), 4096 + 48, A.bitwise_and)
        elif k == 7:
            ts(P("m1", 0, 64), P("mj", 0, 64), half, A.is_equal)
        else:
            iota(P("pm", 0, 2), [[64, 2]], -32, 0, True)

    def slots(k):
        (lambda: iota(P("gl", 6, 12), [[4, 3], [0, 2]], 4, 0),
         lambda: iota(P("gl", 0, 6), [[1, 3], [0, 2]], 1, 4),
         lambda: iota(P("gl", 12, 18), [[16, 3], [0, 2]], 16, 1),
         lambda: iota(P("gl", 18, 24), [[-16, 3], [0, 2]], 16 * (o + 3), 1),
         lambda: ts(element, P("mj", 12, 13), 0.0625, A.mult),
         lambda: ts(place, P("cj", 64, 65), 0.25, A.mult),
         lambda: ts(mixed, P("mj", 5, 6), element, A.add),
         lambda: ts(P("gl", 0, 24), P("gl", 0, 24), 63, A.bitwise_and),
         lambda: [copy(P("glist", 0, 6, 1, 32 * a, 32 * a + 32), P("gl", 6 * a, 6 * a + 6, 1, 32 * a, 32 * a + 32)) for a in (0, 2, 3)],
         lambda: ts(P("glist", 0, 6, 1, 32, 64), P("gl", 6, 12, 1, 32, 64), P("cols", 5, 6, 1, 32, 64), A.add),
         lambda: [act(P("jq", 32 * j, 32 * j + 32), P("zt", 0, 32), F.Identity, 1.0, 0.25 * j) for j in range(3)])[k]()

    def units(k):
        if k < 2:
            zero(P(("f6", "f2")[k], 0, 520))
        elif k == 2:
            select(P("f6", 3, 515, 4), P("f6", 3, 515, 4), [[-1, 128]], A.not_equal, 1.0, 0, 1)
        elif k == 3:
            select(P("f2", 3, 515, 4), P("f6", 3, 515, 4), [[0, 8], [16, 16]], A.not_equal, 1.0, -32, -1)
        elif k == 4:
            select(P("f2", 3, 515, 4), P("f2", 3, 515, 4), [[-1, 8], [1, 16]], A.not_equal, 0.0, -2, 0)
        elif k < 7:
            quant("c2", 128 * k - 640, 128 * k - 512, P("f2", 8 - k, 520 - k))
        else:
            quant("c6", 128 * k - 896, 128 * k - 768, P("f6", 10 - k, 522 - k))

    def weigh(at, row, w, groups=8, step=-128):
        p = P("dd", at, at + 8)
        select(p, p, [[step, 8 // groups], [-16, groups]], A.not_equal, float(w), -row, 1)

    def weights(k):
        if k < 4:
            weigh(0, 6 + k, -256 << (k & 1))
        elif k == 4:
            weigh(0, 0, -4096)
        else:
            x, e = divmod(k - 5, 2)
            if x < 4:
                weigh(8, (2, 4, 4, 6)[x] + e, (-4, -16, -4, -16)[x] << e, (8, 8, 2, 4)[x])
            else:
                weigh(8, 2 + e, -64 << e, 2, -34)

    def tiles(k):
        if k == 0:
            iota(P("dd", 0, 24), [[0, 24]], 0, 0, True)
        elif k == 1:
            iota(P("pat", 0, 64), [[0, 64]], 1, 0, True)
        elif k == 2:
            select(P("pat", 0, 64), P("pat", 0, 64), [[-1, 4], [0, 4], [1, 4]], A.is_equal, 0.0, 0, 0)
        elif k < 7:
            j, e = divmod(k - 3, 2)
            for r in range(4 * e, 4 * e + 4):
                act(P(("f3", "f7")[j], 64 * r, 64 * r + 64), P("pat", 0, 64), scale=P("dd", 8 * j + r, 8 * j + r + 1))
        else:
            quant("c3", 128 * k - 896, 128 * k - 768, P(("f3", "f7")[k - 7], 0, 512))

    state = ["xa", "xb", "xc"]
    mine, theirs = 64 * o, 1 - block
    slot = {r: 64 * (owner[r] & 1) for r in far}
    slot[near[0]] = 128
    spans = pieces + ((0, 256), (256, 512))

    def new_state(t, a, b):
        gather(P(state[t + 1], 4 * a, 4 * b), P("yt", 0, 1040), P("offs", a // 4, b // 4), P(state[t], 4 * a, 4 * b))

    def looked_up(a, b):
        y, i, out = P("yt", 0, 1040), P("offs", a // 4, b // 4), P("yg", 4 * a, 4 * b)
        do("s", lambda: g.scalar.activation(V(out), V(y).indirect(V(i)), F.Copy), [y, i], [out])

    def added(t, a, b):
        tt(P(state[t + 1], 4 * a, 4 * b), P("yg", 4 * a, 4 * b), P(state[t], 4 * a, 4 * b), A.add)

    def marks(k):
        at = 512 * (k // 2)
        tt(P("wm", at + k % 2, at + 512, 4), ps(("scores", k), 0, 128), P("sq", *pieces[k]), A.is_le)
        drop(("scores", k))

    def missing(k, h):
        mm(("missing", k, h), 128, "c1", 256 * (k % 2) + 128 * h, "pq", 128 * k)

    def masked(k, h):
        tt(P(("sa", "sb")[h], *pieces[k]), ps(("missing", k, h), 0, 128), P("sp", *pieces[k]), A.add)
        drop(("missing", k, h))

    def digits(h, k):
        c, n, less, more = [P("acc", 4 * h + i, 4 * h + i + 1) for i in range(4)]
        at = 64 - 64 * h
        if k == 0:
            ts(P("acc", 4 * h + 2, 4 * h + 4), P("pm", 0, 2), c, A.mult)
        else:
            act(P("digits", at, at + 32), P("zt", 0, 32), F.Identity, 1.0, more)
            act(P("digits", at + 32, at + 64), P("m1", 32 * h, 32 * h + 32), F.Identity, n, less)

    def product(h):
        quant("zq", 136 * h, 136 * h + 136, P("zb", 64 - 64 * h, 608 - 64 * h))
        for k in range(2):
            mm(("places", h), 128, "c5", 0, "zq", 136 * h + 8 * k, k == 0, k == 1)

    def places(h):
        copy(P("off", 8 * h, 8 * h + 8), ps(("places", h), 0, 8))
        drop(("places", h))

    def turn(n):
        for first in (0, 64):
            flip(P("bc", 64 * n, 64 * n + 32, 1, first, first + 64), Q("tr", 32 * n, 32 * n + 32))
        for a in range(4):
            first = 64 * (o & 1) + 32 * (1 - a % 2)
            flip(P("bc", 64 * n + 32, 64 * n + 64, 1, 32 * a, 32 * a + 32), P("tr", 32 * n, 32 * n + 32, 1, first, first + 32))

    def fold(n, k):
        if k == 0:
            gather(P("slots", 0, 96), P("bc", 64 * n, 64 * n + 64), P("glist", 0, 6), P("jq", 0, 96))
        elif k == 1:
            flip(P("fold", 0, 96), P("slots", 0, 96))
        else:
            ts(P(("offm", "offe")[n], 0, 3), P("fold", 0, 96, 32), 64.0, A.mult, place, A.add)

    def wishes(j):
        for e in range(2):
            mm("wishes", 128, "c2", 128 * e, "pq", 256 * j + 128)
            act(P("nd", *pieces[2 * j + e]), ps("wishes", 0, 128), F.Sign)
            drop("wishes")

    def offsets(k):
        if k == 0:
            quant("nq", 0, 128, P("nd", 0, 512))
            for j in range(2):
                mm("offsets", 128, "c3", 128 * j, "nq", 0, j == 0, j == 1)
        elif k == 1:
            ts(P("la", 0, 128), ps("offsets", 0, 128), element, A.add, 4.0 * (6 * 64 + 63 - 16) + 4096.0, A.add)
            drop("offsets")
        elif k == 2:
            ts(P("lb", 0, 128), P("la", 0, 128), 4096 + 1023, A.bitwise_and)
        else:
            ts(P("offs", 0, 128), P("lb", 0, 128), 1024.0, A.min)

    def numbers(k):
        if k == 0:
            for k in range(8):
                weigh(16, 2 + k, 1 << k)
        elif k == 1:
            zero(P("f4", 0, 304))
            zero(P("f4", 304, 608))
        elif k == 2:
            for b in range(4):
                act(P("f4", 33 * b, 32 * b + 32, 4), P("dd", 16, 24))
        elif k == 3:
            quant("c4", 0, 152, P("f4", 0, 608))
        elif k == 4:
            for b in range(4):
                mm("numbers", 128, "c4", 8 * b, "nq", 0)
                act(P("wo", b, 512, 4, 0, 8), ps("numbers", 0, 128, 1, 8), F.Identity, -1.0, 255.0)
                drop("numbers")
        else:
            dma("y", T.wl[:, 0:512], T.wo[0:8, 0:512], "done", 0, [P("wo", 0, 512)], [])

    for t in range(ROUNDS):
        X = state[t]
        xq, aq, cq, lq, eq, hq, st, rr, se, ra, rb = [
            "%s%d" % (s, t) for s in ("xq", "aq", "cq", "lq", "eq", "hq", "st", "rr", "se", "ra", "rb")]
        sem = {s: "%s%d" % (s, t) for s in LANDINGS}

        def scores(k):
            a, b = pieces[k]
            quant(xq, a, b, P(X, 4 * a, 4 * b))
            mm(("edges", k), b - a, "up", 0, xq, a)
            mm(("scores", k), b - a, "uq", 0, xq, a)

        def edges(k):
            a, b = pieces[k]
            act(P("sq", a, b), ps(("edges", k), 0, b - a))
            drop(("edges", k))

        def strengths(k, done):
            a, b = spans[k]
            if done:
                act(P("sp", a, b), ps(("strengths", k), 0, b - a), scale=SMALL)
                drop(("strengths", k))
            else:
                mm(("strengths", k), b - a, "up", 128, xq, a)

        def layer(k, e):
            a, b = spans[k]
            mm(("layer", k, e), b - a, "wq", 128 * e, xq, a)

        def scaled(k, e, vector=False):
            a, b = spans[k]
            out, src = P("ha", 4 * a + e, 4 * b, 4), ps(("layer", k, e), 0, b - a)
            if vector:
                ts(out, src, 0.03125, A.mult)
            else:
                act(out, src, scale=0.03125)
            drop(("layer", k, e))

        def maxima(k, h):
            a, b = pieces[k][0], pieces[k][1] + k // 3
            sa, run = P(("sa", "sb")[h], a, b), (ra, rb)[h]
            scan(P(run, a, b), sa, sa, P(run, a - 1, a) if k else LOW, A.max, A.max)
            if k == 3:
                strongest(h)

        def strongest(h):
            top = [P(run, 512, 513) for run in (ra, rb)]
            send([(r, V(top[h]), T[st][:, 4 * o:4 * o + 1], sem["am"]) for r in (far, near)[h]]
                 + [(r, V(top[pair.index(owner[r] >> 1)]), T[se][:, 4 * o:4 * o + 1], sem["bm"]) for r in blocks[theirs] if h],
                 top[:h + 1])
            if h:
                land(sem["am"], from_mates, [P(st, 4 * owner[r], 4 * owner[r] + 1) for r in mates])
                land(sem["bm"], len(outside), [P(se, 0, 16, 4)])

        def counts(h):
            run = (ra, rb)[h]
            below(P("acc", 4 * h, 4 * h + 1), P(run, 15, 512, 32), P(run, 512, 513), P("junk", 544 * h, 544 * h + 16))
            below(P("acc", 4 * h + 1, 4 * h + 2), P(run, 0, 512), P(run, 512, 513), P("junk", 544 * h + 32, 544 * h + 544))

        def packed(k):
            a, b = spans[k][0], spans[k][1] + 2 * (spans[k][1] // 512)
            quant(aq, a, b, P("ha", 4 * a, 4 * b))

        def candidates(k):
            if k == 0:
                pick(cq, 0, 112, aq, 514, "off", 0, 7)
            elif k == 1:
                pick(cq, 128, 176, aq, 514, "off", 12 - 4 * (o & 1), 15 - 4 * (o & 1))
            else:
                pick(lq, mine, mine + 48, aq, 514, "off", 8 + 4 * (o & 1), 11 + 4 * (o & 1))

        def hop1(k, to):
            k = "cs"[k]
            send([(r, side(cq + k, slot[r], slot[r] + 48), side(lq + k, mine, mine + 48), sem["a" + k]) for r in (far, near)[to]],
                 [P(cq + k, slot[r], slot[r] + 48) for r in (far, near)[to]])

        def compare(k):
            if k == 0:
                copy(P(st, 4 * o, 4 * o + 1), P(rb, 512, 513))
            elif k == 1:
                scan(P(rr, 0, 4), P(st, 0, 16, 4), P(st, 0, 16, 4), LOW, A.max, A.max)
            else:
                below(Q("tr", 0, 1), Q(rr, 0, 3), Q(rr, 3, 4), Q("cm", 0, 3))

        def swap():
            scan(Q("cm", 4, 8), Q(se, 0, 16, 4), Q(se, 0, 16, 4), LOW, A.max, A.max)

        def stronger():
            both = (Q(rr, 3, 4), Q("cm", 7, 8))
            ts(Q("tr", 32, 33), both[theirs], both[block], A.is_gt)

        def hop2():
            a, b = 64 * block, 64 * block + 48
            for k in "cs":
                land(sem["a" + k], from_mates, [P(lq + k, 64 * owner[r], 64 * owner[r] + 64) for r in mates])
            pick(eq, a, b, lq, 256, "offm", 0, 3)
            for k in "cs":
                send([(partner, side(eq + k, a, b), side(eq + k, a, b), sem["b" + k])], [P(eq + k, a, b)])
                land(sem["b" + k], len(outside), [P(eq + k, 64 * theirs, 64 * theirs + 48)])

        def hop3():
            pick(hq, 128, 176, eq, 128, "offe", 0, 3)
            spot = {r: 128 + 48 * (o ^ owner[r]) for r in mates}
            for k in "cs":
                send([(r, side(hq + k, 128, 176), side(hq + k, spot[r], spot[r] + 48), sem["gn" if r in near else "gc"]) for r in mates],
                     [P(hq + k, 128, 176)])
            land(sem["gn"], 2 * len(inside), [P(hq + k, 176, 224) for k in "cs"])
            land(sem["gc"], 2 * len(outside), [P(hq + k, 224, 320) for k in "cs"])

        def unpack(j):
            for b in range(4):
                mm(("table", b), 128, "c6", 128 * b, hq, 96 + 96 * j)
            for b in range(4):
                for k in range(2):
                    at = 256 * (o ^ (2 * j + k)) + b
                    (copy if j and b % 2 else act)(P("yt", at, at + 192, 4), ps(("table", b), 32 + 48 * k, 80 + 48 * k))
                drop(("table", b))

        steps = {"s": lambda a, b: new_state(t - 1, 32 * a, 32 * b), "g": lambda a, b: looked_up(32 * a, 32 * b),
                 "o": lambda a, b: added(t - 1, 32 * a, 32 * b), "q": scores, "m": marks, "t": strengths, "h": layer,
                 "p": lambda k: quant("pq", 128 * k, 128 * k + 128, P("wm", 512 * (k // 2), 512 * (k // 2) + 512)),
                 "e": edges, "N": missing, "a": masked, "x": maxima, "u": columns_of_u, "z": blanks, "b": bits, "r": rows,
                 "j": pairs, "l": slots, "i": units, "w": weights, "c": tiles, "y": scaled, "v": lambda k, e: scaled(k, e, True),
                 "n": counts, "D": digits, "P": product, "F": places, "K": candidates, "H": hop1, "A": packed, "C": compare,
                 "T": turn, "W": wishes, "f": fold, "E": swap, "d": stronger, "M": hop2, "G": hop3, "O": offsets, "L": numbers, "U": unpack}
        for step in ORDER[min(t, 1)].split():
            steps[step[0]](*[int(c, 17) for c in step[1:]])

    def scales(q, k):
        dma(q, T.osc[4 * k:4 * k + 4, 0:512], T.xq2s[32 * k:32 * k + 4, 0:512], "done", 0, [P("xq2s", 0, 512)], [])

    def results(a, b):
        quant("xq2", a, b, P(state[ROUNDS], 4 * a, 4 * b))
        mm(("results", a), b - a, "vq", 0, "xq2", a)
        dma("y", T.oc[:, 4 * a:4 * b], side("xq2c", a, b), "done", 0, [P("xq2c", a, b)], [])
        if b == 512:
            for j in range(4):
                scales("ys"[j // 2], j)

    def products(a, b, vector=False):
        (copy if vector else act)(P("yo", a, b), ps(("results", a), 0, b - a))
        drop(("results", a))
        dma("y" if vector else "s", T.y[:, a:b], V(P("yo", a, b)), "done", 0, [P("yo", a, b)], [])

    for step in TAIL.split():
        a, b = [32 * int(c, 17) for c in step[1:]]
        {"s": lambda: new_state(ROUNDS - 1, a, b), "g": lambda: looked_up(a, b), "o": lambda: added(ROUNDS - 1, a, b),
         "r": lambda: results(a, b), "y": lambda: products(a, b), "v": lambda: products(a, b, True)}[step[0]]()
    for s in total:
        if waited.get(s, 0) < total[s]:
            g.wait_ge(T.sem[s], total[s])
